import numpy as np, ml_dtypes
CORES = [2,3,42,43,82,83,122,123]
N = 8
import mx_ref
BF = ml_dtypes.bfloat16
def entries(a):
    return np.ascontiguousarray(a.T).reshape(-1)
def table(e):
    return np.ascontiguousarray(np.reshape(e, (-1, 16)).T).astype(np.int32)
def cols(t, e):
    v = np.concatenate([t.reshape(128, -1, 4), np.zeros((128, 1, 4), BF)], axis=1)
    return np.ascontiguousarray(v[:, e]).reshape(128, -1)
def f(rng, *shape):
    return mx_ref.flush((rng.standard_normal(shape, dtype=np.float32) * np.exp2(rng.integers(-2, 3, shape[:-1] + (1,)))).astype(BF))
def wide(rng, *shape, cols=0):
    v = rng.standard_normal(shape, dtype=np.float32) * np.exp2(rng.integers(-12, 13, shape)).astype(np.float32)
    if cols: v *= np.repeat(np.exp2(rng.integers(-cols, cols + 1, shape[:-2] + (1, shape[-1] // 4))) * (rng.random(shape[:-2] + (1, shape[-1] // 4)) > 0.0625), 4, axis=-1).astype(np.float32)
    return mx_ref.flush(v.astype(BF))
T, O = 256, 4
CAP, ROOM = 288, 320
PAIR, MOVE, BOTH = 48, 16, 60
def turn(v, e):
    v = np.sort(v); return v[np.argsort((v // T - e) % N, kind="stable")]
def play(c1, c2):
    a, b = c1.reshape(-1), c2.reshape(-1)
    first = [turn(np.flatnonzero(a == e), e)[:CAP] for e in range(N)]
    refused = np.setdiff1d(np.arange(N * T), np.concatenate(first))
    second = [turn(refused[b[refused] == e], e)[:ROOM - len(first[e])] for e in range(N)]
    return first, second, refused
def broken(c1, c2):
    b = []
    if c1.min() < 0 or c1.max() >= N: return ["c1"]
    if c2.min() < 0 or c2.max() >= N: return ["c2"]
    if (c1 == c2).any(): b.append("a token with two equal choices")
    if max(np.bincount(v, minlength=N).max() for v in c1) > PAIR: b.append("first choices of a pair of ranks")
    first, second, refused = play(c1, c2)
    if np.bincount(c1.reshape(-1)[refused] * N + c2.reshape(-1)[refused], minlength=N * N).max() > MOVE: b.append("refused tokens of a pair of ranks")
    for e in range(N):
        if np.bincount(np.concatenate([first[e], second[e]]) // T, minlength=N).max() > BOTH: b.append("admitted tokens of a pair of ranks")
    return b
def fill(rng, low, high, total):
    n, p = np.array(low), rng.dirichlet(np.full(len(low), 16.0))
    while n.sum() < total: n = np.minimum(n + rng.multinomial(total - n.sum(), p), high)
    return n
def deal(rng, tot):
    n = np.stack([np.bincount(v, minlength=N) for v in rng.permutation(np.repeat(np.arange(N), tot)).reshape(N, T)])
    while n.max() > PAIR:
        s, e = np.argwhere(n > PAIR)[0]
        q = rng.choice(np.flatnonzero(n[:, e] < PAIR))
        g = rng.choice(np.flatnonzero(n[q] > n[s]))
        n[s, e] -= 1; n[q, e] += 1; n[q, g] -= 1; n[s, g] += 1
    return n
def bounds():
    return np.full(N, T >> 3), np.full(N, N * PAIR), np.zeros((N, N), int), MOVE * (1 - np.eye(N, dtype=int))
def lists(rng, low, high, mlow, mhigh, pair=None, skew=False, force=None):
    for _ in range(50):
        n = deal(rng, fill(rng, low, high, N * T))
        if pair or force:
            s, g, e = pair or (*force, force[1])
            for to in (g, e):
                while n[s, to] < PAIR:
                    h, q = [(h, q) for h in range(N) for q in range(N) if h not in (g, e) and n[s, h] > 0 and q != s and n[q, to] > 0 and n[q, h] < PAIR][0]
                    n[s, to] += 1; n[s, h] -= 1; n[q, to] -= 1; n[q, h] += 1
        c1 = np.concatenate([rng.permutation(np.repeat(np.arange(N), v)) for v in n])
        c2 = (c1 + rng.integers(1, N, N * T)) % N
        for e in range(N):
            at = turn(np.flatnonzero(c1 == e), e)[CAP:]
            c2[at] = rng.permutation(np.repeat(np.arange(N), fill(rng, mlow[e], mhigh[e], len(at))))
            if pair and e == pair[1]:
                mine = at[at // T == pair[0]]; named = c2[at]
                named = np.concatenate([named[named == pair[2]], named[named != pair[2]]]); k = int((named == pair[2]).sum())
                to = rng.permutation(mine)[:k]; c2[np.setdiff1d(at, to)] = named[k:]; c2[to] = pair[2]
        if skew:
            out = np.zeros(N * T, bool)
            for e in range(N): out[turn(np.flatnonzero(c1 == e), e)[CAP:]] = True
            for s in range(N):
                e = (s + rng.integers(3, N)) % N; k = np.arange(s * T, s * T + T)
                k = k[~out[k] & ((c1[k] - s - 1) % N < 2)]; c2[k] = e
        c1, c2 = c1.reshape(N, T), c2.reshape(N, T)
        if not broken(c1, c2): return {"c1": np.stack([table(v) for v in c1]), "c2": np.stack([table(v) for v in c2])}
    raise RuntimeError("no lists found")
def tiles(rng):
    return {"x": f(rng, N, 128, 4 * T), "w": f(rng, N, 128, 512 * O)}
def setup_inputs(rng):
    return {**tiles(rng), **lists(rng, *bounds())}
def setup_inputs_pair(rng):
    low, high, mlow, mhigh = bounds()
    p = rng.permutation(N); g, e, z = p[0], p[1], p[2]; s = (g - 1) % N
    if s in (e, z): e, z = [k for k in p if k not in (g, s)][:2]
    few = N - 2 - (N > 4)
    high[:] = CAP + (few - 1 + (N == 4)) * MOVE
    low[g] = high[g] = CAP + min(PAIR, BOTH - PAIR + few * MOVE); low[e] = N * PAIR >> 2; high[e] = CAP
    mhigh[:, e] = 0; mlow[g, e] = mhigh[g, e] = BOTH - PAIR
    if N > 4: low[z] = high[z] = 0; mhigh[:, z] = 0
    return {**tiles(rng), **lists(rng, low, high, mlow, mhigh, (int(s), int(g), int(e)))}
def setup_inputs_exact(rng):
    low, high, mlow, mhigh = bounds()
    p = rng.permutation(N); src = p[2:2 + (ROOM - CAP) // MOVE]
    high[:] = CAP
    low[p[0]] = CAP
    low[p[1]] = high[p[1]] = CAP + 1
    low[p[-1]] = N * PAIR >> 2
    mhigh[:, p[-1]] = np.minimum(mhigh[:, p[-1]], MOVE >> 1)
    low[src] = high[src] = N * PAIR
    mhigh[:, p[0]] = 0
    mlow[src, p[0]] = mhigh[src, p[0]] = MOVE
    return {**tiles(rng), **lists(rng, low, high, mlow, mhigh, skew=True, force=(int(p[-1] - 1) % N, int(p[-1])))}
def setup_inputs_full(rng):
    low, high, mlow, mhigh = bounds()
    p = rng.permutation(N); src = p[1:1 + 2 * ((ROOM - CAP) // MOVE)]
    low[p[0]] = CAP + 3 * MOVE // 2
    low[src] = CAP + MOVE
    mlow[src, p[0]] = MOVE
    return {**tiles(rng), **lists(rng, low, high, mlow, mhigh)}
def setup_inputs_room(rng):
    low, high, mlow, mhigh = bounds()
    p = rng.permutation(N); src = p[1:2 + (ROOM - CAP) // MOVE]
    low[p[0]] = high[p[0]] = CAP - 1
    low[src] = CAP + MOVE
    mlow[src, p[0]] = MOVE
    return {**tiles(rng), **lists(rng, low, high, mlow, mhigh)}
def setup_inputs_spread(rng):
    d = setup_inputs(rng); d["x"] = wide(rng, N, 128, 4 * T, cols=6); return d
def check_inputs(d):
    return broken(np.stack([entries(v) for v in d["c1"]]), np.stack([entries(v) for v in d["c2"]]))
def reference(x, w, c1, c2):
    first, second, _ = play(np.stack([entries(v) for v in c1]), np.stack([entries(v) for v in c2]))
    tokens = np.concatenate([x[r] for r in range(N)], axis=1)
    y = np.zeros((N, 128, O * ROOM), np.float32)
    for e in range(N):
        held = np.concatenate([first[e], second[e]])
        t = mx_ref.quantize(cols(tokens, np.concatenate([held, np.full(ROOM - len(held), -1)])))
        for o in range(O): y[e][:, ROOM * o:ROOM * o + ROOM] = mx_ref.matmul(mx_ref.quantize(w[e][:, 512 * o:512 * o + 512]), t)
    return {"y": y}

@@ -1,0 +1,424 @@
+from concourse.bass import DstId, RemoteDMATransfer
+from concourse.mybir import dt, AluOpType, AxisListType, ActivationFunctionType
+
+N, TOK, O, CAP, ROOM, BOTH = 8, 256, 4, 288, 320, 60
+SLOT = 64
+FIRST = 48
+ZERO = N * SLOT
+NZ = 128
+WSLOT = 80
+WIN = N * WSLOT
+BACK = 9
+LATE = 400
+
+
+def _sb(n, d):
+    return ("sbuf", [128, n], d)
+
+
+F32, I32, U16, B16, MX, U8 = "float32", "int32", "uint16", "bfloat16", "float8_e4m3fn_x4", "uint8"
+SCRATCH = {
+    "lists": ("dram", [N, 128, 2], I32),
+    "ct": _sb(32, I32), "xin": _sb(4 * TOK, B16), "win": _sb(512 * O, B16), "zin": _sb(4 * NZ, B16),
+    "xq": _sb(TOK, MX), "xs": _sb(TOK, U8), "wq": _sb(128 * O, MX), "wsc": _sb(128 * O, U8),
+    "ra": _sb(128, F32), "ca": _sb(128, F32), "rb": _sb(64, F32), "cb": _sb(64, F32), "e64": _sb(64, I32), "ec": _sb(64, I32),
+    "gr": _sb(64, F32), "gt": _sb(64, F32), "gl": _sb(4, U16), "zpos": _sb(8, F32), "zfix": _sb(8, F32),
+    "l4": _sb(4, I32), "l64": _sb(4, U16), "meq": _sb(32, F32), "meqn": _sb(32, F32), "mgt": _sb(32, F32), "mlt": _sb(32, F32),
+    "v128": _sb(128, B16), "vals": _sb(128, B16), "j0": _sb(20, I32), "ones": _sb(32, F32), "z64": _sb(64, F32),
+    "pre": _sb(256, B16), "mt": _sb(256, B16), "tcol": _sb(8, F32), "bm": _sb(128, F32), "tb": _sb(168, F32), "bcol": _sb(8, F32),
+    "sc1": _sb(64, F32), "d1": _sb(64, F32), "sca": _sb(64, F32), "scb": _sb(64, F32), "wa": _sb(64, F32), "wb": _sb(64, F32),
+    "qa": _sb(64, B16), "qb": _sb(64, B16), "td1": _sb(64, F32), "cs1": _sb(72, F32), "s1": _sb(8, F32),
+    "al": _sb(64, I32), "eqs": _sb(192, B16), "eqj": _sb(64, B16), "gcol": _sb(8, F32), "gme": _sb(8, F32), "bg": _sb(64, F32),
+    "tg": _sb(64, F32), "gs": _sb(8, F32), "b3": _sb(32, F32), "t3": _sb(32, F32), "n16": _sb(16, F32), "n8": _sb(8, F32),
+    "fa": _sb(64, B16), "fb": _sb(64, B16), "r2": _sb(64, B16), "cum": _sb(64, F32), "bm2": _sb(64, F32), "p2": _sb(96, F32),
+    "m16": _sb(16, F32), "m8": _sb(8, F32), "d2c": _sb(64, F32), "d2b": _sb(64, F32), "tdc": _sb(64, F32), "tdb": _sb(64, F32),
+    "cs2": _sb(72, F32), "s2": _sb(8, F32), "s8": _sb(8, F32), "off": _sb(8, U16),
+    "scat": _sb(WIN + 32, B16), "tw": _sb(2 * WIN, B16), "hh": _sb(WIN // 16, F32), "so": _sb(4 * N, U16),
+    "sq1": _sb(2 * SLOT, MX), "sp1": _sb(2 * SLOT, U8), "sq2": _sb(4 * SLOT, MX), "sp2": _sb(4 * SLOT, U8),
+    "sq3": _sb(SLOT, MX), "sp3": _sb(SLOT, U8),
+    "land": _sb(ZERO + NZ, MX), "lsc": _sb(ZERO + NZ, U8),
+    "n8s": _sb(8, F32), "pp": _sb(24, F32), "bb": _sb(24, F32), "de": _sb(24, F32), "dd": _sb(24, F32), "ml": _sb(8, F32),
+    "ta": _sb(180, F32), "tz": _sb(180, F32), "cs3": _sb(192, F32), "t20": _sb(20, F32),
+    "fo": _sb(20, U16), "fq": _sb(ROOM, MX), "fs": _sb(ROOM, U8),
+    "acc": ("psum", [128, 512 * 2 * O], F32), "yo": _sb(ROOM * O, F32),
+}
+SEMAPHORES = ["cv", "cs", "cg", "ct", "dl0", "dc1", "dc2", "dx", "dw", "dal", "dy",
+              "lst", "lsts", "mar", "mars", "dat", "dats"]
+
+ADD, SUB, MUL, MIN, MAX = AluOpType.add, AluOpType.subtract, AluOpType.mult, AluOpType.min, AluOpType.max
+GE, GT, EQ = AluOpType.is_ge, AluOpType.is_gt, AluOpType.is_equal
+AND = AluOpType.bitwise_and
+COPY, IDENT = ActivationFunctionType.Copy, ActivationFunctionType.Identity
+
+
+def plan(me, cores, topo):
+    core = cores[me]
+    mate = [r for r in range(N) if r != me and topo.chip(cores[r]) == topo.chip(core)][0]
+    near = (mate - me - 1) % N
+    far = [z for z in range(N - 1) if z != near]
+    out = topo.engines(core, cores[(me + 1 + far[0]) % N])
+    inn = [e for e in topo.engines(core, cores[mate]) if e not in out]
+
+    def deal(zs):
+        k = len(out) // len(zs)
+        return {z: out[k * i:k * i + k] for i, z in enumerate(zs)}
+
+    calls = []
+    for zs, e in ((far[:2], deal(far[:2])), (far[2:], deal(far[2:])), ([near], {near: inn})):
+        n = SLOT if min(zs) < 2 else BOTH
+        calls += [("q", zs, n, e), ("s", zs, n, e)]
+    return near, calls, out[::4]
+
+
+def rank_program(g, core, T, topo):
+    me = T.rank_of(core)
+    if me is None:
+        return
+    cores = [int(c) for c in T.cores]
+    near, calls, few = plan(me, cores, topo)
+    own = N - 1
+    queue = {"v": g.vector, "s": g.scalar, "t": g.tensor, "g": g, "y": g.sync}
+    cnt, seen, wr, rd = {}, {}, {}, {}
+
+    def need(q, tok):
+        sem, val = tok
+        if val is None:
+            val = cnt[sem]
+        if seen.get((q, sem), 0) < val:
+            queue[q].wait_ge(T.sem[sem], val)
+            seen[(q, sem)] = val
+
+    def before(q, reads, writes):
+        toks = {}
+        for k in reads:
+            for t in wr.get(k, []):
+                toks.setdefault(t[0], []).append(t)
+        for k in writes:
+            for t in wr.get(k, []) + rd.get(k, []):
+                toks.setdefault(t[0], []).append(t)
+        for sem in toks:
+            v = [t[1] for t in toks[sem]]
+            need(q, (sem, None if None in v else max(v)))
+
+    def after(tok, reads, writes, more):
+        for k in writes:
+            wr[k] = (wr.get(k, []) if more else []) + [tok]
+            if not more:
+                rd[k] = []
+        for k in reads:
+            rd.setdefault(k, []).append(tok)
+
+    def op(q, call, args, reads, writes, **kw):
+        before(q, reads, writes)
+        sem = "c" + q
+        call(*args, **kw).then_inc(T.sem[sem], 1)
+        cnt[sem] = cnt.get(sem, 0) + 1
+        after((sem, cnt[sem]), reads, writes, False)
+
+    def dma(q, sem, out, in_, reads, writes, more=False):
+        if not more:
+            before(q, reads, writes)
+        else:
+            before(q, reads, [])
+        queue[q].dma_start(out, in_).then_inc(T.sem[sem], 16)
+        cnt[sem] = cnt.get(sem, 0) + 16
+        after((sem, None), reads, writes, more)
+
+    V = g.vector
+
+    def ts(out, in0, s1, s2, op0, op1, reads, writes):
+        a = (out, in0, s1, s2, op0) if op1 is None else (out, in0, s1, s2, op0, op1)
+        op("v", V.tensor_scalar, a, reads, writes)
+
+    def tt(out, a, b, o, reads, writes):
+        op("v", V.tensor_tensor, (out, a, b, o), reads, writes)
+
+    def cp(out, a, reads, writes):
+        op("v", V.tensor_copy, (out, a), reads, writes)
+
+    def red(out, a, reads, writes):
+        op("v", V.tensor_reduce, (out, a, AxisListType.X, ADD), reads, writes)
+
+    def tr(out, a, reads, writes):
+        op("v", V.transpose, (out, a), reads, writes)
+
+    def quant(oq, os_, tile, reads, writes):
+        op("v", V.quantize_mx, (oq, os_, tile), reads, writes)
+
+    def scan2(out, a, b, init, reads, writes):
+        op("v", V.tensor_tensor_scan, (out, a, b, init, ADD, ADD), reads, writes)
+
+    def scan(out, a, n, init, reads, writes):
+        scan2(out, a, T.z64[:, 0:n], init, reads + ["z64"], writes)
+
+    def fill(ap, val, key):
+        op("v", V.memset, (ap, val), [], [key])
+
+    def iota(ap, key, pattern, base, flag=False):
+        kw = {"allow_small_or_imprecise_dtypes": True} if flag else {}
+        op("g", g.iota, (ap, pattern, base, 0), [], [key], **kw)
+
+    def act(out, a, reads, writes, **kw):
+        op("s", g.scalar.activation, (out, a, COPY), reads, writes, **kw)
+
+    def at(z):
+        rid, pid, _ = topo.addr(cores[(me + 1 + z) % N])
+        return DstId(rid=rid, pnc=pid)
+
+    def place(z):
+        return N - 1 - z
+
+    def mask(engines):
+        m = 0
+        for e in engines:
+            m |= 1 << e
+        return m
+
+    def send(zs, src, dst, engines, sem, lsem, reads):
+        before("g", reads, [])
+        g.remote_dma_fused([RemoteDMATransfer(dst_ids=[at(z)], dma_engine_mask=mask(engines[z]),
+                                              remote_sem=T.sem[sem], src=src(z), dst=dst(z)) for z in zs], local_sem=T.sem[lsem])
+        cnt[lsem] = cnt.get(lsem, 0) + sum(len(engines[z]) for z in zs)
+
+    data_in = list_in = count_in = 0
+    for k in range(1, N):
+        _, c2, f2 = plan((me + k) % N, cores, topo)
+        z = N - 1 - k
+        data_in += sum(len(e[z]) for _, zs, _, e in c2 if z in zs)
+        count_in += sum(len(e[z]) for kind, zs, _, e in c2 if z in zs and kind == "q")
+        list_in += len(f2)
+
+    dma("y", "dl0", T.lists[0], T.c1[:, :], [], ["l0"])
+    for b in range(8):
+        dma("ys"[b % 2], "dc1", T.ct[16 * b:16 * b + 16, 0:16], T.c1[:, :], [], ["c1"], more=True)
+    for b in range(8):
+        dma("sy"[b % 2], "dc2", T.ct[16 * b:16 * b + 16, 16:32], T.c2[:, :], [], ["c2"], more=True)
+    dma("y", "dx", T.xin[:, :], T.x[:, :], [], ["xin"])
+
+    ra, rb = T.ra, T.rb
+    iota(T.l4[:, :], "l4", [[2, 2], [8, 2]], 0)
+    iota(ra[:, 64:96], "ra2", [[1, 2], [4, 2], [0, 8]], 0, flag=True)
+    iota(ra[:, 0:32], "ra0", [[0, 4], [1, 8]], 0, flag=True)
+    iota(ra[:, 32:64], "ra1", [[1, 4], [0, 8]], 0, flag=True)
+    iota(ra[:, 96:128], "ra3", [[0, 4], [WSLOT, 8]], -1, flag=True)
+    iota(T.e64[:, :], "e64", [[1, 64]], me + 1)
+    others = [z for z in range(N) if z != own]
+    before("g", ["l0"], [])
+    g.remote_dma_fused([RemoteDMATransfer(dst_ids=[at(z) for z in others], dma_engine_mask=mask(few), remote_sem=T.sem["lst"],
+                                          srcs=[T.lists[0]], dsts=[T.lists[place(z)] for z in others])], local_sem=T.sem["lsts"])
+    cnt["lsts"] = len(few)
+    cnt["lst"] = list_in
+    wr["lx"] = [("lst", list_in)]
+    iota(rb[:, 32:64], "rb1", [[16, 2], [0, 16]], 0, flag=True)
+    iota(rb[:, 0:32], "rb0", [[0, 2], [1, 16]], 0, flag=True)
+    iota(T.v128[:, :], "v128", [[32, 2], [64, 4], [1, 16]], 0, flag=True)
+    iota(T.gr[:, 0:32], "gr0", [[-1, 2], [WSLOT // 16, 4], [1, 4]], 1, flag=True)
+    iota(T.gr[:, 32:64], "gr1", [[-1, 2], [WSLOT // 16, 4], [1, 4]], 1 + WSLOT // 4, flag=True)
+    iota(T.gr[:, 3:32:16], "gr0", [[-1, 2]], 1 + BACK, flag=True)
+    iota(T.j0[:, :], "j0", [[16, 20]], 0)
+    iota(T.bb[:, 0:8], "bb0", [[SLOT, 8]], 0, flag=True)
+
+    fill(T.ones[:, :], 1.0, "ones")
+    fill(T.z64[:, :], 0.0, "z64")
+    fill(T.cs1[:, 0:8], 0.0, "cs1z")
+    fill(T.cs2[:, 0:8], 0.0, "cs2z")
+    fill(T.pp[:, 0:1], 0.0, "pp0")
+    fill(T.zin[:, :], 0.0, "zin")
+    fill(T.tz[:, :], 0.0, "tzz")
+    fill(T.cs3[:, 0:12], 0.0, "cs3z")
+    fill(T.bb[:, 15:16], float(SLOT * (N - 1) + FIRST), "bb15")
+    fill(T.bb[:, 16:17], float(ZERO), "bb16")
+    tr(T.ca[:, :], ra[:, :], ["ra0", "ra1", "ra2", "ra3"], ["ca"])
+    zc, hc, pc, sc = [T.ca[:, 32 * j:32 * j + 1] for j in range(4)]
+    ts(T.ec[:, :], T.e64[:, :], 7, None, AND, None, ["e64"], ["ec"])
+    ts(T.l64[:, :], T.l4[:, :], pc, None, ADD, None, ["l4", "ca"], ["l64"])
+    ts(T.meq[:, :], ra[:, 0:32], zc, None, EQ, None, ["ra0", "ca"], ["meq"])
+    ts(T.mgt[:, :], ra[:, 32:64], hc, None, GT, None, ["ra1", "ca"], ["mgt"])
+    ts(T.zpos[:, 0:1], zc, 0.0, None, GT, None, ["ca"], ["zpos"])
+    ts(T.zfix[:, 0:1], zc, 0.0, 16.0 * BACK, EQ, MUL, ["ca"], ["zfix"])
+    tt(T.mlt[:, :], T.meq[:, :], T.mgt[:, :], MUL, ["meq", "mgt"], ["mlt"])
+    ts(T.meqn[:, :], ra[:, 0:32], zc, T.zpos[:, 0:1], EQ, MUL, ["ra0", "ca", "zpos"], ["meqn"])
+    act(T.tb[:, 31:32], sc, ["ca"], ["tb0"])
+    op("s", g.scalar.activation, (T.tb[:, 160:161], T.zfix[:, 0:1], IDENT, sc), ["zfix", "ca"], ["tb1"])
+
+    l64 = T.l64[:, 0:4]
+    c1w, c2w = T.ct[:, 0:16].indirect(l64), T.ct[:, 16:32].indirect(l64)
+    m1, ma, mb, mc = [T.mt[:, 64 * i:64 * i + 64] for i in range(4)]
+    tt(T.pre[:, 0:64], c1w, T.ec[:, :], EQ, ["c1", "l64", "ec"], ["pre0"])
+    ts(T.pre[:, 64:128], c1w, float((me + 1) % N), None, EQ, None, ["c1", "l64"], ["pre1"])
+    ts(T.pre[:, 128:192], c1w, float((me + 2) % N), None, EQ, None, ["c1", "l64"], ["pre2"])
+    tt(T.pre[:, 192:256], c2w, T.ec[:, :], EQ, ["c2", "l64", "ec"], ["pre3"])
+    tr(T.mt[:, :], T.pre[:, :], ["pre0", "pre1", "pre2", "pre3"], ["mt"])
+    for i, m in enumerate((m1, ma, mb)):
+        red(T.tcol[:, i:i + 1], m, ["mt"], ["tcol%d" % i])
+    ts(T.bm[:, 0:32], T.mlt[:, :], T.tcol[:, 0:1], None, MUL, None, ["mlt", "tcol0"], ["bm0"])
+    ts(T.bm[:, 32:64], T.mlt[:, :], T.tcol[:, 1:2], LATE / 32, MUL, ADD, ["mlt", "tcol1"], ["bm1"])
+    ts(T.bm[:, 64:96], T.mlt[:, :], T.tcol[:, 2:3], LATE / 32, MUL, ADD, ["mlt", "tcol2"], ["bm2"])
+    ts(T.bm[:, 96:128], T.meqn[:, :], T.tcol[:, 0:1], None, MUL, None, ["meqn", "tcol0"], ["bm3"])
+    tr(T.tb[:, 32:160], T.bm[:, :], ["bm0", "bm1", "bm2", "bm3"], ["tb"])
+    tr(T.cb[:, :], rb[:, :], ["rb0", "rb1"], ["cb"])
+    tt(T.qa[:, :], ma, mc, MUL, ["mt"], ["qa"])
+    bcol = T.bcol
+    red(bcol[:, 1:2], T.tb[:, 64:96], ["tb"], ["ba"])
+    red(bcol[:, 2:3], T.tb[:, 96:128], ["tb"], ["bq"])
+    red(bcol[:, 0:1], T.tb[:, 31:64], ["tb", "tb0"], ["b1"])
+    red(T.p2[:, 31:32], T.tb[:, 128:161], ["tb", "tb1"], ["p2k"])
+    scan(T.sca[:, :], ma, 64, bcol[:, 1:2], ["mt", "ba"], ["sca"])
+    scan(T.scb[:, :], mb, 64, bcol[:, 2:3], ["mt", "bq"], ["scb"])
+    scan(T.sc1[:, :], m1, 64, bcol[:, 0:1], ["mt", "b1"], ["sc1"])
+    tt(T.qb[:, :], mb, mc, MUL, ["mt"], ["qb"])
+    tt(T.wa[:, :], T.qa[:, :], T.sca[:, :], MUL, ["qa", "sca"], ["wa"])
+    tt(T.d1[:, :], m1, T.sc1[:, :], MUL, ["mt", "sc1"], ["d1"])
+    tt(T.wb[:, :], T.qb[:, :], T.scb[:, :], MUL, ["qb", "scb"], ["wb"])
+    tr(T.td1[:, :], T.d1[:, :], ["d1"], ["td1"])
+    quant(T.xq[:, :], T.xs[:, :], T.xin[:, :], ["xin"], ["xq"])
+    scan(T.cs1[:, 8:72], T.td1[:, :], 64, 0.0, ["td1"], ["cs1"])
+    tr(T.gt[:, :], T.gr[:, :], ["gr0", "gr1"], ["gt"])
+    tt(T.s1[:, :], T.cs1[:, 15:72:8], T.cs1[:, 7:64:8], SUB, ["cs1", "cs1z"], ["s1"])
+    cp(T.gl[:, 0:4:2], T.gt[:, 0:64:32], ["gt"], ["gl"])
+
+    for b in range(4):
+        dma("ys"[b % 2], "dal", T.al[32 * b:32 * b + 32, 0:64], T.lists[:, :, :], ["lx", "l0"], ["al"], more=True)
+    dma("y", "dw", T["win"][:, :], T.w[:, :], ["lx"], ["win"])
+    op("s", g.scalar.activation, (T.vals[:, :], T.v128[:, :], IDENT, T.cb[:, 32:33]), ["v128", "cb"], ["vals"])
+    half = (WIN + 32) // 2
+    for i in range(2):
+        act(T.scat[:, half * i:half * i + half], T.zin[:, 0:half], ["zin"], ["sz%d" % i])
+    eqs, gcol = T.eqs, T.gcol
+    for i in range(2):
+        ts(eqs[:, 64 * i:64 * i + 64], T.al[:, :], float((me + 1 + i) % N), None, EQ, None, ["al"], ["eq%d" % i])
+    for i in range(2):
+        red(gcol[:, i:i + 1], eqs[:, 64 * i:64 * i + 64], ["eq%d" % i], ["gc%d" % i])
+    for i in range(2):
+        ts(T.bg[:, 32 * i:32 * i + 32], T.ones[:, :], gcol[:, i:i + 1], None, MUL, None, ["ones", "gc%d" % i], ["bg%d" % i])
+    ts(eqs[:, 128:192], T.al[:, :], float(me), None, EQ, None, ["al"], ["eq2"])
+    tr(T.tg[:, :], T.bg[:, :], ["bg0", "bg1"], ["tg"])
+    for i in range(2):
+        red(T.gs[:, i:i + 1], T.tg[:, 36 * i + 4:32 * i + 32], ["tg"], ["gs%d" % i])
+    act(T.eqj[:, :], eqs[:, 128:192], ["eq2"], ["eqj", "gme"], accum_out=T.gme[:, 0:1])
+    act(T.b3[:, :], T.ones[:, :], ["ones", "gme"], ["b3"], scale=T.gme[:, 0:1])
+
+    lim = float(LATE + CAP + 1)
+    ts(T.fa[:, :], T.wa[:, :], T.gs[:, 0:1], lim, ADD, GE, ["wa", "gs0"], ["fa"])
+    ts(T.fb[:, :], T.wb[:, :], T.gs[:, 1:2], lim, ADD, GE, ["wb", "gs1"], ["fb"])
+    scan2(T.cum[:, :], T.fa[:, :], T.fb[:, :], 0.0, ["fa", "fb"], ["cum"])
+    act(T.bm2[:, 32:64], T.ones[:, :], ["ones", "cum"], ["bm5"], scale=T.cum[:, 63:64])
+    tt(T.r2[:, :], T.fa[:, :], T.fb[:, :], ADD, ["fa", "fb"], ["r2"])
+    ts(T.bm2[:, 0:32], T.mlt[:, :], T.cum[:, 63:64], None, MUL, None, ["mlt", "cum"], ["bm4"])
+    tt(T.d2c[:, :], T.r2[:, :], T.cum[:, :], MUL, ["r2", "cum"], ["d2c"])
+    tr(T.p2[:, 32:96], T.bm2[:, :], ["bm4", "bm5"], ["p2"])
+    tr(T.tdc[:, :], T.d2c[:, :], ["d2c"], ["tdc"])
+    red(bcol[:, 4:5], T.p2[:, 31:64], ["p2", "p2k"], ["b2c"])
+    tt(T.m16[:, :], T.p2[:, 64:80], T.p2[:, 80:96], ADD, ["p2"], ["m16"])
+    ts(T.d2b[:, :], T.r2[:, :], bcol[:, 4:5], None, MUL, None, ["r2", "b2c"], ["d2b"])
+    tt(T.m8[:, :], T.m16[:, 0:8], T.m16[:, 8:16], ADD, ["m16"], ["m8"])
+    for c in (0, 2, 4):
+        send(calls[c][1], lambda z: T.m8[:, z:z + 1], lambda z: T.ml[:, place(z):place(z) + 1], calls[c][3], "mar", "mars", ["m8"])
+    cnt["mar"] = count_in
+    wr["mx"] = [("mar", count_in)]
+    tr(T.tdb[:, :], T.d2b[:, :], ["d2b"], ["tdb"])
+    tr(T.t3[:, :], T.b3[:, :], ["b3"], ["t3"])
+    scan2(T.cs2[:, 8:72], T.tdc[:, :], T.tdb[:, :], 0.0, ["tdc", "tdb"], ["cs2"])
+    tt(T.n16[:, :], T.t3[:, 0:32:2], T.t3[:, 1:32:2], ADD, ["t3"], ["n16"])
+    tt(T.s2[:, :], T.cs2[:, 15:72:8], T.cs2[:, 7:64:8], SUB, ["cs2", "cs2z"], ["s2"])
+    tt(T.n8[:, :], T.n16[:, 0:16:2], T.n16[:, 1:16:2], ADD, ["n16"], ["n8"])
+    tt(T.s8[:, :], T.s1[:, :], T.s2[:, :], MAX, ["s1", "s2"], ["s8"])
+    scan(T.n8s[:, :], T.n8[:, :], 8, 0.0, ["n8"], ["n8s"])
+    cp(T.off[:, :], T.s8[:, :], ["s8"], ["off"])
+    ts(T.ta[:, 0:180:9], T.j0[:, :], T.cb[:, 0:1], None, ADD, None, ["j0", "cb"], ["jj"])
+    cp(T.scat[:, 32:32 + WIN].indirect(T.off[:, 0:8]), T.vals[:, :], ["off", "vals", "sz0", "sz1"], ["scat"])
+
+    pp, bb, dd = T.pp, T.bb, T.dd
+    tw, hh, so = T.tw, T.hh, T.so
+    H = WIN // 2
+
+    def turn(i, late):
+        tr(tw[:, late * WIN + H * i:late * WIN + H * i + H], T.scat[:, 32 - 16 * late + H * i:32 - 16 * late + H * i + H],
+           ["scat"], ["tw%d%d" % (late, i)])
+
+    def join(i, late):
+        a = late * WIN + H * i
+        tt(hh[:, 20 * i + 1 - late:20 * i + 20:2], tw[:, a:a + H:32], tw[:, a + 16:a + H:32], ADD, ["tw%d%d" % (late, i)],
+           ["hh%d%d" % (late, i)])
+
+    def entries(i):
+        cp(so[:, 16 * i:16 * i + 16], hh[:, 0:20 * i + 20].indirect(T.gl[:, 2 * i:2 * i + 1]),
+           ["gl"] + ["hh%d%d" % (a, b) for a in range(2) for b in range(i + 1)], ["so%d" % i])
+
+    def pick(oq, os_, n, iq, is_, m, off, n0, reads, writes):
+        op("v", V.tensor_copy, (oq[:, n0:n0 + n].bitcast(dt.uint32), iq[:, 0:m].bitcast(dt.uint32).indirect(off)), reads, [writes + "q"])
+        act(os_[:, n0:n0 + n], is_[:, 0:m].indirect(off), reads, [writes + "s"])
+
+    def columns(call, sq, sp, key):
+        kind, zs, n, engines = call
+
+        def src(z):
+            c = SLOT * (z - zs[0])
+            return sq[:, c:c + n].bitcast(dt.uint8) if kind == "q" else sp[:, c:c + n]
+
+        def dst(z):
+            c = SLOT * place(z)
+            return T.land[:, c:c + n].bitcast(dt.uint8) if kind == "q" else T.lsc[:, c:c + n]
+        send(zs, src, dst, engines, "dat", "dats", [key + kind])
+
+    def wave(i, lists):
+        (sq, sp), zs, key = ((T.sq1, T.sp1), (T.sq2, T.sp2), (T.sq3, T.sp3))[i], calls[2 * i][1], "w%d" % i
+        za, zb = zs[0], zs[-1] + 1
+        pick(sq, sp, SLOT * (zb - za), T.xq, T.xs, TOK, so[:, 4 * za:4 * zb], 0, lists + ["xq"], key)
+        columns(calls[2 * i], sq, sp, key)
+        columns(calls[2 * i + 1], sq, sp, key)
+
+    turn(0, 0)
+    turn(0, 1)
+    join(0, 0)
+    join(0, 1)
+    turn(1, 0)
+    entries(0)
+    turn(1, 1)
+    wave(0, ["so0"])
+    join(1, 0)
+    join(1, 1)
+    tt(bb[:, 8:15], bb[:, 0:7], T.n8[:, 0:7], ADD, ["bb0", "n8"], ["bb8"])
+    entries(1)
+    ts(pp[:, 1:9], T.n8s[:, :], float(CAP), None, MIN, None, ["n8s"], ["pp1"])
+    wave(1, ["so0", "so1"])
+    wave(2, ["so0", "so1"])
+    pick(T.land, T.lsc, SLOT, T.xq, T.xs, TOK, so[:, 4 * own:4 * own + 4], 0, ["so1", "xq"], "own")
+
+    tt(pp[:, 9:10], pp[:, 8:9], T.m8[:, own:own + 1], ADD, ["pp1", "m8"], ["pp9"])
+    quant(T.land[:, ZERO:ZERO + NZ], T.lsc[:, ZERO:ZERO + NZ], T.zin[:, :], ["zin"], ["zq"])
+    scan2(pp[:, 10:17], T.ml[:, 1:8], T.z64[:, 0:7], pp[:, 9:10], ["mx", "z64", "pp9"], ["pp10"])
+    quant(T.wq[:, :], T.wsc[:, :], T["win"][:, :], ["win"], ["wq"])
+    places = ["pp0", "pp1", "pp9", "pp10"]
+    tt(T.de[:, 0:17], bb[:, 0:17], pp[:, 0:17], SUB, ["bb0", "bb8", "bb15", "bb16"] + places, ["de"])
+    tt(dd[:, 1:17], T.de[:, 1:17], T.de[:, 0:16], SUB, ["de"], ["dd"])
+    for q in range(1, 17):
+        t, i = (T.ta, q) if q < 9 else (T.tz, q - 8)
+        ts(t[:, i:180:9], T.ta[:, 0:180:9], pp[:, q:q + 1], dd[:, q:q + 1], GE, MUL, ["jj", "dd", "tzz"] + places, ["tm%d" % q])
+    scan2(T.cs3[:, 12:192], T.ta[:, :], T.tz[:, :], 0.0, ["jj", "tzz"] + ["tm%d" % q for q in range(1, 17)], ["cs3"])
+    tt(T.t20[:, :], T.cs3[:, 20:192:9], T.cs3[:, 11:183:9], SUB, ["cs3", "cs3z"], ["t20"])
+    ts(T.fo[:, :], T.t20[:, :], float(ZERO + NZ - 1), None, MIN, None, ["t20"], ["fo"])
+
+    cnt["dat"] = data_in
+    wr["dx"] = [("dat", data_in)]
+    got = ["dx", "ownq", "owns", "zq", "fo"]
+    cut = 128
+    for i, (a, b) in enumerate(((0, cut), (cut, ROOM))):
+        pick(T.fq, T.fs, b - a, T.land, T.lsc, ZERO + NZ, T.fo[:, a // 16:b // 16], a, got, "f%d" % i)
+    low, top = ["f0q", "f0s"], ["f1q", "f1s"]
+    pieces = [(0, 0, cut, low), (1, 0, cut, low), (0, cut, ROOM, top), (1, cut, ROOM, top)]
+    for o in range(2, O):
+        pieces += [(o, 0, ROOM // 2, low + top), (o, ROOM // 2, ROOM, low + top)]
+    for i, (o, a, b, keys) in enumerate(pieces):
+        op("t", g.tensor.matmul_mx, (T.acc[:, 512 * i:512 * i + b - a], T.wq[:, 128 * o:128 * o + 128], T.wsc[:, 128 * o:128 * o + 128],
+                                     T.fq[:, a:b], T.fs[:, a:b], True, True), ["wq"] + keys, ["acc%d" % i])
+    for i, (o, a, b, keys) in enumerate(pieces):
+        src, dst = T.acc[:, 512 * i:512 * i + b - a], T.yo[:, ROOM * o + a:ROOM * o + b]
+        (cp if i in (0, 1, 3, 4, 6) else act)(dst, src, ["acc%d" % i], ["yo%d" % i])
+        if o < 2:
+            dma("y", "dy", T.y[:, ROOM * o + a:ROOM * o + b], dst, ["yo%d" % i], ["yout"], more=True)
+        elif a > 0:
+            dma("y", "dy", T.y[:, ROOM * o:ROOM * o + ROOM], T.yo[:, ROOM * o:ROOM * o + ROOM], ["yo%d" % (i - 1), "yo%d" % i],
+                ["yout"], more=True)
+    for sem in sorted(cnt):
+        need("y", (sem, None))

@@ -9,7 +9,9 @@ NZ = 128
 WSLOT = 80
 WIN = N * WSLOT
 BACK = 9
-LATE = 400
+LIMIT = 672
+LATE = LIMIT - CAP - 1
+BIG = 1024.0
 
 
 def _sb(n, d):
@@ -21,61 +23,113 @@ SCRATCH = {
     "lists": ("dram", [N, 128, 2], I32),
     "ct": _sb(32, I32), "xin": _sb(4 * TOK, B16), "win": _sb(512 * O, B16), "zin": _sb(4 * NZ, B16),
     "xq": _sb(TOK, MX), "xs": _sb(TOK, U8), "wq": _sb(128 * O, MX), "wsc": _sb(128 * O, U8),
-    "ra": _sb(128, F32), "ca": _sb(128, F32), "rb": _sb(64, F32), "cb": _sb(64, F32), "e64": _sb(64, I32), "ec": _sb(64, I32),
-    "gr": _sb(64, F32), "gt": _sb(64, F32), "gl": _sb(4, U16), "zpos": _sb(8, F32), "zfix": _sb(8, F32),
-    "l4": _sb(4, I32), "l64": _sb(4, U16), "meq": _sb(32, F32), "meqn": _sb(32, F32), "mgt": _sb(32, F32), "mlt": _sb(32, F32),
-    "v128": _sb(128, B16), "vals": _sb(128, B16), "j0": _sb(20, I32), "ones": _sb(32, F32), "z64": _sb(64, F32),
-    "pre": _sb(256, B16), "mt": _sb(256, B16), "tcol": _sb(8, F32), "bm": _sb(128, F32), "tb": _sb(168, F32), "bcol": _sb(8, F32),
+    "ra": _sb(160, F32), "ca": _sb(128, F32), "e64": _sb(64, I32), "ec": _sb(64, I32), "cut": _sb(64, F32),
+    "gr": _sb(64, F32), "gt": _sb(64, F32), "gl": _sb(4, U16), "l4": _sb(4, I32), "l64": _sb(4, U16),
+    "mk": _sb(96, F32), "mgt": _sb(32, F32), "kc": _sb(8, F32),
+    "v128": _sb(128, B16), "vals": _sb(128, B16), "j0": _sb(20, I32), "z64": _sb(96, B16),
+    "pre": _sb(256, B16), "mt": _sb(256, B16), "tcol": _sb(8, F32), "bm": _sb(160, F32), "tb": _sb(192, F32), "bcol": _sb(8, F32),
     "sc1": _sb(64, F32), "d1": _sb(64, F32), "sca": _sb(64, F32), "scb": _sb(64, F32), "wa": _sb(64, F32), "wb": _sb(64, F32),
-    "qa": _sb(64, B16), "qb": _sb(64, B16), "td1": _sb(64, F32), "cs1": _sb(72, F32), "s1": _sb(8, F32),
-    "al": _sb(64, I32), "eqs": _sb(192, B16), "eqj": _sb(64, B16), "gcol": _sb(8, F32), "gme": _sb(8, F32), "bg": _sb(64, F32),
-    "tg": _sb(64, F32), "gs": _sb(8, F32), "b3": _sb(32, F32), "t3": _sb(32, F32), "n16": _sb(16, F32), "n8": _sb(8, F32),
+    "qa": _sb(64, B16), "qb": _sb(64, B16),
+    "al": _sb(64, I32), "eqs": _sb(192, B16), "bg": _sb(192, B16), "tg": _sb(64, B16), "gs": _sb(8, F32),
+    "n16": _sb(16, F32), "n8": _sb(8, B16), "nl": _sb(128, B16), "cap": _sb(16, F32),
     "fa": _sb(64, B16), "fb": _sb(64, B16), "r2": _sb(64, B16), "cum": _sb(64, F32), "bm2": _sb(64, F32), "p2": _sb(96, F32),
-    "m16": _sb(16, F32), "m8": _sb(8, F32), "d2c": _sb(64, F32), "d2b": _sb(64, F32), "tdc": _sb(64, F32), "tdb": _sb(64, F32),
-    "cs2": _sb(72, F32), "s2": _sb(8, F32), "s8": _sb(8, F32), "off": _sb(8, U16),
+    "m16": _sb(16, F32), "m8": _sb(8, B16), "lid": _sb(64, F32), "c2b": _sb(64, F32), "d2": _sb(64, F32), "td2": _sb(64, F32),
+    "cs2": _sb(64, F32), "off": _sb(8, U16),
     "scat": _sb(WIN + 32, B16), "tw": _sb(2 * WIN, B16), "hh": _sb(WIN // 16, F32), "so": _sb(4 * N, U16),
-    "sq1": _sb(2 * SLOT, MX), "sp1": _sb(2 * SLOT, U8), "sq2": _sb(4 * SLOT, MX), "sp2": _sb(4 * SLOT, U8),
-    "sq3": _sb(SLOT, MX), "sp3": _sb(SLOT, U8),
+    "sq0": _sb(2 * SLOT, MX), "sp0": _sb(2 * SLOT, U8), "sq1": _sb(2 * SLOT, MX), "sp1": _sb(2 * SLOT, U8),
+    "sq2": _sb(3 * SLOT, MX), "sp2": _sb(3 * SLOT, U8),
+    "hn": _sb(2, B16), "hq": _sb(2 * SLOT, MX), "hs": _sb(2 * SLOT, U8),
     "land": _sb(ZERO + NZ, MX), "lsc": _sb(ZERO + NZ, U8),
-    "n8s": _sb(8, F32), "pp": _sb(24, F32), "bb": _sb(24, F32), "de": _sb(24, F32), "dd": _sb(24, F32), "ml": _sb(8, F32),
+    "pp": _sb(24, F32), "bb": _sb(24, F32), "de": _sb(24, F32), "dd": _sb(24, F32),
     "ta": _sb(180, F32), "tz": _sb(180, F32), "cs3": _sb(192, F32), "t20": _sb(20, F32),
     "fo": _sb(20, U16), "fq": _sb(ROOM, MX), "fs": _sb(ROOM, U8),
     "acc": ("psum", [128, 512 * 2 * O], F32), "yo": _sb(ROOM * O, F32),
 }
-SEMAPHORES = ["cv", "cs", "cg", "ct", "dl0", "dc1", "dc2", "dx", "dw", "dal", "dy",
-              "lst", "lsts", "mar", "mars", "dat", "dats"]
+SEMAPHORES = ["cv", "cs", "cg", "ct", "dl0", "dc1", "dc2", "dx", "dw0", "dw1", "dal", "dy", "lst", "num", "mar",
+              "dat", "hn", "hq", "hs", "left"]
 
 ADD, SUB, MUL, MIN, MAX = AluOpType.add, AluOpType.subtract, AluOpType.mult, AluOpType.min, AluOpType.max
 GE, GT, EQ = AluOpType.is_ge, AluOpType.is_gt, AluOpType.is_equal
 AND = AluOpType.bitwise_and
-COPY, IDENT = ActivationFunctionType.Copy, ActivationFunctionType.Identity
+COPY, IDENT, SIGN = ActivationFunctionType.Copy, ActivationFunctionType.Identity, ActivationFunctionType.Sign
+
+
+def deal(keys, engines):
+    k = len(engines) // len(keys)
+    return {z: engines[k * i:k * i + k] for i, z in enumerate(keys)}
 
 
 def plan(me, cores, topo):
     core = cores[me]
-    mate = [r for r in range(N) if r != me and topo.chip(cores[r]) == topo.chip(core)][0]
-    near = (mate - me - 1) % N
+    to = [cores[(me + 1 + z) % N] for z in range(N - 1)]
+    near = [z for z in range(N - 1) if topo.chip(to[z]) == topo.chip(core)][0]
     far = [z for z in range(N - 1) if z != near]
-    out = topo.engines(core, cores[(me + 1 + far[0]) % N])
-    inn = [e for e in topo.engines(core, cores[mate]) if e not in out]
+    pairs = [far[0:2], far[2:4], far[4:6]]
+    out = topo.engines(core, to[far[0]])
+    inn = [e for e in topo.engines(core, to[near]) if e not in out]
+    turn = sorted((core, to[near])).index(core)
+    free = [c for c in topo.cores_of(core) if c not in cores]
+    wide = [c for c in free if topo.may_write(c, to[far[0]])]
+    other = [c for c in free if c not in wide and topo.die(c) != topo.die(core)]
+    same = [c for c in free if c not in wide and topo.die(c) == topo.die(core)]
+    helpers = {wide[turn]: pairs[0], other[turn]: pairs[1][:1], same[turn]: pairs[1][1:]}
+    every = out + inn
+    return {"near": near, "pairs": pairs, "helpers": helpers, "out": out, "inn": inn, "to": to, "lists": out[::4],
+            "handed": [{wide[turn]: every}, deal([other[turn], same[turn]], every)],
+            "numbers": {wide[turn]: inn[:4], **deal([other[turn], same[turn]], inn[4:])},
+            "counts": {**deal(pairs[2], out[:4]), near: out[4:]}, "straight": {**deal(pairs[2], out), near: inn},
+            "seconds": [{**deal(far[:2], out), near: inn}, deal(far[2:], out)]}
 
-    def deal(zs):
-        k = len(out) // len(zs)
-        return {z: out[k * i:k * i + k] for i, z in enumerate(zs)}
 
-    calls = []
-    for zs, e in ((far[:2], deal(far[:2])), (far[2:], deal(far[2:])), ([near], {near: inn})):
-        n = SLOT if min(zs) < 2 else BOTH
-        calls += [("q", zs, n, e), ("s", zs, n, e)]
-    return near, calls, out[::4]
+def mask(engines):
+    m = 0
+    for e in engines:
+        m |= 1 << e
+    return m
+
+
+def at(core, topo):
+    rid, pid, _ = topo.addr(core)
+    return DstId(rid=rid, pnc=pid)
+
+
+def codes(buf, c, n):
+    return buf[:, c:c + n].bitcast(dt.uint8)
+
+
+def place(z):
+    return N - 1 - z
+
+
+def number(T, k, n):
+    return T.nl[:, 8 * k:8 * k + n]
+
+
+def helper_program(g, p, core, T, topo):
+    zs = p["helpers"][core]
+    n = SLOT if min(zs) < 2 else BOTH
+    engines = deal(zs, p["out"])
+    every = sum(len(e.get(core, [])) for e in p["handed"])
+    for sem, count, far, src, dst in (
+            ("hn", len(p["numbers"][core]), "num", lambda j: T.hn[:, j:j + 1], lambda k: number(T, k, 1)),
+            ("hq", every, "dat", lambda j: codes(T.hq, SLOT * j, n), lambda k: codes(T.land, SLOT * k, n)),
+            ("hs", every, "dat", lambda j: T.hs[:, SLOT * j:SLOT * j + n], lambda k: T.lsc[:, SLOT * k:SLOT * k + n])):
+        g.wait_ge(T.sem[sem], count)
+        g.remote_dma_fused([RemoteDMATransfer(dst_ids=[at(p["to"][z], topo)], dma_engine_mask=mask(engines[z]), remote_sem=T.sem[far],
+                                              src=src(j), dst=dst(place(z))) for j, z in enumerate(zs)], local_sem=T.sem["left"])
+    g.wait_ge(T.sem["left"], 3 * len(p["out"]))
 
 
 def rank_program(g, core, T, topo):
+    cores = [int(c) for c in T.cores]
     me = T.rank_of(core)
     if me is None:
+        for r in range(N):
+            p = plan(r, cores, topo)
+            if core in p["helpers"]:
+                helper_program(g, p, core, T, topo)
         return
-    cores = [int(c) for c in T.cores]
-    near, calls, few = plan(me, cores, topo)
+    p = plan(me, cores, topo)
     own = N - 1
     queue = {"v": g.vector, "s": g.scalar, "t": g.tensor, "g": g, "y": g.sync}
     cnt, seen, wr, rd = {}, {}, {}, {}
@@ -91,7 +145,7 @@ def rank_program(g, core, T, topo):
     def before(q, reads, writes):
         toks = {}
         for k in reads:
-            for t in wr.get(k, []):
+            for t in wr[k]:
                 toks.setdefault(t[0], []).append(t)
         for k in writes:
             for t in wr.get(k, []) + rd.get(k, []):
@@ -115,14 +169,11 @@ def rank_program(g, core, T, topo):
         cnt[sem] = cnt.get(sem, 0) + 1
         after((sem, cnt[sem]), reads, writes, False)
 
-    def dma(q, sem, out, in_, reads, writes, more=False):
-        if not more:
-            before(q, reads, writes)
-        else:
-            before(q, reads, [])
+    def dma(q, sem, out, in_, reads, writes):
+        before(q, reads, [])
         queue[q].dma_start(out, in_).then_inc(T.sem[sem], 16)
         cnt[sem] = cnt.get(sem, 0) + 16
-        after((sem, None), reads, writes, more)
+        after((sem, None), reads, writes, True)
 
     V = g.vector
 
@@ -136,8 +187,8 @@ def rank_program(g, core, T, topo):
     def cp(out, a, reads, writes):
         op("v", V.tensor_copy, (out, a), reads, writes)
 
-    def red(out, a, reads, writes):
-        op("v", V.tensor_reduce, (out, a, AxisListType.X, ADD), reads, writes)
+    def red(out, a, reads, writes, **kw):
+        op("v", V.tensor_reduce, (out, a, AxisListType.X, ADD), reads, writes, **kw)
 
     def tr(out, a, reads, writes):
         op("v", V.transpose, (out, a), reads, writes)
@@ -151,184 +202,168 @@ def rank_program(g, core, T, topo):
     def scan(out, a, n, init, reads, writes):
         scan2(out, a, T.z64[:, 0:n], init, reads + ["z64"], writes)
 
+    def top8(out, a, reads, writes):
+        op("v", V.tensor_tensor_scan, (out, T.cut[:, :], a, 0.0, MIN, MAX), reads + ["cut"], writes)
+
     def fill(ap, val, key):
         op("v", V.memset, (ap, val), [], [key])
 
-    def iota(ap, key, pattern, base, flag=False):
+    def iota(ap, key, pattern, base, flag=True):
         kw = {"allow_small_or_imprecise_dtypes": True} if flag else {}
         op("g", g.iota, (ap, pattern, base, 0), [], [key], **kw)
 
     def act(out, a, reads, writes, **kw):
         op("s", g.scalar.activation, (out, a, COPY), reads, writes, **kw)
 
-    def at(z):
-        rid, pid, _ = topo.addr(cores[(me + 1 + z) % N])
-        return DstId(rid=rid, pnc=pid)
+    def line(out, a, scale, bias, reads, writes):
+        op("s", g.scalar.activation, (out, a, IDENT, bias, scale), reads, writes)
 
-    def place(z):
-        return N - 1 - z
-
-    def mask(engines):
-        m = 0
-        for e in engines:
-            m |= 1 << e
-        return m
-
-    def send(zs, src, dst, engines, sem, lsem, reads):
+    def call(transfers, reads):
         before("g", reads, [])
-        g.remote_dma_fused([RemoteDMATransfer(dst_ids=[at(z)], dma_engine_mask=mask(engines[z]),
-                                              remote_sem=T.sem[sem], src=src(z), dst=dst(z)) for z in zs], local_sem=T.sem[lsem])
-        cnt[lsem] = cnt.get(lsem, 0) + sum(len(engines[z]) for z in zs)
+        g.remote_dma_fused([RemoteDMATransfer(dst_ids=[at(c, topo) for c in to], dma_engine_mask=mask(e), remote_sem=T.sem[sem],
+                                              srcs=[src], dsts=dst) for to, e, sem, src, dst in transfers], local_sem=T.sem["left"])
+        cnt["left"] = cnt.get("left", 0) + sum(len(t[1]) for t in transfers)
 
-    data_in = list_in = count_in = 0
+    cnt["lst"] = cnt["num"] = cnt["mar"] = cnt["dat"] = 0
     for k in range(1, N):
-        _, c2, f2 = plan((me + k) % N, cores, topo)
-        z = N - 1 - k
-        data_in += sum(len(e[z]) for _, zs, _, e in c2 if z in zs)
-        count_in += sum(len(e[z]) for kind, zs, _, e in c2 if z in zs and kind == "q")
-        list_in += len(f2)
+        o, z = plan((me + k) % N, cores, topo), N - 1 - k
+        handed = sum(len(o["out"]) // len(zs) for zs in o["helpers"].values() if z in zs)
+        cnt["lst"] += len(o["lists"])
+        cnt["num"] += len(o["counts"][z]) if z in o["counts"] else handed
+        cnt["mar"] += sum(len(e.get(z, [])) for e in o["seconds"])
+        cnt["dat"] += 2 * (len(o["straight"][z]) if z in o["straight"] else handed)
+    for sem in ("lst", "num", "mar", "dat"):
+        wr[sem] = [(sem, cnt[sem])]
 
     dma("y", "dl0", T.lists[0], T.c1[:, :], [], ["l0"])
     for b in range(8):
-        dma("ys"[b % 2], "dc1", T.ct[16 * b:16 * b + 16, 0:16], T.c1[:, :], [], ["c1"], more=True)
+        dma("ys"[b % 2], "dc1", T.ct[16 * b:16 * b + 16, 0:16], T.c1[:, :], [], ["c1"])
     for b in range(8):
-        dma("sy"[b % 2], "dc2", T.ct[16 * b:16 * b + 16, 16:32], T.c2[:, :], [], ["c2"], more=True)
+        dma("sy"[b % 2], "dc2", T.ct[16 * b:16 * b + 16, 16:32], T.c2[:, :], [], ["c2"])
     dma("y", "dx", T.xin[:, :], T.x[:, :], [], ["xin"])
+    dma("y", "dw0", T["win"][:, 0:1024], T.w[:, 0:1024], [], ["win0"])
 
-    ra, rb = T.ra, T.rb
-    iota(T.l4[:, :], "l4", [[2, 2], [8, 2]], 0)
-    iota(ra[:, 64:96], "ra2", [[1, 2], [4, 2], [0, 8]], 0, flag=True)
-    iota(ra[:, 0:32], "ra0", [[0, 4], [1, 8]], 0, flag=True)
-    iota(ra[:, 32:64], "ra1", [[1, 4], [0, 8]], 0, flag=True)
-    iota(ra[:, 96:128], "ra3", [[0, 4], [WSLOT, 8]], -1, flag=True)
-    iota(T.e64[:, :], "e64", [[1, 64]], me + 1)
-    others = [z for z in range(N) if z != own]
-    before("g", ["l0"], [])
-    g.remote_dma_fused([RemoteDMATransfer(dst_ids=[at(z) for z in others], dma_engine_mask=mask(few), remote_sem=T.sem["lst"],
-                                          srcs=[T.lists[0]], dsts=[T.lists[place(z)] for z in others])], local_sem=T.sem["lsts"])
-    cnt["lsts"] = len(few)
-    cnt["lst"] = list_in
-    wr["lx"] = [("lst", list_in)]
-    iota(rb[:, 32:64], "rb1", [[16, 2], [0, 16]], 0, flag=True)
-    iota(rb[:, 0:32], "rb0", [[0, 2], [1, 16]], 0, flag=True)
-    iota(T.v128[:, :], "v128", [[32, 2], [64, 4], [1, 16]], 0, flag=True)
-    iota(T.gr[:, 0:32], "gr0", [[-1, 2], [WSLOT // 16, 4], [1, 4]], 1, flag=True)
-    iota(T.gr[:, 32:64], "gr1", [[-1, 2], [WSLOT // 16, 4], [1, 4]], 1 + WSLOT // 4, flag=True)
-    iota(T.gr[:, 3:32:16], "gr0", [[-1, 2]], 1 + BACK, flag=True)
-    iota(T.j0[:, :], "j0", [[16, 20]], 0)
-    iota(T.bb[:, 0:8], "bb0", [[SLOT, 8]], 0, flag=True)
+    ra, kc, mk, pp, bb, dd = T.ra, T.kc, T.mk, T.pp, T.bb, T.dd
+    iota(ra[:, 64:96], "ra1", [[1, 2], [4, 2], [0, 8]], 0)
+    iota(ra[:, 0:64], "ra0", [[0, 8], [1, 8]], 0)
+    iota(ra[:, 96:128], "ra2", [[1, 4], [0, 8]], 0)
+    iota(ra[:, 128:160], "ra3", [[16, 2], [0, 16]], 0)
+    iota(T.l4[:, :], "l4", [[2, 2], [8, 2]], 0, flag=False)
+    iota(T.e64[:, :], "e64", [[1, 64]], me + 1, flag=False)
+    call([(p["to"], p["lists"], "lst", T.lists[0], [T.lists[place(z)] for z in range(N - 1)])], ["l0"])
+    iota(T.v128[:, :], "v128", [[32, 2], [64, 4], [1, 16]], 0)
 
-    fill(T.ones[:, :], 1.0, "ones")
+    def later():
+        iota(T.gr[:, 0:32], "gr0", [[-1, 2], [WSLOT // 16, 4], [1, 4]], 1)
+        iota(T.gr[:, 32:64], "gr1", [[-1, 2], [WSLOT // 16, 4], [1, 4]], 1 + WSLOT // 4)
+        iota(T.gr[:, 3:32:16], "gr0", [[-1, 2]], 1 + BACK)
+        iota(T.j0[:, :], "j0", [[16, 20]], 0, flag=False)
+        iota(bb[:, 0:8], "bb0", [[SLOT, 8]], 0)
+        iota(T.cap[:, :], "cap", [[int(BIG), 2], [0, 8]], CAP)
+        iota(bb[:, 15:17], "bb15", [[SLOT - FIRST, 2]], SLOT * (N - 1) + FIRST)
+
+    fill(T.scat[:, :], 0.0, "scat")
     fill(T.z64[:, :], 0.0, "z64")
-    fill(T.cs1[:, 0:8], 0.0, "cs1z")
-    fill(T.cs2[:, 0:8], 0.0, "cs2z")
-    fill(T.pp[:, 0:1], 0.0, "pp0")
+    fill(mk[:, 32:64], 1.0, "ones")
+    fill(T.eqs[:, 0:192], 0.0, "eqz")
     fill(T.zin[:, :], 0.0, "zin")
-    fill(T.tz[:, :], 0.0, "tzz")
-    fill(T.cs3[:, 0:12], 0.0, "cs3z")
-    fill(T.bb[:, 15:16], float(SLOT * (N - 1) + FIRST), "bb15")
-    fill(T.bb[:, 16:17], float(ZERO), "bb16")
-    tr(T.ca[:, :], ra[:, :], ["ra0", "ra1", "ra2", "ra3"], ["ca"])
-    zc, hc, pc, sc = [T.ca[:, 32 * j:32 * j + 1] for j in range(4)]
-    ts(T.ec[:, :], T.e64[:, :], 7, None, AND, None, ["e64"], ["ec"])
+    tr(T.ca[:, :], ra[:, 32:160], ["ra0", "ra1", "ra2", "ra3"], ["ca"])
+    zc, pc, hc, odd = [T.ca[:, 32 * j:32 * j + 1] for j in range(4)]
+    zpos, t1, t2, q4, qc = [kc[:, j:j + 1] for j in range(5)]
     ts(T.l64[:, :], T.l4[:, :], pc, None, ADD, None, ["l4", "ca"], ["l64"])
-    ts(T.meq[:, :], ra[:, 0:32], zc, None, EQ, None, ["ra0", "ca"], ["meq"])
-    ts(T.mgt[:, :], ra[:, 32:64], hc, None, GT, None, ["ra1", "ca"], ["mgt"])
-    ts(T.zpos[:, 0:1], zc, 0.0, None, GT, None, ["ca"], ["zpos"])
-    ts(T.zfix[:, 0:1], zc, 0.0, 16.0 * BACK, EQ, MUL, ["ca"], ["zfix"])
-    tt(T.mlt[:, :], T.meq[:, :], T.mgt[:, :], MUL, ["meq", "mgt"], ["mlt"])
-    ts(T.meqn[:, :], ra[:, 0:32], zc, T.zpos[:, 0:1], EQ, MUL, ["ra0", "ca", "zpos"], ["meqn"])
-    act(T.tb[:, 31:32], sc, ["ca"], ["tb0"])
-    op("s", g.scalar.activation, (T.tb[:, 160:161], T.zfix[:, 0:1], IDENT, sc), ["zfix", "ca"], ["tb1"])
+    ts(mk[:, 64:96], ra[:, 0:32], zc, None, EQ, None, ["ra0", "ca"], ["meq"])
+    ts(T.mgt[:, :], ra[:, 96:128], hc, None, GT, None, ["ra2", "ca"], ["mgt"])
+    ts(T.ec[:, :], T.e64[:, :], 7, None, AND, None, ["e64"], ["ec"])
+    tt(mk[:, 0:32], mk[:, 64:96], T.mgt[:, :], MUL, ["meq", "mgt"], ["mlt"])
+    line(T.tb[:, 31:32], zc, float(WSLOT), -1.0, ["ca"], ["tb0"])
+    op("s", g.scalar.activation, (zpos, zc, SIGN), ["ca"], ["zpos"])
+    line(t1, zc, float(WSLOT), 16.0 * BACK - 1, ["ca"], ["t1"])
+    line(t2, zpos, -16.0 * BACK, t1, ["zpos", "t1"], ["t2"])
+    line(T.cut[:, :], ra[:, 0:64], 4 * BIG, 0.0, ["ra0"], ["cut"])
+    line(q4, odd, -1 / 16, pc, ["ca"], ["q4"])
+    line(qc, q4, 2.0, zc, ["q4", "ca"], ["qc"])
 
     l64 = T.l64[:, 0:4]
     c1w, c2w = T.ct[:, 0:16].indirect(l64), T.ct[:, 16:32].indirect(l64)
     m1, ma, mb, mc = [T.mt[:, 64 * i:64 * i + 64] for i in range(4)]
     tt(T.pre[:, 0:64], c1w, T.ec[:, :], EQ, ["c1", "l64", "ec"], ["pre0"])
     ts(T.pre[:, 64:128], c1w, float((me + 1) % N), None, EQ, None, ["c1", "l64"], ["pre1"])
+    tr(m1, T.pre[:, 0:64], ["pre0"], ["m1"])
     ts(T.pre[:, 128:192], c1w, float((me + 2) % N), None, EQ, None, ["c1", "l64"], ["pre2"])
+    red(T.tcol[:, 0:1], m1, ["m1"], ["tcol0"])
+    fill(T.cs3[:, 0:12], 0.0, "cs3z")
+    ts(T.bm[:, 0:96], mk[:, :], T.tcol[:, 0:1], None, MUL, None, ["meq", "mlt", "ones", "tcol0"], ["bm0"])
+    fill(pp[:, 0:1], 0.0, "pp0")
+    tr(T.tb[:, 32:128], T.bm[:, 0:96], ["bm0"], ["tb"])
     tt(T.pre[:, 192:256], c2w, T.ec[:, :], EQ, ["c2", "l64", "ec"], ["pre3"])
-    tr(T.mt[:, :], T.pre[:, :], ["pre0", "pre1", "pre2", "pre3"], ["mt"])
-    for i, m in enumerate((m1, ma, mb)):
+    tt(T.n16[:, :], T.tb[:, 64:80], T.tb[:, 80:96], ADD, ["tb"], ["n16"])
+    tr(T.mt[:, 64:256], T.pre[:, 64:256], ["pre1", "pre2", "pre3"], ["mt"])
+    tt(T.n8[:, :], T.n16[:, 0:8], T.n16[:, 8:16], ADD, ["n16"], ["n8"])
+    call([([h], p["numbers"][h], "hn", T.n8[:, zs[0]:zs[0] + 2], [T.hn[:, :]]) for h, zs in p["helpers"].items()]
+         + [([p["to"][z]], e, "num", T.n8[:, z:z + 2], [number(T, place(z), 2)]) for z, e in p["counts"].items()], ["n8"])
+    act(number(T, 0, 1), T.n8[:, own:own + 1], ["n8"], ["nl0"])
+    later()
+    for i, m in ((1, ma), (2, mb)):
         red(T.tcol[:, i:i + 1], m, ["mt"], ["tcol%d" % i])
-    ts(T.bm[:, 0:32], T.mlt[:, :], T.tcol[:, 0:1], None, MUL, None, ["mlt", "tcol0"], ["bm0"])
-    ts(T.bm[:, 32:64], T.mlt[:, :], T.tcol[:, 1:2], LATE / 32, MUL, ADD, ["mlt", "tcol1"], ["bm1"])
-    ts(T.bm[:, 64:96], T.mlt[:, :], T.tcol[:, 2:3], LATE / 32, MUL, ADD, ["mlt", "tcol2"], ["bm2"])
-    ts(T.bm[:, 96:128], T.meqn[:, :], T.tcol[:, 0:1], None, MUL, None, ["meqn", "tcol0"], ["bm3"])
-    tr(T.tb[:, 32:160], T.bm[:, :], ["bm0", "bm1", "bm2", "bm3"], ["tb"])
-    tr(T.cb[:, :], rb[:, :], ["rb0", "rb1"], ["cb"])
-    tt(T.qa[:, :], ma, mc, MUL, ["mt"], ["qa"])
     bcol = T.bcol
-    red(bcol[:, 1:2], T.tb[:, 64:96], ["tb"], ["ba"])
-    red(bcol[:, 2:3], T.tb[:, 96:128], ["tb"], ["bq"])
     red(bcol[:, 0:1], T.tb[:, 31:64], ["tb", "tb0"], ["b1"])
-    red(T.p2[:, 31:32], T.tb[:, 128:161], ["tb", "tb1"], ["p2k"])
+    ts(T.bm[:, 96:128], mk[:, 0:32], T.tcol[:, 1:2], LATE / 32, MUL, ADD, ["mlt", "tcol1"], ["bm1"])
+    ts(T.bm[:, 128:160], mk[:, 0:32], T.tcol[:, 2:3], LATE / 32, MUL, ADD, ["mlt", "tcol2"], ["bm2"])
+    red(bcol[:, 3:4], T.tb[:, 96:128], ["tb"], ["nz"])
+    tr(T.tb[:, 128:192], T.bm[:, 96:160], ["bm1", "bm2"], ["tc"])
+    line(T.p2[:, 31:32], bcol[:, 3:4], zpos, t2, ["nz", "zpos", "t2"], ["p2k"])
+    scan(T.sc1[:, :], m1, 64, bcol[:, 0:1], ["m1", "b1"], ["sc1"])
+    red(bcol[:, 1:2], T.tb[:, 128:160], ["tc"], ["ba"])
+    red(bcol[:, 2:3], T.tb[:, 160:192], ["tc"], ["bq"])
+    tt(T.qa[:, :], ma, mc, MUL, ["mt"], ["qa"])
     scan(T.sca[:, :], ma, 64, bcol[:, 1:2], ["mt", "ba"], ["sca"])
     scan(T.scb[:, :], mb, 64, bcol[:, 2:3], ["mt", "bq"], ["scb"])
-    scan(T.sc1[:, :], m1, 64, bcol[:, 0:1], ["mt", "b1"], ["sc1"])
     tt(T.qb[:, :], mb, mc, MUL, ["mt"], ["qb"])
     tt(T.wa[:, :], T.qa[:, :], T.sca[:, :], MUL, ["qa", "sca"], ["wa"])
-    tt(T.d1[:, :], m1, T.sc1[:, :], MUL, ["mt", "sc1"], ["d1"])
     tt(T.wb[:, :], T.qb[:, :], T.scb[:, :], MUL, ["qb", "scb"], ["wb"])
-    tr(T.td1[:, :], T.d1[:, :], ["d1"], ["td1"])
+    tt(T.d1[:, :], m1, T.sc1[:, :], MUL, ["m1", "sc1"], ["d1"])
     quant(T.xq[:, :], T.xs[:, :], T.xin[:, :], ["xin"], ["xq"])
-    scan(T.cs1[:, 8:72], T.td1[:, :], 64, 0.0, ["td1"], ["cs1"])
-    tr(T.gt[:, :], T.gr[:, :], ["gr0", "gr1"], ["gt"])
-    tt(T.s1[:, :], T.cs1[:, 15:72:8], T.cs1[:, 7:64:8], SUB, ["cs1", "cs1z"], ["s1"])
-    cp(T.gl[:, 0:4:2], T.gt[:, 0:64:32], ["gt"], ["gl"])
+    quant(T.land[:, ZERO:ZERO + NZ], T.lsc[:, ZERO:ZERO + NZ], T.zin[:, :], ["zin"], ["zq"])
+    fill(T.tz[:, 0:180:9], 0.0, "tzz")
+    quant(T.wq[:, 0:256], T.wsc[:, 0:256], T["win"][:, 0:1024], ["win0"], ["wq0"])
 
+    line(T.vals[:, :], T.v128[:, :], 1.0, odd, ["v128", "ca"], ["vals"])
     for b in range(4):
-        dma("ys"[b % 2], "dal", T.al[32 * b:32 * b + 32, 0:64], T.lists[:, :, :], ["lx", "l0"], ["al"], more=True)
-    dma("y", "dw", T["win"][:, :], T.w[:, :], ["lx"], ["win"])
-    op("s", g.scalar.activation, (T.vals[:, :], T.v128[:, :], IDENT, T.cb[:, 32:33]), ["v128", "cb"], ["vals"])
-    half = (WIN + 32) // 2
+        dma("ys"[b % 2], "dal", T.al[32 * b:32 * b + 32, 0:64], T.lists[:, :, :], ["lst", "l0"], ["al"])
+    dma("y", "dw1", T["win"][:, 1024:2048], T.w[:, 1024:2048], ["lst"], ["win1"])
+    eqs = T.eqs
     for i in range(2):
-        act(T.scat[:, half * i:half * i + half], T.zin[:, 0:half], ["zin"], ["sz%d" % i])
-    eqs, gcol = T.eqs, T.gcol
+        ts(eqs[:, 96 * i:96 * i + 64], T.al[:, :], float((me + 1 + i) % N), None, EQ, None, ["al", "eqz"], ["eq%d" % i])
     for i in range(2):
-        ts(eqs[:, 64 * i:64 * i + 64], T.al[:, :], float((me + 1 + i) % N), None, EQ, None, ["al"], ["eq%d" % i])
+        scan(T.bg[:, 96 * i:96 * i + 96], eqs[:, 96 * i:96 * i + 96], 96, -LIMIT / (28.0 - 4 * i), ["eq%d" % i, "eqz"], ["bg%d" % i])
     for i in range(2):
-        red(gcol[:, i:i + 1], eqs[:, 64 * i:64 * i + 64], ["eq%d" % i], ["gc%d" % i])
+        tr(T.tg[:, 32 * i:32 * i + 32], T.bg[:, 96 * i + 64:96 * i + 96], ["bg%d" % i], ["tg%d" % i])
     for i in range(2):
-        ts(T.bg[:, 32 * i:32 * i + 32], T.ones[:, :], gcol[:, i:i + 1], None, MUL, None, ["ones", "gc%d" % i], ["bg%d" % i])
-    ts(eqs[:, 128:192], T.al[:, :], float(me), None, EQ, None, ["al"], ["eq2"])
-    tr(T.tg[:, :], T.bg[:, :], ["bg0", "bg1"], ["tg"])
-    for i in range(2):
-        red(T.gs[:, i:i + 1], T.tg[:, 36 * i + 4:32 * i + 32], ["tg"], ["gs%d" % i])
-    act(T.eqj[:, :], eqs[:, 128:192], ["eq2"], ["eqj", "gme"], accum_out=T.gme[:, 0:1])
-    act(T.b3[:, :], T.ones[:, :], ["ones", "gme"], ["b3"], scale=T.gme[:, 0:1])
+        red(T.gs[:, i:i + 1], T.tg[:, 36 * i + 4:32 * i + 32], ["tg%d" % i], ["gs%d" % i], negate=True)
 
-    lim = float(LATE + CAP + 1)
-    ts(T.fa[:, :], T.wa[:, :], T.gs[:, 0:1], lim, ADD, GE, ["wa", "gs0"], ["fa"])
-    ts(T.fb[:, :], T.wb[:, :], T.gs[:, 1:2], lim, ADD, GE, ["wb", "gs1"], ["fb"])
+    ts(T.fa[:, :], T.wa[:, :], T.gs[:, 0:1], BIG, GE, MUL, ["wa", "gs0"], ["fa"])
+    ts(T.fb[:, :], T.wb[:, :], T.gs[:, 1:2], BIG, GE, MUL, ["wb", "gs1"], ["fb"])
     scan2(T.cum[:, :], T.fa[:, :], T.fb[:, :], 0.0, ["fa", "fb"], ["cum"])
-    act(T.bm2[:, 32:64], T.ones[:, :], ["ones", "cum"], ["bm5"], scale=T.cum[:, 63:64])
     tt(T.r2[:, :], T.fa[:, :], T.fb[:, :], ADD, ["fa", "fb"], ["r2"])
-    ts(T.bm2[:, 0:32], T.mlt[:, :], T.cum[:, 63:64], None, MUL, None, ["mlt", "cum"], ["bm4"])
-    tt(T.d2c[:, :], T.r2[:, :], T.cum[:, :], MUL, ["r2", "cum"], ["d2c"])
-    tr(T.p2[:, 32:96], T.bm2[:, :], ["bm4", "bm5"], ["p2"])
-    tr(T.tdc[:, :], T.d2c[:, :], ["d2c"], ["tdc"])
-    red(bcol[:, 4:5], T.p2[:, 31:64], ["p2", "p2k"], ["b2c"])
+    ts(T.bm2[:, :], mk[:, 0:64], T.cum[:, 63:64], 1 / BIG, MUL, MUL, ["mlt", "ones", "cum"], ["bm3"])
+    tr(T.p2[:, 32:96], T.bm2[:, :], ["bm3"], ["p2"])
+    tt(T.lid[:, :], T.r2[:, :], T.d1[:, :], ADD, ["r2", "d1"], ["lid"])
+    red(bcol[:, 4:5], T.p2[:, 31:64], ["p2", "p2k"], ["b2"])
     tt(T.m16[:, :], T.p2[:, 64:80], T.p2[:, 80:96], ADD, ["p2"], ["m16"])
-    ts(T.d2b[:, :], T.r2[:, :], bcol[:, 4:5], None, MUL, None, ["r2", "b2c"], ["d2b"])
+    ts(T.c2b[:, :], T.cum[:, :], 1 / BIG, bcol[:, 4:5], MUL, ADD, ["cum", "b2"], ["c2b"])
     tt(T.m8[:, :], T.m16[:, 0:8], T.m16[:, 8:16], ADD, ["m16"], ["m8"])
-    for c in (0, 2, 4):
-        send(calls[c][1], lambda z: T.m8[:, z:z + 1], lambda z: T.ml[:, place(z):place(z) + 1], calls[c][3], "mar", "mars", ["m8"])
-    cnt["mar"] = count_in
-    wr["mx"] = [("mar", count_in)]
-    tr(T.tdb[:, :], T.d2b[:, :], ["d2b"], ["tdb"])
-    tr(T.t3[:, :], T.b3[:, :], ["b3"], ["t3"])
-    scan2(T.cs2[:, 8:72], T.tdc[:, :], T.tdb[:, :], 0.0, ["tdc", "tdb"], ["cs2"])
-    tt(T.n16[:, :], T.t3[:, 0:32:2], T.t3[:, 1:32:2], ADD, ["t3"], ["n16"])
-    tt(T.s2[:, :], T.cs2[:, 15:72:8], T.cs2[:, 7:64:8], SUB, ["cs2", "cs2z"], ["s2"])
-    tt(T.n8[:, :], T.n16[:, 0:16:2], T.n16[:, 1:16:2], ADD, ["n16"], ["n8"])
-    tt(T.s8[:, :], T.s1[:, :], T.s2[:, :], MAX, ["s1", "s2"], ["s8"])
-    scan(T.n8s[:, :], T.n8[:, :], 8, 0.0, ["n8"], ["n8s"])
-    cp(T.off[:, :], T.s8[:, :], ["s8"], ["off"])
-    ts(T.ta[:, 0:180:9], T.j0[:, :], T.cb[:, 0:1], None, ADD, None, ["j0", "cb"], ["jj"])
-    cp(T.scat[:, 32:32 + WIN].indirect(T.off[:, 0:8]), T.vals[:, :], ["off", "vals", "sz0", "sz1"], ["scat"])
+    tt(T.d2[:, :], T.c2b[:, :], T.lid[:, :], MIN, ["c2b", "lid"], ["d2"])
+    for engines in p["seconds"]:
+        call([([p["to"][z]], e, "mar", T.m8[:, z:z + 1], [number(T, N + place(z), 1)]) for z, e in engines.items()], ["m8"])
+    act(number(T, N, 1), T.m8[:, own:own + 1], ["m8"], ["ml0"])
+    tr(T.gt[:, :], T.gr[:, :], ["gr0", "gr1"], ["gt"])
+    tr(T.td2[:, :], T.d2[:, :], ["d2"], ["td2"])
+    cp(T.gl[:, 0:4:2], T.gt[:, 0:64:32], ["gt"], ["gl"])
+    top8(T.cs2[:, :], T.td2[:, :], ["td2"], ["cs2"])
+    ts(T.ta[:, 0:180:9], T.j0[:, :], qc, None, ADD, None, ["j0", "qc"], ["jj"])
+    cp(T.off[:, :], T.cs2[:, 7:64:8], ["cs2"], ["off"])
+    op("v", V.tensor_copy, (T.scat[:, 32:32 + WIN].indirect(T.off[:, 0:8]), T.vals[:, :]), ["off", "vals"], ["scat"])
 
-    pp, bb, dd = T.pp, T.bb, T.dd
     tw, hh, so = T.tw, T.hh, T.so
     H = WIN // 2
 
@@ -349,24 +384,18 @@ def rank_program(g, core, T, topo):
         op("v", V.tensor_copy, (oq[:, n0:n0 + n].bitcast(dt.uint32), iq[:, 0:m].bitcast(dt.uint32).indirect(off)), reads, [writes + "q"])
         act(os_[:, n0:n0 + n], is_[:, 0:m].indirect(off), reads, [writes + "s"])
 
-    def columns(call, sq, sp, key):
-        kind, zs, n, engines = call
-
-        def src(z):
-            c = SLOT * (z - zs[0])
-            return sq[:, c:c + n].bitcast(dt.uint8) if kind == "q" else sp[:, c:c + n]
-
-        def dst(z):
-            c = SLOT * place(z)
-            return T.land[:, c:c + n].bitcast(dt.uint8) if kind == "q" else T.lsc[:, c:c + n]
-        send(zs, src, dst, engines, "dat", "dats", [key + kind])
-
-    def wave(i, lists):
-        (sq, sp), zs, key = ((T.sq1, T.sp1), (T.sq2, T.sp2), (T.sq3, T.sp3))[i], calls[2 * i][1], "w%d" % i
+    def slots(sq, sp, zs, c0, key):
         za, zb = zs[0], zs[-1] + 1
-        pick(sq, sp, SLOT * (zb - za), T.xq, T.xs, TOK, so[:, 4 * za:4 * zb], 0, lists + ["xq"], key)
-        columns(calls[2 * i], sq, sp, key)
-        columns(calls[2 * i + 1], sq, sp, key)
+        lists = ["so%d" % i for i in range(2) if za < 4 * i + 4 and zb > 4 * i]
+        pick(sq, sp, SLOT * (zb - za), T.xq, T.xs, TOK, so[:, 4 * za:4 * zb], c0, lists + ["xq"], key)
+
+    def handed(i):
+        sq, sp, key = T["sq%d" % i], T["sp%d" % i], "w%d" % i
+        slots(sq, sp, p["pairs"][i], 0, key)
+        to = list(enumerate(p["handed"][i].items()))
+        n = 2 * SLOT // len(to)
+        call([([h], e, "hq", codes(sq, n * j, n), [codes(T.hq, 0, n)]) for j, (h, e) in to], [key + "q"])
+        call([([h], e, "hs", sp[:, n * j:n * j + n], [T.hs[:, 0:n]]) for j, (h, e) in to], [key + "s"])
 
     turn(0, 0)
     turn(0, 1)
@@ -375,50 +404,49 @@ def rank_program(g, core, T, topo):
     turn(1, 0)
     entries(0)
     turn(1, 1)
-    wave(0, ["so0"])
+    handed(0)
     join(1, 0)
     join(1, 1)
-    tt(bb[:, 8:15], bb[:, 0:7], T.n8[:, 0:7], ADD, ["bb0", "n8"], ["bb8"])
     entries(1)
-    ts(pp[:, 1:9], T.n8s[:, :], float(CAP), None, MIN, None, ["n8s"], ["pp1"])
-    wave(1, ["so0", "so1"])
-    wave(2, ["so0", "so1"])
-    pick(T.land, T.lsc, SLOT, T.xq, T.xs, TOK, so[:, 4 * own:4 * own + 4], 0, ["so1", "xq"], "own")
+    handed(1)
+    slots(T.sq2, T.sp2, p["pairs"][2], 0, "w2")
+    slots(T.sq2, T.sp2, [p["near"]], 2 * SLOT, "w3")
+    n = SLOT if p["near"] < 2 else BOTH
+    last = list(enumerate(p["straight"].items()))
+    call([([p["to"][z]], e, "dat", codes(T.sq2, SLOT * j, n), [codes(T.land, SLOT * place(z), n)]) for j, (z, e) in last], ["w2q", "w3q"])
+    call([([p["to"][z]], e, "dat", T.sp2[:, SLOT * j:SLOT * j + n], [T.lsc[:, SLOT * place(z):SLOT * place(z) + n]])
+          for j, (z, e) in last], ["w2s", "w3s"])
 
-    tt(pp[:, 9:10], pp[:, 8:9], T.m8[:, own:own + 1], ADD, ["pp1", "m8"], ["pp9"])
-    quant(T.land[:, ZERO:ZERO + NZ], T.lsc[:, ZERO:ZERO + NZ], T.zin[:, :], ["zin"], ["zq"])
-    scan2(pp[:, 10:17], T.ml[:, 1:8], T.z64[:, 0:7], pp[:, 9:10], ["mx", "z64", "pp9"], ["pp10"])
-    quant(T.wq[:, :], T.wsc[:, :], T["win"][:, :], ["win"], ["wq"])
-    places = ["pp0", "pp1", "pp9", "pp10"]
-    tt(T.de[:, 0:17], bb[:, 0:17], pp[:, 0:17], SUB, ["bb0", "bb8", "bb15", "bb16"] + places, ["de"])
+    op("v", V.tensor_tensor_scan, (pp[:, 1:17], T.nl[:, 0:128:8], T.cap[:, :], 0.0, ADD, MIN), ["num", "mar", "nl0", "ml0", "cap"], ["pp1"])
+    tt(bb[:, 8:15], bb[:, 0:7], T.nl[:, 0:56:8], ADD, ["bb0", "num", "nl0"], ["bb8"])
+    tt(T.de[:, 0:17], bb[:, 0:17], pp[:, 0:17], SUB, ["bb0", "bb8", "bb15", "pp0", "pp1"], ["de"])
+    slots(T.land, T.lsc, [own], 0, "own")
     tt(dd[:, 1:17], T.de[:, 1:17], T.de[:, 0:16], SUB, ["de"], ["dd"])
     for q in range(1, 17):
         t, i = (T.ta, q) if q < 9 else (T.tz, q - 8)
-        ts(t[:, i:180:9], T.ta[:, 0:180:9], pp[:, q:q + 1], dd[:, q:q + 1], GE, MUL, ["jj", "dd", "tzz"] + places, ["tm%d" % q])
+        ts(t[:, i:180:9], T.ta[:, 0:180:9], pp[:, q:q + 1], dd[:, q:q + 1], GE, MUL, ["jj", "pp1", "dd"], ["tm%d" % q])
     scan2(T.cs3[:, 12:192], T.ta[:, :], T.tz[:, :], 0.0, ["jj", "tzz"] + ["tm%d" % q for q in range(1, 17)], ["cs3"])
     tt(T.t20[:, :], T.cs3[:, 20:192:9], T.cs3[:, 11:183:9], SUB, ["cs3", "cs3z"], ["t20"])
     ts(T.fo[:, :], T.t20[:, :], float(ZERO + NZ - 1), None, MIN, None, ["t20"], ["fo"])
 
-    cnt["dat"] = data_in
-    wr["dx"] = [("dat", data_in)]
-    got = ["dx", "ownq", "owns", "zq", "fo"]
+    got = ["dat", "ownq", "owns", "zq", "fo"]
     cut = 128
     for i, (a, b) in enumerate(((0, cut), (cut, ROOM))):
         pick(T.fq, T.fs, b - a, T.land, T.lsc, ZERO + NZ, T.fo[:, a // 16:b // 16], a, got, "f%d" % i)
+    quant(T.wq[:, 256:512], T.wsc[:, 256:512], T["win"][:, 1024:2048], ["win1"], ["wq1"])
     low, top = ["f0q", "f0s"], ["f1q", "f1s"]
     pieces = [(0, 0, cut, low), (1, 0, cut, low), (0, cut, ROOM, top), (1, cut, ROOM, top)]
     for o in range(2, O):
         pieces += [(o, 0, ROOM // 2, low + top), (o, ROOM // 2, ROOM, low + top)]
     for i, (o, a, b, keys) in enumerate(pieces):
         op("t", g.tensor.matmul_mx, (T.acc[:, 512 * i:512 * i + b - a], T.wq[:, 128 * o:128 * o + 128], T.wsc[:, 128 * o:128 * o + 128],
-                                     T.fq[:, a:b], T.fs[:, a:b], True, True), ["wq"] + keys, ["acc%d" % i])
+                                     T.fq[:, a:b], T.fs[:, a:b], True, True), ["wq%d" % (o // 2)] + keys, ["acc%d" % i])
     for i, (o, a, b, keys) in enumerate(pieces):
         src, dst = T.acc[:, 512 * i:512 * i + b - a], T.yo[:, ROOM * o + a:ROOM * o + b]
-        (cp if i in (0, 1, 3, 4, 6) else act)(dst, src, ["acc%d" % i], ["yo%d" % i])
+        (cp if i in (1, 3, 4, 6) else act)(dst, src, ["acc%d" % i], ["yo%d" % i])
         if o < 2:
-            dma("y", "dy", T.y[:, ROOM * o + a:ROOM * o + b], dst, ["yo%d" % i], ["yout"], more=True)
+            dma("y", "dy", T.y[:, ROOM * o + a:ROOM * o + b], dst, ["yo%d" % i], ["yout"])
         elif a > 0:
-            dma("y", "dy", T.y[:, ROOM * o:ROOM * o + ROOM], T.yo[:, ROOM * o:ROOM * o + ROOM], ["yo%d" % (i - 1), "yo%d" % i],
-                ["yout"], more=True)
+            dma("y", "dy", T.y[:, ROOM * o:ROOM * o + ROOM], T.yo[:, ROOM * o:ROOM * o + ROOM], ["yo%d" % (i - 1), "yo%d" % i], ["yout"])
     for sem in sorted(cnt):
         need("y", (sem, None))

@@ -9,8 +9,7 @@ NZ = 128
 WSLOT = 80
 WIN = N * WSLOT
 BACK = 9
-LIMIT = 672
-LATE = LIMIT - CAP - 1
+BASE = 160
 BIG = 1024.0
 
 
@@ -27,17 +26,15 @@ SCRATCH = {
     "gr": _sb(64, F32), "gt": _sb(64, F32), "gl": _sb(4, U16), "l4": _sb(4, I32), "l64": _sb(4, U16),
     "mk": _sb(96, F32), "mgt": _sb(32, F32), "kc": _sb(8, F32),
     "v128": _sb(128, B16), "vals": _sb(128, B16), "j0": _sb(20, I32), "z64": _sb(96, B16),
-    "pre": _sb(256, B16), "mt": _sb(256, B16), "tcol": _sb(8, F32), "bm": _sb(160, F32), "tb": _sb(192, F32), "bcol": _sb(8, F32),
-    "sc1": _sb(64, F32), "d1": _sb(64, F32), "sca": _sb(64, F32), "scb": _sb(64, F32), "wa": _sb(64, F32), "wb": _sb(64, F32),
-    "qa": _sb(64, B16), "qb": _sb(64, B16),
+    "pre": _sb(128, B16), "m1": _sb(64, B16), "tcol": _sb(8, F32), "bm": _sb(96, F32), "tb": _sb(128, F32), "bcol": _sb(8, F32),
+    "sc1": _sb(64, F32), "d1": _sb(64, F32), "td1": _sb(64, F32), "l8": _sb(8, U16), "kw": _sb(128, F32), "wk": _sb(128, F32),
     "al": _sb(64, I32), "eqs": _sb(192, B16), "bg": _sb(192, B16), "tg": _sb(64, B16), "gs": _sb(8, F32),
     "n16": _sb(16, F32), "n8": _sb(8, B16), "nl": _sb(128, B16), "cap": _sb(16, F32),
     "fa": _sb(64, B16), "fb": _sb(64, B16), "r2": _sb(64, B16), "cum": _sb(64, F32), "bm2": _sb(64, F32), "p2": _sb(96, F32),
     "m16": _sb(16, F32), "m8": _sb(8, B16), "lid": _sb(64, F32), "c2b": _sb(64, F32), "d2": _sb(64, F32), "td2": _sb(64, F32),
     "cs2": _sb(64, F32), "off": _sb(8, U16),
-    "scat": _sb(WIN + 32, B16), "tw": _sb(2 * WIN, B16), "hh": _sb(WIN // 16, F32), "so": _sb(4 * N, U16),
-    "sq0": _sb(2 * SLOT, MX), "sp0": _sb(2 * SLOT, U8), "sq1": _sb(2 * SLOT, MX), "sp1": _sb(2 * SLOT, U8),
-    "sq2": _sb(3 * SLOT, MX), "sp2": _sb(3 * SLOT, U8),
+    "scat": _sb(BASE + WIN, B16), "tw": _sb(2 * WIN, B16), "hh": _sb(WIN // 16, F32), "so": _sb(4 * N, U16),
+    "sq": _sb((N - 1) * SLOT, MX), "sp": _sb((N - 1) * SLOT, U8),
     "hn": _sb(2, B16), "hq": _sb(2 * SLOT, MX), "hs": _sb(2 * SLOT, U8),
     "land": _sb(ZERO + NZ, MX), "lsc": _sb(ZERO + NZ, U8),
     "pp": _sb(24, F32), "bb": _sb(24, F32), "de": _sb(24, F32), "dd": _sb(24, F32),
@@ -46,7 +43,7 @@ SCRATCH = {
     "acc": ("psum", [128, 512 * 2 * O], F32), "yo": _sb(ROOM * O, F32),
 }
 SEMAPHORES = ["cv", "cs", "cg", "ct", "dl0", "dc1", "dc2", "dx", "dw0", "dw1", "dal", "dy", "lst", "num", "mar",
-              "dat", "hn", "hq", "hs", "left"]
+              "dat", "hn", "hq", "hs", "left", "sent"]
 
 ADD, SUB, MUL, MIN, MAX = AluOpType.add, AluOpType.subtract, AluOpType.mult, AluOpType.min, AluOpType.max
 GE, GT, EQ = AluOpType.is_ge, AluOpType.is_gt, AluOpType.is_equal
@@ -70,15 +67,19 @@ def plan(me, cores, topo):
     turn = sorted((core, to[near])).index(core)
     free = [c for c in topo.cores_of(core) if c not in cores]
     wide = [c for c in free if topo.may_write(c, to[far[0]])]
-    other = [c for c in free if c not in wide and topo.die(c) != topo.die(core)]
     same = [c for c in free if c not in wide and topo.die(c) == topo.die(core)]
-    helpers = {wide[turn]: pairs[0], other[turn]: pairs[1][:1], same[turn]: pairs[1][1:]}
-    every = out + inn
-    return {"near": near, "pairs": pairs, "helpers": helpers, "out": out, "inn": inn, "to": to, "lists": out[::4],
-            "handed": [{wide[turn]: every}, deal([other[turn], same[turn]], every)],
-            "numbers": {wide[turn]: inn[:4], **deal([other[turn], same[turn]], inn[4:])},
-            "counts": {**deal(pairs[2], out[:4]), near: out[4:]}, "straight": {**deal(pairs[2], out), near: inn},
-            "seconds": [{**deal(far[:2], out), near: inn}, deal(far[2:], out)]}
+    other = [c for c in free if c not in wide and topo.die(c) != topo.die(core)]
+    first, second, third = wide[turn], other[turn], same[turn]
+    ways = {"out": out, "to": to, "lists": out[::4], "seconds": [{**deal(far[:2], out), near: inn}, deal(far[2:], out)]}
+    last = [(pairs[2], {}, deal(pairs[2], out)), ([near], {}, {near: inn})]
+    if pairs[1][1] < N // 2:
+        return {**ways, "helpers": {first: pairs[0], third: pairs[1][1:]}, "early": 2,
+                "waves": [(pairs[0], {first: out + inn}, {}), (pairs[1], {third: inn}, {pairs[1][0]: out})] + last,
+                "numbers": deal([first, third], inn), "counts": deal(pairs[1][:1] + pairs[2] + [near], out)}
+    return {**ways, "helpers": {first: pairs[0], second: pairs[1][:1], third: pairs[1][1:]}, "early": 1,
+            "waves": [(pairs[0], {first: out + inn}, {}), (pairs[1], {second: out, third: inn}, {})] + last,
+            "numbers": {**deal([first, second], inn), third: [e for e in out if e not in ways["lists"]][:4]},
+            "counts": {**deal(pairs[2], out[:4]), near: out[4:]}}
 
 
 def mask(engines):
@@ -101,23 +102,27 @@ def place(z):
     return N - 1 - z
 
 
+def width(zs):
+    return SLOT if min(zs) < 2 else BOTH
+
+
 def number(T, k, n):
     return T.nl[:, 8 * k:8 * k + n]
 
 
 def helper_program(g, p, core, T, topo):
     zs = p["helpers"][core]
-    n = SLOT if min(zs) < 2 else BOTH
+    n = width(zs)
     engines = deal(zs, p["out"])
-    every = sum(len(e.get(core, [])) for e in p["handed"])
-    for sem, count, far, src, dst in (
-            ("hn", len(p["numbers"][core]), "num", lambda j: T.hn[:, j:j + 1], lambda k: number(T, k, 1)),
-            ("hq", every, "dat", lambda j: codes(T.hq, SLOT * j, n), lambda k: codes(T.land, SLOT * k, n)),
-            ("hs", every, "dat", lambda j: T.hs[:, SLOT * j:SLOT * j + n], lambda k: T.lsc[:, SLOT * k:SLOT * k + n])):
+    every = sum(len(handed.get(core, [])) for _, handed, _ in p["waves"])
+    steps = [("hn", len(p["numbers"][core]), "num", lambda j: T.hn[:, j:j + 1], lambda k: number(T, k, 1)),
+             ("hq", every, "dat", lambda j: codes(T.hq, SLOT * j, n), lambda k: codes(T.land, SLOT * k, n)),
+             ("hs", every, "dat", lambda j: T.hs[:, SLOT * j:SLOT * j + n], lambda k: T.lsc[:, SLOT * k:SLOT * k + n])]
+    for sem, count, far, src, dst in steps:
         g.wait_ge(T.sem[sem], count)
         g.remote_dma_fused([RemoteDMATransfer(dst_ids=[at(p["to"][z], topo)], dma_engine_mask=mask(engines[z]), remote_sem=T.sem[far],
                                               src=src(j), dst=dst(place(z))) for j, z in enumerate(zs)], local_sem=T.sem["left"])
-    g.wait_ge(T.sem["left"], 3 * len(p["out"]))
+    g.wait_ge(T.sem["left"], len(steps) * len(p["out"]))
 
 
 def rank_program(g, core, T, topo):
@@ -218,11 +223,11 @@ def rank_program(g, core, T, topo):
     def line(out, a, scale, bias, reads, writes):
         op("s", g.scalar.activation, (out, a, IDENT, bias, scale), reads, writes)
 
-    def call(transfers, reads):
+    def call(transfers, reads, left="left"):
         before("g", reads, [])
         g.remote_dma_fused([RemoteDMATransfer(dst_ids=[at(c, topo) for c in to], dma_engine_mask=mask(e), remote_sem=T.sem[sem],
-                                              srcs=[src], dsts=dst) for to, e, sem, src, dst in transfers], local_sem=T.sem["left"])
-        cnt["left"] = cnt.get("left", 0) + sum(len(t[1]) for t in transfers)
+                                              srcs=[src], dsts=dst) for to, e, sem, src, dst in transfers], local_sem=T.sem[left])
+        cnt[left] = cnt.get(left, 0) + sum(len(t[1]) for t in transfers)
 
     cnt["lst"] = cnt["num"] = cnt["mar"] = cnt["dat"] = 0
     for k in range(1, N):
@@ -231,7 +236,7 @@ def rank_program(g, core, T, topo):
         cnt["lst"] += len(o["lists"])
         cnt["num"] += len(o["counts"][z]) if z in o["counts"] else handed
         cnt["mar"] += sum(len(e.get(z, [])) for e in o["seconds"])
-        cnt["dat"] += 2 * (len(o["straight"][z]) if z in o["straight"] else handed)
+        cnt["dat"] += 2 * (handed + sum(len(e.get(z, [])) for _, _, e in o["waves"]))
     for sem in ("lst", "num", "mar", "dat"):
         wr[sem] = [(sem, cnt[sem])]
 
@@ -241,7 +246,6 @@ def rank_program(g, core, T, topo):
     for b in range(8):
         dma("sy"[b % 2], "dc2", T.ct[16 * b:16 * b + 16, 16:32], T.c2[:, :], [], ["c2"])
     dma("y", "dx", T.xin[:, :], T.x[:, :], [], ["xin"])
-    dma("y", "dw0", T["win"][:, 0:1024], T.w[:, 0:1024], [], ["win0"])
 
     ra, kc, mk, pp, bb, dd = T.ra, T.kc, T.mk, T.pp, T.bb, T.dd
     iota(ra[:, 64:96], "ra1", [[1, 2], [4, 2], [0, 8]], 0)
@@ -253,96 +257,92 @@ def rank_program(g, core, T, topo):
     call([(p["to"], p["lists"], "lst", T.lists[0], [T.lists[place(z)] for z in range(N - 1)])], ["l0"])
     iota(T.v128[:, :], "v128", [[32, 2], [64, 4], [1, 16]], 0)
 
-    def later():
-        iota(T.gr[:, 0:32], "gr0", [[-1, 2], [WSLOT // 16, 4], [1, 4]], 1)
-        iota(T.gr[:, 32:64], "gr1", [[-1, 2], [WSLOT // 16, 4], [1, 4]], 1 + WSLOT // 4)
+    def blocks():
+        for i in range(2):
+            iota(T.gr[:, 32 * i:32 * i + 32], "gr%d" % i, [[-1, 2], [WSLOT // 16, 4], [1, 4]], 1 + WSLOT // 4 * i)
         iota(T.gr[:, 3:32:16], "gr0", [[-1, 2]], 1 + BACK)
+
+    def later():
         iota(T.j0[:, :], "j0", [[16, 20]], 0, flag=False)
         iota(bb[:, 0:8], "bb0", [[SLOT, 8]], 0)
         iota(T.cap[:, :], "cap", [[int(BIG), 2], [0, 8]], CAP)
         iota(bb[:, 15:17], "bb15", [[SLOT - FIRST, 2]], SLOT * (N - 1) + FIRST)
 
-    fill(T.scat[:, :], 0.0, "scat")
+    fill(T.scat[:, BASE - 16:BASE + WIN], 0.0, "scat")
     fill(T.z64[:, :], 0.0, "z64")
     fill(mk[:, 32:64], 1.0, "ones")
     fill(T.eqs[:, 0:192], 0.0, "eqz")
-    fill(T.zin[:, :], 0.0, "zin")
+    fill(T.cs3[:, 0:12], 0.0, "cs3z")
+    fill(pp[:, 0:1], 0.0, "pp0")
     tr(T.ca[:, :], ra[:, 32:160], ["ra0", "ra1", "ra2", "ra3"], ["ca"])
     zc, pc, hc, odd = [T.ca[:, 32 * j:32 * j + 1] for j in range(4)]
-    zpos, t1, t2, q4, qc = [kc[:, j:j + 1] for j in range(5)]
+    zpos, t1, t2, q4, q8, q9, qc = [kc[:, j:j + 1] for j in range(7)]
     ts(T.l64[:, :], T.l4[:, :], pc, None, ADD, None, ["l4", "ca"], ["l64"])
     ts(mk[:, 64:96], ra[:, 0:32], zc, None, EQ, None, ["ra0", "ca"], ["meq"])
-    ts(T.mgt[:, :], ra[:, 96:128], hc, None, GT, None, ["ra2", "ca"], ["mgt"])
     ts(T.ec[:, :], T.e64[:, :], 7, None, AND, None, ["e64"], ["ec"])
-    tt(mk[:, 0:32], mk[:, 64:96], T.mgt[:, :], MUL, ["meq", "mgt"], ["mlt"])
-    line(T.tb[:, 31:32], zc, float(WSLOT), -1.0, ["ca"], ["tb0"])
-    op("s", g.scalar.activation, (zpos, zc, SIGN), ["ca"], ["zpos"])
-    line(t1, zc, float(WSLOT), 16.0 * BACK - 1, ["ca"], ["t1"])
-    line(t2, zpos, -16.0 * BACK, t1, ["zpos", "t1"], ["t2"])
-    line(T.cut[:, :], ra[:, 0:64], 4 * BIG, 0.0, ["ra0"], ["cut"])
     line(q4, odd, -1 / 16, pc, ["ca"], ["q4"])
+    line(T.tb[:, 31:32], zc, float(WSLOT), BASE - 1.0, ["ca"], ["tb0"])
+    line(q8, q4, 2.0, 0.0, ["q4"], ["q8"])
+    line(q9, q4, 2.0, 1.0, ["q4"], ["q9"])
     line(qc, q4, 2.0, zc, ["q4", "ca"], ["qc"])
+    op("s", g.scalar.activation, (zpos, zc, SIGN), ["ca"], ["zpos"])
+    line(t1, zc, float(WSLOT), BASE + 16.0 * BACK - 1, ["ca"], ["t1"])
+    line(T.cut[:, :], ra[:, 0:64], 4 * BIG, 0.0, ["ra0"], ["cut"])
+    line(t2, zpos, -16.0 * BACK, t1, ["zpos", "t1"], ["t2"])
 
     l64 = T.l64[:, 0:4]
     c1w, c2w = T.ct[:, 0:16].indirect(l64), T.ct[:, 16:32].indirect(l64)
-    m1, ma, mb, mc = [T.mt[:, 64 * i:64 * i + 64] for i in range(4)]
+    m1, bcol = T.m1[:, :], T.bcol
     tt(T.pre[:, 0:64], c1w, T.ec[:, :], EQ, ["c1", "l64", "ec"], ["pre0"])
-    ts(T.pre[:, 64:128], c1w, float((me + 1) % N), None, EQ, None, ["c1", "l64"], ["pre1"])
+    ts(T.mgt[:, :], ra[:, 96:128], hc, None, GT, None, ["ra2", "ca"], ["mgt"])
     tr(m1, T.pre[:, 0:64], ["pre0"], ["m1"])
-    ts(T.pre[:, 128:192], c1w, float((me + 2) % N), None, EQ, None, ["c1", "l64"], ["pre2"])
-    red(T.tcol[:, 0:1], m1, ["m1"], ["tcol0"])
-    fill(T.cs3[:, 0:12], 0.0, "cs3z")
-    ts(T.bm[:, 0:96], mk[:, :], T.tcol[:, 0:1], None, MUL, None, ["meq", "mlt", "ones", "tcol0"], ["bm0"])
-    fill(pp[:, 0:1], 0.0, "pp0")
-    tr(T.tb[:, 32:128], T.bm[:, 0:96], ["bm0"], ["tb"])
-    tt(T.pre[:, 192:256], c2w, T.ec[:, :], EQ, ["c2", "l64", "ec"], ["pre3"])
-    tt(T.n16[:, :], T.tb[:, 64:80], T.tb[:, 80:96], ADD, ["tb"], ["n16"])
-    tr(T.mt[:, 64:256], T.pre[:, 64:256], ["pre1", "pre2", "pre3"], ["mt"])
-    tt(T.n8[:, :], T.n16[:, 0:8], T.n16[:, 8:16], ADD, ["n16"], ["n8"])
-    call([([h], p["numbers"][h], "hn", T.n8[:, zs[0]:zs[0] + 2], [T.hn[:, :]]) for h, zs in p["helpers"].items()]
-         + [([p["to"][z]], e, "num", T.n8[:, z:z + 2], [number(T, place(z), 2)]) for z, e in p["counts"].items()], ["n8"])
-    act(number(T, 0, 1), T.n8[:, own:own + 1], ["n8"], ["nl0"])
-    later()
-    for i, m in ((1, ma), (2, mb)):
-        red(T.tcol[:, i:i + 1], m, ["mt"], ["tcol%d" % i])
-    bcol = T.bcol
+    tt(mk[:, 0:32], mk[:, 64:96], T.mgt[:, :], MUL, ["meq", "mgt"], ["mlt"])
+    red(T.tcol[:, 0:1], m1, ["m1"], ["tcol"])
+    tt(T.pre[:, 64:128], c2w, T.ec[:, :], EQ, ["c2", "l64", "ec"], ["pre1"])
+    ts(T.bm[:, :], mk[:, :], T.tcol[:, 0:1], None, MUL, None, ["meq", "mlt", "ones", "tcol"], ["bm"])
+    ts(T.l8[:, 0:4], ra[:, 0:4], 16.0, q8, MUL, ADD, ["ra0", "q8"], ["l80"])
+    tr(T.tb[:, 32:128], T.bm[:, :], ["bm"], ["tb"])
+    ts(T.l8[:, 4:8], ra[:, 0:4], 16.0, q9, MUL, ADD, ["ra0", "q9"], ["l81"])
     red(bcol[:, 0:1], T.tb[:, 31:64], ["tb", "tb0"], ["b1"])
-    ts(T.bm[:, 96:128], mk[:, 0:32], T.tcol[:, 1:2], LATE / 32, MUL, ADD, ["mlt", "tcol1"], ["bm1"])
-    ts(T.bm[:, 128:160], mk[:, 0:32], T.tcol[:, 2:3], LATE / 32, MUL, ADD, ["mlt", "tcol2"], ["bm2"])
-    red(bcol[:, 3:4], T.tb[:, 96:128], ["tb"], ["nz"])
-    tr(T.tb[:, 128:192], T.bm[:, 96:160], ["bm1", "bm2"], ["tc"])
-    line(T.p2[:, 31:32], bcol[:, 3:4], zpos, t2, ["nz", "zpos", "t2"], ["p2k"])
+    tt(T.n16[:, :], T.tb[:, 64:80], T.tb[:, 80:96], ADD, ["tb"], ["n16"])
     scan(T.sc1[:, :], m1, 64, bcol[:, 0:1], ["m1", "b1"], ["sc1"])
-    red(bcol[:, 1:2], T.tb[:, 128:160], ["tc"], ["ba"])
-    red(bcol[:, 2:3], T.tb[:, 160:192], ["tc"], ["bq"])
-    tt(T.qa[:, :], ma, mc, MUL, ["mt"], ["qa"])
-    scan(T.sca[:, :], ma, 64, bcol[:, 1:2], ["mt", "ba"], ["sca"])
-    scan(T.scb[:, :], mb, 64, bcol[:, 2:3], ["mt", "bq"], ["scb"])
-    tt(T.qb[:, :], mb, mc, MUL, ["mt"], ["qb"])
-    tt(T.wa[:, :], T.qa[:, :], T.sca[:, :], MUL, ["qa", "sca"], ["wa"])
-    tt(T.wb[:, :], T.qb[:, :], T.scb[:, :], MUL, ["qb", "scb"], ["wb"])
-    tt(T.d1[:, :], m1, T.sc1[:, :], MUL, ["m1", "sc1"], ["d1"])
-    quant(T.xq[:, :], T.xs[:, :], T.xin[:, :], ["xin"], ["xq"])
-    quant(T.land[:, ZERO:ZERO + NZ], T.lsc[:, ZERO:ZERO + NZ], T.zin[:, :], ["zin"], ["zq"])
-    fill(T.tz[:, 0:180:9], 0.0, "tzz")
-    quant(T.wq[:, 0:256], T.wsc[:, 0:256], T["win"][:, 0:1024], ["win0"], ["wq0"])
-
-    line(T.vals[:, :], T.v128[:, :], 1.0, odd, ["v128", "ca"], ["vals"])
+    tt(T.n8[:, :], T.n16[:, 0:8], T.n16[:, 8:16], ADD, ["n16"], ["n8"])
     for b in range(4):
         dma("ys"[b % 2], "dal", T.al[32 * b:32 * b + 32, 0:64], T.lists[:, :, :], ["lst", "l0"], ["al"])
-    dma("y", "dw1", T["win"][:, 1024:2048], T.w[:, 1024:2048], ["lst"], ["win1"])
+    call([([h], p["numbers"][h], "hn", T.n8[:, zs[0]:zs[0] + 2], [T.hn[:, :]]) for h, zs in p["helpers"].items()], ["n8"])
+    blocks()
+    call([([p["to"][z]], e, "num", T.n8[:, z:z + 1], [number(T, place(z), 1)]) for z, e in p["counts"].items()], ["n8", "lst"], "sent")
+    wr["sent"] = [("sent", cnt["sent"])]
+    later()
+    dma("y", "dw0", T["win"][:, 0:1024], T.w[:, 0:1024], ["al"], ["win0"])
+    dma("y", "dw1", T["win"][:, 1024:2048], T.w[:, 1024:2048], ["sent"], ["win1"])
+    act(number(T, 0, 1), T.n8[:, own:own + 1], ["n8"], ["nl0"])
+    act(T.mgt[:, :], T.tb[:, 96:128], ["tb"], ["mgt", "nz"], accum_out=bcol[:, 3:4])
+    line(T.p2[:, 31:32], bcol[:, 3:4], zpos, t2, ["nz", "zpos", "t2"], ["p2k"])
+    tt(T.d1[:, :], m1, T.sc1[:, :], MUL, ["m1", "sc1"], ["d1"])
+    quant(T.xq[:, :], T.xs[:, :], T.xin[:, :], ["xin"], ["xq"])
+    tr(T.td1[:, :], T.d1[:, :], ["d1"], ["td1"])
+    fill(T.tz[:, 0:180:9], 0.0, "tzz")
+    for i in range(2):
+        tt(T.kw[:, 64 * i:64 * i + 64], T.td1[:, :].indirect(T.l8[:, 4 * i:4 * i + 4]), T.pre[:, 64:128], MUL,
+           ["td1", "l8%d" % i, "pre1"], ["kw%d" % i])
+    tr(T.wk[:, :], T.kw[:, :], ["kw0", "kw1"], ["wk"])
+
+    line(T.vals[:, :], T.v128[:, :], 1.0, odd, ["v128", "ca"], ["vals"])
     eqs = T.eqs
+    act(T.zin[:, :], T.xin[:, 0:4 * NZ], ["xin"], ["zin"], scale=0.0)
     for i in range(2):
         ts(eqs[:, 96 * i:96 * i + 64], T.al[:, :], float((me + 1 + i) % N), None, EQ, None, ["al", "eqz"], ["eq%d" % i])
     for i in range(2):
-        scan(T.bg[:, 96 * i:96 * i + 96], eqs[:, 96 * i:96 * i + 96], 96, -LIMIT / (28.0 - 4 * i), ["eq%d" % i, "eqz"], ["bg%d" % i])
+        scan(T.bg[:, 96 * i:96 * i + 96], eqs[:, 96 * i:96 * i + 96], 96, -(BASE + WSLOT * i + CAP) / (28.0 - 4 * i),
+             ["eq%d" % i, "eqz"], ["bg%d" % i])
     for i in range(2):
         tr(T.tg[:, 32 * i:32 * i + 32], T.bg[:, 96 * i + 64:96 * i + 96], ["bg%d" % i], ["tg%d" % i])
     for i in range(2):
         red(T.gs[:, i:i + 1], T.tg[:, 36 * i + 4:32 * i + 32], ["tg%d" % i], ["gs%d" % i], negate=True)
 
-    ts(T.fa[:, :], T.wa[:, :], T.gs[:, 0:1], BIG, GE, MUL, ["wa", "gs0"], ["fa"])
-    ts(T.fb[:, :], T.wb[:, :], T.gs[:, 1:2], BIG, GE, MUL, ["wb", "gs1"], ["fb"])
+    ts(T.fa[:, :], T.wk[:, 0:64], T.gs[:, 0:1], BIG, GE, MUL, ["wk", "gs0"], ["fa"])
+    ts(T.fb[:, :], T.wk[:, 64:128], T.gs[:, 1:2], BIG, GE, MUL, ["wk", "gs1"], ["fb"])
     scan2(T.cum[:, :], T.fa[:, :], T.fb[:, :], 0.0, ["fa", "fb"], ["cum"])
     tt(T.r2[:, :], T.fa[:, :], T.fb[:, :], ADD, ["fa", "fb"], ["r2"])
     ts(T.bm2[:, :], mk[:, 0:64], T.cum[:, 63:64], 1 / BIG, MUL, MUL, ["mlt", "ones", "cum"], ["bm3"])
@@ -362,71 +362,56 @@ def rank_program(g, core, T, topo):
     top8(T.cs2[:, :], T.td2[:, :], ["td2"], ["cs2"])
     ts(T.ta[:, 0:180:9], T.j0[:, :], qc, None, ADD, None, ["j0", "qc"], ["jj"])
     cp(T.off[:, :], T.cs2[:, 7:64:8], ["cs2"], ["off"])
-    op("v", V.tensor_copy, (T.scat[:, 32:32 + WIN].indirect(T.off[:, 0:8]), T.vals[:, :]), ["off", "vals"], ["scat"])
+    op("v", V.tensor_copy, (T.scat[:, :].indirect(T.off[:, 0:8]), T.vals[:, :]), ["off", "vals"], ["scat"])
 
     tw, hh, so = T.tw, T.hh, T.so
-    H = WIN // 2
-
-    def turn(i, late):
-        tr(tw[:, late * WIN + H * i:late * WIN + H * i + H], T.scat[:, 32 - 16 * late + H * i:32 - 16 * late + H * i + H],
-           ["scat"], ["tw%d%d" % (late, i)])
-
-    def join(i, late):
-        a = late * WIN + H * i
-        tt(hh[:, 20 * i + 1 - late:20 * i + 20:2], tw[:, a:a + H:32], tw[:, a + 16:a + H:32], ADD, ["tw%d%d" % (late, i)],
-           ["hh%d%d" % (late, i)])
-
-    def entries(i):
-        cp(so[:, 16 * i:16 * i + 16], hh[:, 0:20 * i + 20].indirect(T.gl[:, 2 * i:2 * i + 1]),
-           ["gl"] + ["hh%d%d" % (a, b) for a in range(2) for b in range(i + 1)], ["so%d" % i])
+    def lists(i):
+        a, b = WIN // 2 * i, WIN // 2 * (i + 1)
+        for late in range(2):
+            tr(tw[:, late * WIN + a:late * WIN + b], T.scat[:, BASE - 16 * late + a:BASE - 16 * late + b], ["scat"], ["tw%d%d" % (late, i)])
+        for late in range(2):
+            c, d = late * WIN + a, late * WIN + b
+            tt(hh[:, a // 16 + 1 - late:b // 16:2], tw[:, c:d:32], tw[:, c + 16:d:32], ADD, ["tw%d%d" % (late, i)], ["hh%d%d" % (late, i)])
+        cp(so[:, 16 * i:16 * i + 16], hh[:, 0:b // 16].indirect(T.gl[:, 2 * i:2 * i + 1]),
+           ["gl"] + ["hh%d%d" % (late, j) for late in range(2) for j in range(i + 1)], ["so%d" % i])
 
     def pick(oq, os_, n, iq, is_, m, off, n0, reads, writes):
         op("v", V.tensor_copy, (oq[:, n0:n0 + n].bitcast(dt.uint32), iq[:, 0:m].bitcast(dt.uint32).indirect(off)), reads, [writes + "q"])
         act(os_[:, n0:n0 + n], is_[:, 0:m].indirect(off), reads, [writes + "s"])
 
-    def slots(sq, sp, zs, c0, key):
-        za, zb = zs[0], zs[-1] + 1
-        lists = ["so%d" % i for i in range(2) if za < 4 * i + 4 and zb > 4 * i]
-        pick(sq, sp, SLOT * (zb - za), T.xq, T.xs, TOK, so[:, 4 * za:4 * zb], c0, lists + ["xq"], key)
+    def slots(sq, sp, a, b, c0, key):
+        pick(sq, sp, SLOT * (b - a), T.xq, T.xs, TOK, so[:, 4 * a:4 * b], c0, ["so%d" % (a // 4), "so%d" % ((b - 1) // 4), "xq"], key)
 
-    def handed(i):
-        sq, sp, key = T["sq%d" % i], T["sp%d" % i], "w%d" % i
-        slots(sq, sp, p["pairs"][i], 0, key)
-        to = list(enumerate(p["handed"][i].items()))
-        n = 2 * SLOT // len(to)
-        call([([h], e, "hq", codes(sq, n * j, n), [codes(T.hq, 0, n)]) for j, (h, e) in to], [key + "q"])
-        call([([h], e, "hs", sp[:, n * j:n * j + n], [T.hs[:, 0:n]]) for j, (h, e) in to], [key + "s"])
+    def wave(zs, handed, straight):
+        key = "w%d" % zs[0]
+        slots(T.sq, T.sp, zs[0], zs[-1] + 1, SLOT * zs[0], key)
+        for kind in "qs":
+            cut = codes if kind == "q" else (lambda t, c, n: t[:, c:c + n])
+            src, far, home = (T.sq, T.land, T.hq) if kind == "q" else (T.sp, T.lsc, T.hs)
+            n = SLOT * (len(zs) // (len(handed) + len(straight)) - 1) + width(zs)
+            call([([h], e, "h" + kind, cut(src, SLOT * p["helpers"][h][0], n), [cut(home, 0, n)]) for h, e in handed.items()]
+                 + [([p["to"][z]], e, "dat", cut(src, SLOT * z, n), [cut(far, SLOT * place(z), n)]) for z, e in straight.items()],
+                 [key + kind])
 
-    turn(0, 0)
-    turn(0, 1)
-    join(0, 0)
-    join(0, 1)
-    turn(1, 0)
-    entries(0)
-    turn(1, 1)
-    handed(0)
-    join(1, 0)
-    join(1, 1)
-    entries(1)
-    handed(1)
-    slots(T.sq2, T.sp2, p["pairs"][2], 0, "w2")
-    slots(T.sq2, T.sp2, [p["near"]], 2 * SLOT, "w3")
-    n = SLOT if p["near"] < 2 else BOTH
-    last = list(enumerate(p["straight"].items()))
-    call([([p["to"][z]], e, "dat", codes(T.sq2, SLOT * j, n), [codes(T.land, SLOT * place(z), n)]) for j, (z, e) in last], ["w2q", "w3q"])
-    call([([p["to"][z]], e, "dat", T.sp2[:, SLOT * j:SLOT * j + n], [T.lsc[:, SLOT * place(z):SLOT * place(z) + n]])
-          for j, (z, e) in last], ["w2s", "w3s"])
+    lists(0)
+    for w in p["waves"][:p["early"]]:
+        wave(*w)
+    lists(1)
+    for w in p["waves"][p["early"]:]:
+        wave(*w)
 
     op("v", V.tensor_tensor_scan, (pp[:, 1:17], T.nl[:, 0:128:8], T.cap[:, :], 0.0, ADD, MIN), ["num", "mar", "nl0", "ml0", "cap"], ["pp1"])
     tt(bb[:, 8:15], bb[:, 0:7], T.nl[:, 0:56:8], ADD, ["bb0", "num", "nl0"], ["bb8"])
     tt(T.de[:, 0:17], bb[:, 0:17], pp[:, 0:17], SUB, ["bb0", "bb8", "bb15", "pp0", "pp1"], ["de"])
-    slots(T.land, T.lsc, [own], 0, "own")
+    slots(T.land, T.lsc, own, N, 0, "own")
     tt(dd[:, 1:17], T.de[:, 1:17], T.de[:, 0:16], SUB, ["de"], ["dd"])
     for q in range(1, 17):
         t, i = (T.ta, q) if q < 9 else (T.tz, q - 8)
         ts(t[:, i:180:9], T.ta[:, 0:180:9], pp[:, q:q + 1], dd[:, q:q + 1], GE, MUL, ["jj", "pp1", "dd"], ["tm%d" % q])
     scan2(T.cs3[:, 12:192], T.ta[:, :], T.tz[:, :], 0.0, ["jj", "tzz"] + ["tm%d" % q for q in range(1, 17)], ["cs3"])
+    quant(T.land[:, ZERO:ZERO + NZ], T.lsc[:, ZERO:ZERO + NZ], T.zin[:, :], ["zin"], ["zq"])
     tt(T.t20[:, :], T.cs3[:, 20:192:9], T.cs3[:, 11:183:9], SUB, ["cs3", "cs3z"], ["t20"])
+    quant(T.wq[:, 0:256], T.wsc[:, 0:256], T["win"][:, 0:1024], ["win0"], ["wq0"])
     ts(T.fo[:, :], T.t20[:, :], float(ZERO + NZ - 1), None, MIN, None, ["t20"], ["fo"])
 
     got = ["dat", "ownq", "owns", "zq", "fo"]

@@ -1,16 +1,19 @@
 from concourse.bass import DstId, RemoteDMATransfer
 from concourse.mybir import dt, AluOpType, AxisListType, ActivationFunctionType
 
-N, TOK, O, CAP, ROOM, BOTH = 8, 256, 4, 288, 320, 60
-SLOT = 64
+N, TOK, O, CAP, ROOM = 8, 256, 4, 288, 320
+HALF = 32
+SLOT = 2 * HALF
 FIRST = 48
 ZERO = N * SLOT
 NZ = 128
-WSLOT = 80
-WIN = N * WSLOT
-BACK = 9
-BASE = 160
+WIN = N * FIRST
+BASE = 64
+LATE = BASE + WIN
+BACK = 5
+ROW = TOK + 32
 BIG = 1024.0
+ASIDE = 4
 
 
 def _sb(n, d):
@@ -20,35 +23,44 @@ def _sb(n, d):
 F32, I32, U16, B16, MX, U8 = "float32", "int32", "uint16", "bfloat16", "float8_e4m3fn_x4", "uint8"
 SCRATCH = {
     "lists": ("dram", [N, 128, 2], I32),
-    "ct": _sb(32, I32), "xin": _sb(4 * TOK, B16), "win": _sb(512 * O, B16), "zin": _sb(4 * NZ, B16),
+    "ct": _sb(48, I32), "xin": _sb(4 * TOK, B16), "win": _sb(512 * O, B16), "zin": _sb(4 * NZ, B16),
     "xq": _sb(TOK, MX), "xs": _sb(TOK, U8), "wq": _sb(128 * O, MX), "wsc": _sb(128 * O, U8),
-    "ra": _sb(160, F32), "ca": _sb(128, F32), "e64": _sb(64, I32), "ec": _sb(64, I32), "cut": _sb(64, F32),
-    "gr": _sb(64, F32), "gt": _sb(64, F32), "gl": _sb(4, U16), "l4": _sb(4, I32), "l64": _sb(4, U16),
-    "mk": _sb(96, F32), "mgt": _sb(32, F32), "kc": _sb(8, F32),
-    "v128": _sb(128, B16), "vals": _sb(128, B16), "j0": _sb(20, I32), "z64": _sb(96, B16),
-    "pre": _sb(128, B16), "m1": _sb(64, B16), "tcol": _sb(8, F32), "bm": _sb(96, F32), "tb": _sb(128, F32), "bcol": _sb(8, F32),
-    "sc1": _sb(64, F32), "d1": _sb(64, F32), "td1": _sb(64, F32), "l8": _sb(8, U16), "kw": _sb(128, F32), "wk": _sb(128, F32),
+    "cnt": _sb(8, F32), "ra": _sb(96, F32), "ca": _sb(96, F32), "ec": _sb(128, I32), "cut": _sb(128, F32), "seg": _sb(340, F32),
+    "gr": _sb(64, F32), "gt": _sb(64, F32), "gl": _sb(4, U16), "lc": _sb(8, U16), "lf": _sb(12, F32), "lb": _sb(16, U16), "kc": _sb(16, F32),
+    "v128": _sb(128, B16), "vals": _sb(128, B16), "j0": _sb(20, F32), "cap": _sb(8, F32),
+    "pre": _sb(ROW, B16), "m1": _sb(ROW, B16), "cum1": _sb(ROW, B16), "t1": _sb(ROW, B16), "one1": _sb(64, B16),
+    "one2": _sb(72, B16), "gm1": _sb(64, F32), "top1": _sb(64, F32), "tk": _sb(56, F32), "zi": _sb(16, I32),
+    "off": _sb(16, U16), "kw": _sb(TOK, B16), "key": _sb(ROW, B16), "far2": _sb(64, F32),
     "al": _sb(64, I32), "eqs": _sb(192, B16), "bg": _sb(192, B16), "tg": _sb(64, B16), "gs": _sb(8, F32),
-    "n16": _sb(16, F32), "n8": _sb(8, B16), "nl": _sb(128, B16), "cap": _sb(16, F32),
-    "fa": _sb(64, B16), "fb": _sb(64, B16), "r2": _sb(64, B16), "cum": _sb(64, F32), "bm2": _sb(64, F32), "p2": _sb(96, F32),
-    "m16": _sb(16, F32), "m8": _sb(8, B16), "lid": _sb(64, F32), "c2b": _sb(64, F32), "d2": _sb(64, F32), "td2": _sb(64, F32),
-    "cs2": _sb(64, F32), "off": _sb(8, U16),
-    "scat": _sb(BASE + WIN, B16), "tw": _sb(2 * WIN, B16), "hh": _sb(WIN // 16, F32), "so": _sb(4 * N, U16),
-    "sq": _sb((N - 1) * SLOT, MX), "sp": _sb((N - 1) * SLOT, U8),
-    "hn": _sb(2, B16), "hq": _sb(2 * SLOT, MX), "hs": _sb(2 * SLOT, U8),
+    "nl0": _sb(8 * N, B16), "nl1": _sb(8 * N, B16),
+    "fa": _sb(ROW, B16), "fb": _sb(ROW, B16), "rf": _sb(8, F32), "ref": _sb(64, F32), "cum2": _sb(ROW, B16), "t2": _sb(ROW, B16),
+    "both": _sb(128, F32), "top2": _sb(128, F32),
+    "scat": _sb(LATE + WIN, B16), "tw": _sb(4 * WIN, B16), "hh": _sb(48, F32), "so": _sb(32, U16),
+    "sq": _sb(2 * (N - 1) * HALF, MX), "sp": _sb(2 * (N - 1) * HALF, U8),
+    "hn0": _sb(2 * N, B16), "hn1": _sb(2 * N, B16), "hq": _sb(2 * (N - 1) * HALF, MX), "hs": _sb(2 * (N - 1) * HALF, U8),
     "land": _sb(ZERO + NZ, MX), "lsc": _sb(ZERO + NZ, U8),
-    "pp": _sb(24, F32), "bb": _sb(24, F32), "de": _sb(24, F32), "dd": _sb(24, F32),
-    "ta": _sb(180, F32), "tz": _sb(180, F32), "cs3": _sb(192, F32), "t20": _sb(20, F32),
+    "pp": _sb(24, F32), "nn": _sb(24, F32), "dd": _sb(24, F32), "sd": _sb(16, F32), "sg": _sb(20 * ASIDE, F32),
+    "ta": _sb(340, F32), "cs3": _sb(340, F32),
     "fo": _sb(20, U16), "fq": _sb(ROOM, MX), "fs": _sb(ROOM, U8),
     "acc": ("psum", [128, 512 * 2 * O], F32), "yo": _sb(ROOM * O, F32),
 }
-SEMAPHORES = ["cv", "cs", "cg", "ct", "dl0", "dc1", "dc2", "dx", "dw0", "dw1", "dal", "dy", "lst", "num", "mar",
-              "dat", "hn", "hq", "hs", "left", "sent"]
+SEMAPHORES = ["cv", "cs", "cg", "ct", "dl0", "dc1", "dc2", "dx", "dw0", "dw1", "dal", "dy", "lst", "num", "mar", "dat",
+              "hn0", "hn1", "hq0", "hs0", "hq1", "hs1", "left"]
+
+ORDER = """
+loads patterns send_lists cut pad tails blocks gaps blanks constants
+columns pre columns2 z0 m1 sign lb one1 clear0 values less cum1 z1 t1 one2 edge gm1 top1 over
+kk pos1 kw u2 off0 own_n0 far2 reload hand_n0 straight_n0 patterns4 w0 w1 scatter0 named0 named1 gt counted0 counted1 gl
+turned0 turned1 key ahead0 ahead1 refused turn00 fa fb stay cum2 turn01 t2 own_n1 clear1 hand_n1 straight_n1 join00 join01
+ref quant_x gm2 lists0 top2 pick_h0 off1 pick_s0 scatter1 wave0 jj zeros turn10 turn11 join10 join11 lists1 pick_h1 pick_s1 wave1 seg
+pp spill pick_own nc aside p2 dd9 dd8 quant_w0 seconds firsts quant_z cs3 quant_w1 fo products
+""".split()
 
 ADD, SUB, MUL, MIN, MAX = AluOpType.add, AluOpType.subtract, AluOpType.mult, AluOpType.min, AluOpType.max
-GE, GT, EQ = AluOpType.is_ge, AluOpType.is_gt, AluOpType.is_equal
+GE, GT, LT, EQ = AluOpType.is_ge, AluOpType.is_gt, AluOpType.is_lt, AluOpType.is_equal
 AND = AluOpType.bitwise_and
-COPY, IDENT, SIGN = ActivationFunctionType.Copy, ActivationFunctionType.Identity, ActivationFunctionType.Sign
+COPY, IDENT, SIGN, RELU, ABS = (ActivationFunctionType.Copy, ActivationFunctionType.Identity, ActivationFunctionType.Sign,
+                                ActivationFunctionType.Relu, ActivationFunctionType.Abs)
 
 
 def deal(keys, engines):
@@ -69,17 +81,12 @@ def plan(me, cores, topo):
     wide = [c for c in free if topo.may_write(c, to[far[0]])]
     same = [c for c in free if c not in wide and topo.die(c) == topo.die(core)]
     other = [c for c in free if c not in wide and topo.die(c) != topo.die(core)]
-    first, second, third = wide[turn], other[turn], same[turn]
-    ways = {"out": out, "to": to, "lists": out[::4], "seconds": [{**deal(far[:2], out), near: inn}, deal(far[2:], out)]}
-    last = [(pairs[2], {}, deal(pairs[2], out)), ([near], {}, {near: inn})]
-    if pairs[1][1] < N // 2:
-        return {**ways, "helpers": {first: pairs[0], third: pairs[1][1:]}, "early": 2,
-                "waves": [(pairs[0], {first: out + inn}, {}), (pairs[1], {third: inn}, {pairs[1][0]: out})] + last,
-                "numbers": deal([first, third], inn), "counts": deal(pairs[1][:1] + pairs[2] + [near], out)}
-    return {**ways, "helpers": {first: pairs[0], second: pairs[1][:1], third: pairs[1][1:]}, "early": 1,
-            "waves": [(pairs[0], {first: out + inn}, {}), (pairs[1], {second: out, third: inn}, {})] + last,
-            "numbers": {**deal([first, second], inn), third: [e for e in out if e not in ways["lists"]][:4]},
-            "counts": {**deal(pairs[2], out[:4]), near: out[4:]}}
+    first, second = wide[turn], (same, other)[turn][turn]
+    on = {first: deal(pairs[0], out), second: deal(pairs[1], out)}
+    counts = {"hand": {first: (pairs[0], inn[:4]), second: (pairs[1], inn[4:])}, "straight": {**deal(pairs[2], out), near: inn}, "on": on}
+    columns = {"hand": {first: (pairs[0], out), second: (pairs[1], inn)}, "straight": {**deal(pairs[2], out), near: inn}, "on": on}
+    return {"to": to, "lists": out[::4], "last": far[3], "n0": counts, "n1": counts,
+            "q0": columns, "s0": columns, "q1": columns, "s1": columns}
 
 
 def mask(engines):
@@ -98,31 +105,42 @@ def codes(buf, c, n):
     return buf[:, c:c + n].bitcast(dt.uint8)
 
 
+def plane(buf, c, n):
+    return buf[:, c:c + n]
+
+
 def place(z):
     return N - 1 - z
 
 
-def width(zs):
-    return SLOT if min(zs) < 2 else BOTH
+def entry(late, z):
+    return 2 * N - 1 - z if late else z
 
 
-def number(T, k, n):
-    return T.nl[:, 8 * k:8 * k + n]
+def goods(T):
+    def columns(late, cut, src, home, far):
+        return (lambda z: entry(late, z) - 2 * late, lambda a, n: cut(src, HALF * a, HALF * n),
+                lambda a, n: cut(home, HALF * a, HALF * n), lambda k: cut(far, SLOT * k + HALF * late, HALF), "dat")
+
+    def counts(src, c, home, far, sem):
+        return (lambda z: z, lambda a, n: src[:, c + 2 * a:c + 2 * (a + n) - 1], lambda a, n: home[:, 2 * a:2 * (a + n) - 1],
+                lambda k: far[:, 8 * k:8 * k + 1], sem)
+
+    return {"n0": counts(T.t1, TOK + 2 * N, T.hn0, T.nl0, "num"),
+            "n1": counts(T.t2, TOK, T.hn1, T.nl1, "mar"),
+            "q0": columns(0, codes, T.sq, T.hq, T.land), "s0": columns(0, plane, T.sp, T.hs, T.lsc),
+            "q1": columns(1, codes, T.sq, T.hq, T.land), "s1": columns(1, plane, T.sp, T.hs, T.lsc)}
 
 
 def helper_program(g, p, core, T, topo):
-    zs = p["helpers"][core]
-    n = width(zs)
-    engines = deal(zs, p["out"])
-    every = sum(len(handed.get(core, [])) for _, handed, _ in p["waves"])
-    steps = [("hn", len(p["numbers"][core]), "num", lambda j: T.hn[:, j:j + 1], lambda k: number(T, k, 1)),
-             ("hq", every, "dat", lambda j: codes(T.hq, SLOT * j, n), lambda k: codes(T.land, SLOT * k, n)),
-             ("hs", every, "dat", lambda j: T.hs[:, SLOT * j:SLOT * j + n], lambda k: T.lsc[:, SLOT * k:SLOT * k + n])]
-    for sem, count, far, src, dst in steps:
-        g.wait_ge(T.sem[sem], count)
-        g.remote_dma_fused([RemoteDMATransfer(dst_ids=[at(p["to"][z], topo)], dma_engine_mask=mask(engines[z]), remote_sem=T.sem[far],
-                                              src=src(j), dst=dst(place(z))) for j, z in enumerate(zs)], local_sem=T.sem["left"])
-    g.wait_ge(T.sem["left"], len(steps) * len(p["out"]))
+    left = 0
+    for name, (number, _, home, far, sem) in goods(T).items():
+        engines = p[name]["on"][core]
+        g.wait_ge(T.sem["h" + name], len(p[name]["hand"][core][1]))
+        g.remote_dma_fused([RemoteDMATransfer(dst_ids=[at(p["to"][z], topo)], dma_engine_mask=mask(e), remote_sem=T.sem[sem],
+                                              src=home(number(z), 1), dst=far(place(z))) for z, e in engines.items()], local_sem=T.sem["left"])
+        left += sum(len(e) for e in engines.values())
+    g.wait_ge(T.sem["left"], left)
 
 
 def rank_program(g, core, T, topo):
@@ -131,7 +149,7 @@ def rank_program(g, core, T, topo):
     if me is None:
         for r in range(N):
             p = plan(r, cores, topo)
-            if core in p["helpers"]:
+            if core in p["q0"]["on"]:
                 helper_program(g, p, core, T, topo)
         return
     p = plan(me, cores, topo)
@@ -192,8 +210,8 @@ def rank_program(g, core, T, topo):
     def cp(out, a, reads, writes):
         op("v", V.tensor_copy, (out, a), reads, writes)
 
-    def red(out, a, reads, writes, **kw):
-        op("v", V.tensor_reduce, (out, a, AxisListType.X, ADD), reads, writes, **kw)
+    def red(out, a, reads, writes):
+        op("v", V.tensor_reduce, (out, a, AxisListType.X, ADD), reads, writes)
 
     def tr(out, a, reads, writes):
         op("v", V.transpose, (out, a), reads, writes)
@@ -201,237 +219,314 @@ def rank_program(g, core, T, topo):
     def quant(oq, os_, tile, reads, writes):
         op("v", V.quantize_mx, (oq, os_, tile), reads, writes)
 
-    def scan2(out, a, b, init, reads, writes):
-        op("v", V.tensor_tensor_scan, (out, a, b, init, ADD, ADD), reads, writes)
+    def scan(out, a, b, init, op0, op1, reads, writes):
+        op("v", V.tensor_tensor_scan, (out, a, b, init, op0, op1), reads, writes)
 
-    def scan(out, a, n, init, reads, writes):
-        scan2(out, a, T.z64[:, 0:n], init, reads + ["z64"], writes)
+    def count(out, a, init, reads, writes):
+        scan(out, a, a, init, ADD, MAX, reads, writes)
 
-    def top8(out, a, reads, writes):
-        op("v", V.tensor_tensor_scan, (out, T.cut[:, :], a, 0.0, MIN, MAX), reads + ["cut"], writes)
+    def top(out, cut, a, reads, writes):
+        scan(out, cut, a, 0.0, MIN, MAX, reads + ["cut"], writes)
 
     def fill(ap, val, key):
         op("v", V.memset, (ap, val), [], [key])
 
-    def iota(ap, key, pattern, base, flag=True):
-        kw = {"allow_small_or_imprecise_dtypes": True} if flag else {}
-        op("g", g.iota, (ap, pattern, base, 0), [], [key], **kw)
+    def iota(ap, key, pattern, base):
+        op("g", g.iota, (ap, pattern, base, 0), [], [key], allow_small_or_imprecise_dtypes=True)
 
     def act(out, a, reads, writes, **kw):
         op("s", g.scalar.activation, (out, a, COPY), reads, writes, **kw)
 
-    def line(out, a, scale, bias, reads, writes):
-        op("s", g.scalar.activation, (out, a, IDENT, bias, scale), reads, writes)
+    def line(out, a, scale, bias, reads, writes, func=IDENT):
+        op("s", g.scalar.activation, (out, a, func, bias, scale), reads, writes)
 
-    def call(transfers, reads, left="left"):
+    def call(transfers, reads):
         before("g", reads, [])
         g.remote_dma_fused([RemoteDMATransfer(dst_ids=[at(c, topo) for c in to], dma_engine_mask=mask(e), remote_sem=T.sem[sem],
-                                              srcs=[src], dsts=dst) for to, e, sem, src, dst in transfers], local_sem=T.sem[left])
-        cnt[left] = cnt.get(left, 0) + sum(len(t[1]) for t in transfers)
+                                              srcs=[src], dsts=dst) for to, e, sem, src, dst in transfers], local_sem=T.sem["left"])
+        cnt["left"] = cnt.get("left", 0) + sum(len(t[1]) for t in transfers)
 
+    sent = goods(T)
     cnt["lst"] = cnt["num"] = cnt["mar"] = cnt["dat"] = 0
     for k in range(1, N):
         o, z = plan((me + k) % N, cores, topo), N - 1 - k
-        handed = sum(len(o["out"]) // len(zs) for zs in o["helpers"].values() if z in zs)
         cnt["lst"] += len(o["lists"])
-        cnt["num"] += len(o["counts"][z]) if z in o["counts"] else handed
-        cnt["mar"] += sum(len(e.get(z, [])) for e in o["seconds"])
-        cnt["dat"] += 2 * (handed + sum(len(e.get(z, [])) for _, _, e in o["waves"]))
+        for name, piece in sent.items():
+            cnt[piece[4]] += sum(len(e.get(z, [])) for e in [o[name]["straight"]] + list(o[name]["on"].values()))
     for sem in ("lst", "num", "mar", "dat"):
         wr[sem] = [(sem, cnt[sem])]
 
-    dma("y", "dl0", T.lists[0], T.c1[:, :], [], ["l0"])
-    for b in range(8):
-        dma("ys"[b % 2], "dc1", T.ct[16 * b:16 * b + 16, 0:16], T.c1[:, :], [], ["c1"])
-    for b in range(8):
-        dma("sy"[b % 2], "dc2", T.ct[16 * b:16 * b + 16, 16:32], T.c2[:, :], [], ["c2"])
-    dma("y", "dx", T.xin[:, :], T.x[:, :], [], ["xin"])
+    def hand(name, reads):
+        number, src, home, _, _ = sent[name]
+        runs = [(h, e, min(number(z) for z in zs), len(zs)) for h, (zs, e) in p[name]["hand"].items()]
+        call([([h], e, "h" + name, src(a, n), [home(a, n)]) for h, e, a, n in runs], reads)
 
-    ra, kc, mk, pp, bb, dd = T.ra, T.kc, T.mk, T.pp, T.bb, T.dd
-    iota(ra[:, 64:96], "ra1", [[1, 2], [4, 2], [0, 8]], 0)
-    iota(ra[:, 0:64], "ra0", [[0, 8], [1, 8]], 0)
-    iota(ra[:, 96:128], "ra2", [[1, 4], [0, 8]], 0)
-    iota(ra[:, 128:160], "ra3", [[16, 2], [0, 16]], 0)
-    iota(T.l4[:, :], "l4", [[2, 2], [8, 2]], 0, flag=False)
-    iota(T.e64[:, :], "e64", [[1, 64]], me + 1, flag=False)
-    call([(p["to"], p["lists"], "lst", T.lists[0], [T.lists[place(z)] for z in range(N - 1)])], ["l0"])
-    iota(T.v128[:, :], "v128", [[32, 2], [64, 4], [1, 16]], 0)
+    def straight(name, reads):
+        number, src, _, far, sem = sent[name]
+        call([([p["to"][z]], e, sem, src(number(z), 1), [far(place(z))]) for z, e in p[name]["straight"].items()], reads)
+
+    ra, kc, pre, scat, key, tk, zi, lb, rf = T.ra, T.kc, T.pre, T.scat, T.key, T.tk, T.zi, T.lb, T.rf
+    eqs, tg, gs, pp, nn, dd, tw, hh, so, ta = T.eqs, T.tg, T.gs, T.pp, T.nn, T.dd, T.tw, T.hh, T.so, T.ta
+    zc, hi, odd = [T.ca[:, 32 * j:32 * j + 1] for j in range(3)]
+    base1, qc, z2, two, less, over, half0, many0, mid, reach = [kc[:, j:j + 1] for j in range(10)]
+    sgn, kk, edge, pos1, u2, way = [tk[:, 8 * j:8 * j + 8] for j in range(6)]
+    ec, kw = ["ec%d" % z for z in range(N)], ["kw%d" % b for b in range(8)]
+    num1 = T.top1[:, 7:64:8]
+    step = {}
+
+    def loads():
+        dma("y", "dl0", T.lists[0], T.c1[:, :], [], ["l0"])
+        for b in range(8):
+            dma("sy"[b % 2], "dc1", T.ct[16 * b:16 * b + 16, 8 - b % 2:24 - b % 2], T.c1[:, :], [], ["c1"])
+        for b in range(8):
+            dma("sy"[b % 2], "dc2", T.ct[16 * b:16 * b + 16, 32 - b % 2:48 - b % 2], T.c2[:, :], [], ["c2"])
+        dma("y", "dx", T.xin[:, :], T.x[:, :], [], ["xin"])
+
+    def reload():
+        for b in range(4):
+            dma("y", "dal", T.al[32 * b:32 * b + 32, 0:64], T.lists[:, :, :], ["lst", "l0"], ["al"])
+
+    step.update(
+        loads=loads, reload=reload,
+        w0=lambda: dma("y", "dw0", T["win"][:, 0:1024], T.w[:, 0:1024], ["al"], ["win0"]),
+        w1=lambda: dma("y", "dw1", T["win"][:, 1024:2048], T.w[:, 1024:2048], ["al"], ["win1"]),
+        send_lists=lambda: call([(p["to"], p["lists"], "lst", T.lists[0], [T.lists[place(z)] for z in range(N - 1)])], ["l0"]),
+        hand_n0=lambda: hand("n0", ["t1", "al"]), straight_n0=lambda: straight("n0", ["t1"]),
+        hand_n1=lambda: hand("n1", ["t2"]), straight_n1=lambda: straight("n1", ["t2"]))
+
+    def patterns():
+        iota(T.cnt[:, :], "cnt", [[1, 8]], 0)
+        iota(ra[:, 0:32], "ra0", [[0, 4], [1, 8]], 0)
+        iota(ra[:, 32:64], "ra1", [[0, 2], [1, 2], [0, 8]], 0)
+        iota(ra[:, 64:96], "ra2", [[16, 2], [0, 16]], 0)
 
     def blocks():
-        for i in range(2):
-            iota(T.gr[:, 32 * i:32 * i + 32], "gr%d" % i, [[-1, 2], [WSLOT // 16, 4], [1, 4]], 1 + WSLOT // 4 * i)
-        iota(T.gr[:, 3:32:16], "gr0", [[-1, 2]], 1 + BACK)
+        iota(T.v128[:, :], "v128", [[32, 8], [1, 16]], 0)
+        n = FIRST // 16
+        iota(T.gr[:, 32:64], "gr1", [[-1, 2], [-n, N], [1, 2]], 1 + n * own)
+        iota(T.gr[:, 0:32], "gr0", [[-1, 2], [n, N], [1, 2]], 1)
+        iota(T.gr[:, 47:64:16], "gr1", [[-1, 2]], 1 + BACK)
 
-    def later():
-        iota(T.j0[:, :], "j0", [[16, 20]], 0, flag=False)
-        iota(bb[:, 0:8], "bb0", [[SLOT, 8]], 0)
-        iota(T.cap[:, :], "cap", [[int(BIG), 2], [0, 8]], CAP)
-        iota(bb[:, 15:17], "bb15", [[SLOT - FIRST, 2]], SLOT * (N - 1) + FIRST)
+    def blanks():
+        iota(key[:, TOK:ROW], "keyz", [[0, 32]], 0)
+        iota(T.both[:, 0:128:2], "bothz", [[0, 64]], 0)
 
-    fill(T.scat[:, BASE - 16:BASE + WIN], 0.0, "scat")
-    fill(T.z64[:, :], 0.0, "z64")
-    fill(mk[:, 32:64], 1.0, "ones")
-    fill(T.eqs[:, 0:192], 0.0, "eqz")
-    fill(T.cs3[:, 0:12], 0.0, "cs3z")
-    fill(pp[:, 0:1], 0.0, "pp0")
-    tr(T.ca[:, :], ra[:, 32:160], ["ra0", "ra1", "ra2", "ra3"], ["ca"])
-    zc, pc, hc, odd = [T.ca[:, 32 * j:32 * j + 1] for j in range(4)]
-    zpos, t1, t2, q4, q8, q9, qc = [kc[:, j:j + 1] for j in range(7)]
-    ts(T.l64[:, :], T.l4[:, :], pc, None, ADD, None, ["l4", "ca"], ["l64"])
-    ts(mk[:, 64:96], ra[:, 0:32], zc, None, EQ, None, ["ra0", "ca"], ["meq"])
-    ts(T.ec[:, :], T.e64[:, :], 7, None, AND, None, ["e64"], ["ec"])
-    line(q4, odd, -1 / 16, pc, ["ca"], ["q4"])
-    line(T.tb[:, 31:32], zc, float(WSLOT), BASE - 1.0, ["ca"], ["tb0"])
-    line(q8, q4, 2.0, 0.0, ["q4"], ["q8"])
-    line(q9, q4, 2.0, 1.0, ["q4"], ["q9"])
-    line(qc, q4, 2.0, zc, ["q4", "ca"], ["qc"])
-    op("s", g.scalar.activation, (zpos, zc, SIGN), ["ca"], ["zpos"])
-    line(t1, zc, float(WSLOT), BASE + 16.0 * BACK - 1, ["ca"], ["t1"])
-    line(T.cut[:, :], ra[:, 0:64], 4 * BIG, 0.0, ["ra0"], ["cut"])
-    line(t2, zpos, -16.0 * BACK, t1, ["zpos", "t1"], ["t2"])
+    def clear0():
+        for a, b in ((BASE - 16, BASE + TOK), (BASE + TOK, LATE)):
+            act(scat[:, a:b], pre[:, 0:b - a], ["pre"], ["scat%d" % a], scale=0.0)
 
-    l64 = T.l64[:, 0:4]
-    c1w, c2w = T.ct[:, 0:16].indirect(l64), T.ct[:, 16:32].indirect(l64)
-    m1, bcol = T.m1[:, :], T.bcol
-    tt(T.pre[:, 0:64], c1w, T.ec[:, :], EQ, ["c1", "l64", "ec"], ["pre0"])
-    ts(T.mgt[:, :], ra[:, 96:128], hc, None, GT, None, ["ra2", "ca"], ["mgt"])
-    tr(m1, T.pre[:, 0:64], ["pre0"], ["m1"])
-    tt(mk[:, 0:32], mk[:, 64:96], T.mgt[:, :], MUL, ["meq", "mgt"], ["mlt"])
-    red(T.tcol[:, 0:1], m1, ["m1"], ["tcol"])
-    tt(T.pre[:, 64:128], c2w, T.ec[:, :], EQ, ["c2", "l64", "ec"], ["pre1"])
-    ts(T.bm[:, :], mk[:, :], T.tcol[:, 0:1], None, MUL, None, ["meq", "mlt", "ones", "tcol"], ["bm"])
-    ts(T.l8[:, 0:4], ra[:, 0:4], 16.0, q8, MUL, ADD, ["ra0", "q8"], ["l80"])
-    tr(T.tb[:, 32:128], T.bm[:, :], ["bm"], ["tb"])
-    ts(T.l8[:, 4:8], ra[:, 0:4], 16.0, q9, MUL, ADD, ["ra0", "q9"], ["l81"])
-    red(bcol[:, 0:1], T.tb[:, 31:64], ["tb", "tb0"], ["b1"])
-    tt(T.n16[:, :], T.tb[:, 64:80], T.tb[:, 80:96], ADD, ["tb"], ["n16"])
-    scan(T.sc1[:, :], m1, 64, bcol[:, 0:1], ["m1", "b1"], ["sc1"])
-    tt(T.n8[:, :], T.n16[:, 0:8], T.n16[:, 8:16], ADD, ["n16"], ["n8"])
-    for b in range(4):
-        dma("ys"[b % 2], "dal", T.al[32 * b:32 * b + 32, 0:64], T.lists[:, :, :], ["lst", "l0"], ["al"])
-    call([([h], p["numbers"][h], "hn", T.n8[:, zs[0]:zs[0] + 2], [T.hn[:, :]]) for h, zs in p["helpers"].items()], ["n8"])
-    blocks()
-    call([([p["to"][z]], e, "num", T.n8[:, z:z + 1], [number(T, place(z), 1)]) for z, e in p["counts"].items()], ["n8", "lst"], "sent")
-    wr["sent"] = [("sent", cnt["sent"])]
-    later()
-    dma("y", "dw0", T["win"][:, 0:1024], T.w[:, 0:1024], ["al"], ["win0"])
-    dma("y", "dw1", T["win"][:, 1024:2048], T.w[:, 1024:2048], ["sent"], ["win1"])
-    act(number(T, 0, 1), T.n8[:, own:own + 1], ["n8"], ["nl0"])
-    act(T.mgt[:, :], T.tb[:, 96:128], ["tb"], ["mgt", "nz"], accum_out=bcol[:, 3:4])
-    line(T.p2[:, 31:32], bcol[:, 3:4], zpos, t2, ["nz", "zpos", "t2"], ["p2k"])
-    tt(T.d1[:, :], m1, T.sc1[:, :], MUL, ["m1", "sc1"], ["d1"])
-    quant(T.xq[:, :], T.xs[:, :], T.xin[:, :], ["xin"], ["xq"])
-    tr(T.td1[:, :], T.d1[:, :], ["d1"], ["td1"])
-    fill(T.tz[:, 0:180:9], 0.0, "tzz")
-    for i in range(2):
-        tt(T.kw[:, 64 * i:64 * i + 64], T.td1[:, :].indirect(T.l8[:, 4 * i:4 * i + 4]), T.pre[:, 64:128], MUL,
-           ["td1", "l8%d" % i, "pre1"], ["kw%d" % i])
-    tr(T.wk[:, :], T.kw[:, :], ["kw0", "kw1"], ["wk"])
+    def patterns4():
+        iota(T.j0[:, :], "j0", [[16, 20]], 0)
+        iota(T.cap[:, :], "cap", [[0, 8]], CAP)
+        iota(nn[:, 14:16], "spill6", [[0, 2]], 0)
+        iota(nn[:, 21:23], "jump5", [[HALF - FIRST, 2]], SLOT + FIRST - HALF)
+        iota(nn[:, 23:24], "jump7", [[0, 1]], SLOT - FIRST)
+        iota(pp[:, 0:1], "pp0", [[0, 1]], 0)
 
-    line(T.vals[:, :], T.v128[:, :], 1.0, odd, ["v128", "ca"], ["vals"])
-    eqs = T.eqs
-    act(T.zin[:, :], T.xin[:, 0:4 * NZ], ["xin"], ["zin"], scale=0.0)
-    for i in range(2):
-        ts(eqs[:, 96 * i:96 * i + 64], T.al[:, :], float((me + 1 + i) % N), None, EQ, None, ["al", "eqz"], ["eq%d" % i])
-    for i in range(2):
-        scan(T.bg[:, 96 * i:96 * i + 96], eqs[:, 96 * i:96 * i + 96], 96, -(BASE + WSLOT * i + CAP) / (28.0 - 4 * i),
-             ["eq%d" % i, "eqz"], ["bg%d" % i])
-    for i in range(2):
-        tr(T.tg[:, 32 * i:32 * i + 32], T.bg[:, 96 * i + 64:96 * i + 96], ["bg%d" % i], ["tg%d" % i])
-    for i in range(2):
-        red(T.gs[:, i:i + 1], T.tg[:, 36 * i + 4:32 * i + 32], ["tg%d" % i], ["gs%d" % i], negate=True)
+    def constants():
+        for z in range(N):
+            fill(T.ec[:, z:128:N], (me + 1 + z) % N, "ec%d" % z)
+        fill(pre[:, :], 0.0, "pre")
+        ts(T.lc[:, :], T.cnt[:, :], 2.0, None, MUL, None, ["cnt"], ["lc0"])
 
-    ts(T.fa[:, :], T.wk[:, 0:64], T.gs[:, 0:1], BIG, GE, MUL, ["wk", "gs0"], ["fa"])
-    ts(T.fb[:, :], T.wk[:, 64:128], T.gs[:, 1:2], BIG, GE, MUL, ["wk", "gs1"], ["fb"])
-    scan2(T.cum[:, :], T.fa[:, :], T.fb[:, :], 0.0, ["fa", "fb"], ["cum"])
-    tt(T.r2[:, :], T.fa[:, :], T.fb[:, :], ADD, ["fa", "fb"], ["r2"])
-    ts(T.bm2[:, :], mk[:, 0:64], T.cum[:, 63:64], 1 / BIG, MUL, MUL, ["mlt", "ones", "cum"], ["bm3"])
-    tr(T.p2[:, 32:96], T.bm2[:, :], ["bm3"], ["p2"])
-    tt(T.lid[:, :], T.r2[:, :], T.d1[:, :], ADD, ["r2", "d1"], ["lid"])
-    red(bcol[:, 4:5], T.p2[:, 31:64], ["p2", "p2k"], ["b2"])
-    tt(T.m16[:, :], T.p2[:, 64:80], T.p2[:, 80:96], ADD, ["p2"], ["m16"])
-    ts(T.c2b[:, :], T.cum[:, :], 1 / BIG, bcol[:, 4:5], MUL, ADD, ["cum", "b2"], ["c2b"])
-    tt(T.m8[:, :], T.m16[:, 0:8], T.m16[:, 8:16], ADD, ["m16"], ["m8"])
-    tt(T.d2[:, :], T.c2b[:, :], T.lid[:, :], MIN, ["c2b", "lid"], ["d2"])
-    for engines in p["seconds"]:
-        call([([p["to"][z]], e, "mar", T.m8[:, z:z + 1], [number(T, N + place(z), 1)]) for z, e in engines.items()], ["m8"])
-    act(number(T, N, 1), T.m8[:, own:own + 1], ["m8"], ["ml0"])
-    tr(T.gt[:, :], T.gr[:, :], ["gr0", "gr1"], ["gt"])
-    tr(T.td2[:, :], T.d2[:, :], ["d2"], ["td2"])
-    cp(T.gl[:, 0:4:2], T.gt[:, 0:64:32], ["gt"], ["gl"])
-    top8(T.cs2[:, :], T.td2[:, :], ["td2"], ["cs2"])
-    ts(T.ta[:, 0:180:9], T.j0[:, :], qc, None, ADD, None, ["j0", "qc"], ["jj"])
-    cp(T.off[:, :], T.cs2[:, 7:64:8], ["cs2"], ["off"])
-    op("v", V.tensor_copy, (T.scat[:, :].indirect(T.off[:, 0:8]), T.vals[:, :]), ["off", "vals"], ["scat"])
+    def columns2():
+        f8, f2, fr = [T.lf[:, 4 * j:4 * j + 4] for j in range(3)]
+        line(fr, T.cnt[:, 0:4], 2.0, hi, ["cnt", "ca"], ["fr"])
+        line(z2, zc, 2.0, 0.0, ["ca"], ["z2"])
+        line(base1, odd, (1.0 - BASE) / 16, BASE - 1.0, ["ca"], ["base1"])
+        line(qc, hi, 8.0, zc, ["ca"], ["qc"])
+        line(f8, fr, 32.0, z2, ["fr", "z2"], ["f8"])
+        line(f2, fr, 2.0, 0.0, ["fr"], ["f2"])
+        line(two, qc, 1.0, -3.5, ["qc"], ["two"], SIGN)
 
-    tw, hh, so = T.tw, T.hh, T.so
-    def lists(i):
-        a, b = WIN // 2 * i, WIN // 2 * (i + 1)
-        for late in range(2):
-            tr(tw[:, late * WIN + a:late * WIN + b], T.scat[:, BASE - 16 * late + a:BASE - 16 * late + b], ["scat"], ["tw%d%d" % (late, i)])
-        for late in range(2):
-            c, d = late * WIN + a, late * WIN + b
-            tt(hh[:, a // 16 + 1 - late:b // 16:2], tw[:, c:d:32], tw[:, c + 16:d:32], ADD, ["tw%d%d" % (late, i)], ["hh%d%d" % (late, i)])
-        cp(so[:, 16 * i:16 * i + 16], hh[:, 0:b // 16].indirect(T.gl[:, 2 * i:2 * i + 1]),
-           ["gl"] + ["hh%d%d" % (late, j) for late in range(2) for j in range(i + 1)], ["so%d" % i])
+    l8, l2, lr = [lb[:, 4 * j:4 * j + 4] for j in range(3)]
+    step.update(
+        patterns=patterns, blocks=blocks, blanks=blanks, clear0=clear0, patterns4=patterns4, constants=constants, columns2=columns2,
+        cut=lambda: iota(T.cut[:, :], "cut", [[0, 8], [int(BIG), 16]], 0),
+        values=lambda: line(T.vals[:, :], T.v128[:, :], 1.0, odd, ["v128", "ca"], ["vals"]),
+        seg=lambda: iota(T.seg[:, :], "seg", [[0, 20], [int(BIG), 17]], 0),
+        clear1=lambda: act(scat[:, LATE:LATE + WIN], T.xin[:, 0:WIN], ["xin"], ["scat%d" % LATE], scale=0.0),
+        pad=lambda: iota(T.one2[:, 64:72], "one2z", [[0, 8]], 0), gaps=lambda: iota(T.kw[:, 1:TOK:2], "kwz", [[0, 128]], 0),
+        less=lambda: line(less, two, BIG, -(BASE + HALF - 1.0 + BIG), ["two"], ["less"]),
+        tails=lambda: [iota(eqs[:, 96 * i + 64:96 * i + 96], "eqz%d" % i, [[0, 32]], 0) for i in range(2)],
+        columns=lambda: tr(T.ca[:, :], ra[:, :], ["ra0", "ra1", "ra2"], ["ca"]),
+        lb=lambda: cp(lb[:, 0:12], T.lf[:, :], ["f8", "f2", "fr"], ["l8", "l2", "lr"]),
+        gt=lambda: tr(T.gt[:, :], T.gr[:, :], ["gr0", "gr1"], ["gt"]),
+        gl=lambda: cp(T.gl[:, 0:4:2], T.gt[:, 0:64:32], ["gt"], ["gl"]))
+
+    def keys():
+        for b in range(8):
+            line(T.kw[:, 32 * b:32 * b + 32:2], T.one2[:, 8 * b:8 * b + 16], tk[:, 8 + b:9 + b], 0.0, ["one2", "one2z", "kk"], ["kw%d" % b])
+
+    def begins():
+        for z in range(N):
+            act(T.far2[:, z:64:N], T.one2[:, z:64:N], ["one2"], ["far%d" % z], scale=LATE - 1.0 + {0: 16 * BACK, 1: FIRST + 16}.get(z, FIRST * z))
+
+    def moved():
+        line(way, num1, 1.0, -(BASE + HALF - 0.5), ["top1"], ["way"], SIGN)
+        line(u2, way, (WIN - HALF) / 2, (WIN - HALF) / 2, ["way"], ["u2"])
+
+    step.update(
+        pre=lambda: tt(pre[:, 0:TOK:2], T.ct[:, 8:23].indirect(T.lc[:, 0:8]), T.ec[:, :], EQ, ["c1", "lc0"] + ec, ["pre"]),
+        m1=lambda: tr(T.m1[:, :], pre[:, :], ["pre"], ["m1"]),
+        sign=lambda: tt(sgn, pre[:, 0:TOK:32], pre[:, 2:TOK:32], SUB, ["pre"], ["sgn"]),
+        one1=lambda: act(T.one1[:, :], pre[:, 0:TOK].indirect(l8), ["pre", "l8"], ["one1"]),
+        cum1=lambda: count(T.cum1[:, :], T.m1[:, :], base1, ["m1", "base1"], ["cum1"]),
+        one2=lambda: tt(T.one2[:, 0:64], T.ct[:, 32:47].indirect(l2), T.ec[:, 0:64], EQ, ["c2", "l2"] + ec, ["one2"]),
+        t1=lambda: tr(T.t1[:, :], T.cum1[:, :], ["cum1"], ["t1"]),
+        gm1=lambda: tt(T.gm1[:, :], T.t1[:, 0:TOK].indirect(l8), T.one1[:, :], MUL, ["t1", "l8", "one1"], ["gm1"]),
+        top1=lambda: top(T.top1[:, :], T.cut[:, 0:128:2], T.gm1[:, :], ["gm1"], ["top1"]),
+        pos1=lambda: tt(pos1, num1, edge, ADD, ["top1", "edge"], ["pos1"]),
+        off0=lambda: cp(T.off[:, 0:8], pos1, ["pos1"], ["off0"]),
+        over=lambda: line(over, T.cum1[:, ROW - 1:ROW], 1.0, less, ["cum1", "less"], ["over"], RELU),
+        z0=lambda: ts(zi[:, 0:8], T.ct[:, 8:23:2], float(N - 1 - me), None, ADD, None, ["c1"], ["zi0"]),
+        z1=lambda: ts(zi[:, 8:16], zi[:, 0:8], N - 1, None, AND, None, ["zi0"], ["zi1"]),
+        edge=lambda: ts(edge, zi[:, 8:16], float(FIRST), None, MUL, None, ["zi1"], ["edge"]),
+        u2=moved,
+        far2=begins,
+        stay=lambda: tt(T.both[:, 0:128:16], u2, pos1, ADD, ["u2", "pos1", "bothz"], ["stay"]),
+        kk=lambda: tt(kk, num1, sgn, MUL, ["top1", "sgn"], ["kk"]),
+        kw=keys,
+        key=lambda: tr(key[:, 0:TOK], T.kw[:, :], kw + ["kwz"], ["key"]))
+
+    def named(i):
+        ts(eqs[:, 96 * i:96 * i + 64], T.al[:, :], float((me + 1 + i) % N), None, EQ, None, ["al"], ["eq%d" % i])
+
+    def counted(i):
+        count(T.bg[:, 96 * i:96 * i + 96], eqs[:, 96 * i:96 * i + 96], 0.0, ["eq%d" % i, "eqz%d" % i], ["bg%d" % i])
+
+    def turned(i):
+        tr(tg[:, 32 * i:32 * i + 32], T.bg[:, 96 * i + 64:96 * i + 96], ["bg%d" % i], ["tg%d" % i])
+
+    def ahead(i):
+        red(gs[:, i:i + 1], tg[:, 36 * i + 4:32 * i + 32], ["tg%d" % i], ["gs%d" % i])
+
+    limit = CAP + BASE - 1.0
+
+    def refused():
+        line(half0, gs[:, 0:1], 0.5, 0.0, ["gs0"], ["half0"])
+        line(many0, gs[:, 0:1], BIG / 2, -BIG * limit, ["gs0"], ["many0"])
+        line(mid, gs[:, 1:2], -0.5, half0, ["gs1", "half0"], ["mid"])
+        line(reach, gs[:, 1:2], BIG / 2, many0, ["gs1", "many0"], ["reach"])
+        line(way, kk, 1.0, mid, ["kk", "mid"], ["way"], ABS)
+        line(rf[:, :], way, BIG, reach, ["way", "reach"], ["rf"], RELU)
+
+    step.update(
+        refused=refused,
+        fa=lambda: ts(T.fa[:, :], key[:, :], gs[:, 0:1], limit, ADD, GT, ["key", "keyz", "gs0"], ["fa"]),
+        fb=lambda: ts(T.fb[:, :], key[:, :], gs[:, 1:2], -limit, SUB, LT, ["key", "keyz", "gs1"], ["fb"]),
+        cum2=lambda: scan(T.cum2[:, :], T.fa[:, :], T.fb[:, :], over, ADD, ADD, ["fa", "fb", "over"], ["cum2"]),
+        t2=lambda: tr(T.t2[:, :], T.cum2[:, :], ["cum2"], ["t2"]),
+        ref=lambda: tt(T.ref[:, :], rf[:, :].indirect(lr), T.far2[:, :], MIN, ["rf", "lr"] + ["far%d" % z for z in range(N)], ["ref"]),
+        gm2=lambda: tt(T.both[:, 1:128:2], T.t2[:, :].indirect(l8), T.ref[:, :], ADD, ["t2", "ref", "l8"], ["gm2"]),
+        top2=lambda: top(T.top2[:, :], T.cut[:, :], T.both[:, :], ["gm2", "stay", "bothz"], ["top2"]),
+        off1=lambda: cp(T.off[:, 8:16], T.top2[:, 15:128:16], ["top2"], ["off1"]))
+
+    def scatter(late):
+        op("v", V.tensor_copy, (scat[:, 0:LATE + WIN * late].indirect(T.off[:, 8 * late:8 * late + 8]), T.vals[:, :]),
+           ["off%d" % late, "vals"] + ["scat%d" % a for a in (BASE - 16, BASE + TOK, LATE)[:2 + late]], ["scat"])
+
+    def turn(late, j):
+        a, c = BASE + WIN * late - 16 * j, WIN * (2 * late + j)
+        tr(tw[:, c:c + WIN], scat[:, a:a + WIN], ["scat"], ["tw%d%d" % (late, j)])
+
+    def join(late, j):
+        c = WIN * (2 * late + j)
+        tt(hh[:, 24 * late + 1 - j:24 * late + 24:2], tw[:, c:c + WIN:32], tw[:, c + 16:c + WIN:32], ADD, ["tw%d%d" % (late, j)], ["hh%d%d" % (late, j)])
+
+    def lists(late):
+        cp(so[:, 16 * late:16 * late + 16], hh[:, 24 * late:24 * late + 24].indirect(T.gl[:, 2 * late:2 * late + 1]),
+           ["gl", "hh%d0" % late, "hh%d1" % late], ["so%d" % late])
 
     def pick(oq, os_, n, iq, is_, m, off, n0, reads, writes):
-        op("v", V.tensor_copy, (oq[:, n0:n0 + n].bitcast(dt.uint32), iq[:, 0:m].bitcast(dt.uint32).indirect(off)), reads, [writes + "q"])
-        act(os_[:, n0:n0 + n], is_[:, 0:m].indirect(off), reads, [writes + "s"])
+        op("v", V.tensor_copy, (oq[:, n0:n0 + n].bitcast(dt.uint32), iq[:, 0:m].bitcast(dt.uint32).indirect(off)), reads, [k + "q" for k in writes])
+        act(os_[:, n0:n0 + n], is_[:, 0:m].indirect(off), reads, [k + "s" for k in writes])
 
-    def slots(sq, sp, a, b, c0, key):
-        pick(sq, sp, SLOT * (b - a), T.xq, T.xs, TOK, so[:, 4 * a:4 * b], c0, ["so%d" % (a // 4), "so%d" % ((b - 1) // 4), "xq"], key)
+    def slots(late, zs, keys):
+        a, b = min(entry(late, z) for z in zs), max(entry(late, z) for z in zs) + 1
+        pick(T.sq, T.sp, HALF * (b - a), T.xq, T.xs, TOK, so[:, 2 * a:2 * b], HALF * (a - 2 * late), ["so%d" % late, "xq"], keys)
 
-    def wave(zs, handed, straight):
-        key = "w%d" % zs[0]
-        slots(T.sq, T.sp, zs[0], zs[-1] + 1, SLOT * zs[0], key)
+    def wave(late):
         for kind in "qs":
-            cut = codes if kind == "q" else (lambda t, c, n: t[:, c:c + n])
-            src, far, home = (T.sq, T.land, T.hq) if kind == "q" else (T.sp, T.lsc, T.hs)
-            n = SLOT * (len(zs) // (len(handed) + len(straight)) - 1) + width(zs)
-            call([([h], e, "h" + kind, cut(src, SLOT * p["helpers"][h][0], n), [cut(home, 0, n)]) for h, e in handed.items()]
-                 + [([p["to"][z]], e, "dat", cut(src, SLOT * z, n), [cut(far, SLOT * place(z), n)]) for z, e in straight.items()],
-                 [key + kind])
+            hand(kind + str(late), ["h%d%s" % (late, kind)])
+        for kind in "qs":
+            straight(kind + str(late), ["h%d%s" % (late, kind), "s%d%s" % (late, kind)])
 
-    lists(0)
-    for w in p["waves"][:p["early"]]:
-        wave(*w)
-    lists(1)
-    for w in p["waves"][p["early"]:]:
-        wave(*w)
+    last = p["last"]
+    for i in range(2):
+        for name, f in (("named", named), ("counted", counted), ("turned", turned), ("ahead", ahead), ("scatter", scatter),
+                        ("lists", lists), ("wave", wave)):
+            step[name + str(i)] = lambda f=f, i=i: f(i)
+        for j in range(2):
+            step["turn%d%d" % (i, j)] = lambda i=i, j=j: turn(i, j)
+            step["join%d%d" % (i, j)] = lambda i=i, j=j: join(i, j)
+        step["pick_h%d" % i] = lambda i=i: slots(i, range(last + 1), ["h%d" % i])
+        step["pick_s%d" % i] = lambda i=i: slots(i, range(last + 1, own), ["s%d" % i])
 
-    op("v", V.tensor_tensor_scan, (pp[:, 1:17], T.nl[:, 0:128:8], T.cap[:, :], 0.0, ADD, MIN), ["num", "mar", "nl0", "ml0", "cap"], ["pp1"])
-    tt(bb[:, 8:15], bb[:, 0:7], T.nl[:, 0:56:8], ADD, ["bb0", "num", "nl0"], ["bb8"])
-    tt(T.de[:, 0:17], bb[:, 0:17], pp[:, 0:17], SUB, ["bb0", "bb8", "bb15", "pp0", "pp1"], ["de"])
-    slots(T.land, T.lsc, own, N, 0, "own")
-    tt(dd[:, 1:17], T.de[:, 1:17], T.de[:, 0:16], SUB, ["de"], ["dd"])
-    for q in range(1, 17):
-        t, i = (T.ta, q) if q < 9 else (T.tz, q - 8)
-        ts(t[:, i:180:9], T.ta[:, 0:180:9], pp[:, q:q + 1], dd[:, q:q + 1], GE, MUL, ["jj", "pp1", "dd"], ["tm%d" % q])
-    scan2(T.cs3[:, 12:192], T.ta[:, :], T.tz[:, :], 0.0, ["jj", "tzz"] + ["tm%d" % q for q in range(1, 17)], ["cs3"])
-    quant(T.land[:, ZERO:ZERO + NZ], T.lsc[:, ZERO:ZERO + NZ], T.zin[:, :], ["zin"], ["zq"])
-    tt(T.t20[:, :], T.cs3[:, 20:192:9], T.cs3[:, 11:183:9], SUB, ["cs3", "cs3z"], ["t20"])
-    quant(T.wq[:, 0:256], T.wsc[:, 0:256], T["win"][:, 0:1024], ["win0"], ["wq0"])
-    ts(T.fo[:, :], T.t20[:, :], float(ZERO + NZ - 1), None, MIN, None, ["t20"], ["fo"])
+    n0, n1 = T.nl0[:, 0:8 * N:8], T.nl1[:, 0:8 * N:8]
+    places = ta[:, 0:340:17]
 
-    got = ["dat", "ownq", "owns", "zq", "fo"]
-    cut = 128
-    for i, (a, b) in enumerate(((0, cut), (cut, ROOM))):
-        pick(T.fq, T.fs, b - a, T.land, T.lsc, ZERO + NZ, T.fo[:, a // 16:b // 16], a, got, "f%d" % i)
-    quant(T.wq[:, 256:512], T.wsc[:, 256:512], T["win"][:, 1024:2048], ["win1"], ["wq1"])
-    low, top = ["f0q", "f0s"], ["f1q", "f1s"]
-    pieces = [(0, 0, cut, low), (1, 0, cut, low), (0, cut, ROOM, top), (1, cut, ROOM, top)]
-    for o in range(2, O):
-        pieces += [(o, 0, ROOM // 2, low + top), (o, ROOM // 2, ROOM, low + top)]
-    for i, (o, a, b, keys) in enumerate(pieces):
-        op("t", g.tensor.matmul_mx, (T.acc[:, 512 * i:512 * i + b - a], T.wq[:, 128 * o:128 * o + 128], T.wsc[:, 128 * o:128 * o + 128],
-                                     T.fq[:, a:b], T.fs[:, a:b], True, True), ["wq%d" % (o // 2)] + keys, ["acc%d" % i])
-    for i, (o, a, b, keys) in enumerate(pieces):
-        src, dst = T.acc[:, 512 * i:512 * i + b - a], T.yo[:, ROOM * o + a:ROOM * o + b]
-        (cp if i in (1, 3, 4, 6) else act)(dst, src, ["acc%d" % i], ["yo%d" % i])
-        if o < 2:
-            dma("y", "dy", T.y[:, ROOM * o + a:ROOM * o + b], dst, ["yo%d" % i], ["yout"])
-        elif a > 0:
-            dma("y", "dy", T.y[:, ROOM * o:ROOM * o + ROOM], T.yo[:, ROOM * o:ROOM * o + ROOM], ["yo%d" % (i - 1), "yo%d" % i], ["yout"])
+    def runs(qs, reads):
+        for q in qs:
+            ts(ta[:, q:q + 324:17], places, pp[:, q:q + 1], dd[:, q:q + 1], GE, MUL, ["jj"] + reads, ["run%d" % q])
+
+    def spill():
+        line(nn[:, 8:14], T.nl0[:, 0:48:8], 1.0, -float(HALF), ["num", "nl0"], ["spill"], RELU)
+        line(nn[:, 16:21], nn[:, 9:14], 1.0, float(SLOT), ["spill"], ["jump"])
+
+    def aside():
+        sd, sg = T.sd, T.sg
+        line(sd[:, 0:ASIDE], pp[:, 1:1 + ASIDE], -1.0, 0.5, ["pp"], ["sd0"])
+        line(dd[:, 1:8], nn[:, 0:7], -1.0, float(SLOT), ["nc"], ["dd1"])
+        line(sd[:, 8:8 + ASIDE], nn[:, 0:ASIDE], -0.5, SLOT / 2, ["nc"], ["sd1"])
+        for q in range(ASIDE):
+            line(sg[:, 20 * q:20 * q + 20], places, 1.0, sd[:, q:q + 1], ["jj", "sd0"], ["sg%d" % q], SIGN)
+        for q in range(ASIDE):
+            half = sd[:, 8 + q:9 + q]
+            line(ta[:, q + 1:q + 325:17], sg[:, 20 * q:20 * q + 20], half, half, ["sg%d" % q, "sd1"], ["run%d" % (q + 1)])
+
+    step.update(
+        spill=spill, aside=aside,
+        own_n0=lambda: act(T.nl0[:, 0:1], sent["n0"][1](own, 1), ["t1"], ["nl0"]),
+        own_n1=lambda: act(T.nl1[:, 0:1], sent["n1"][1](own, 1), ["t2"], ["nl1"]),
+        jj=lambda: line(places, T.j0[:, :], 1.0, qc, ["j0", "qc"], ["jj"]),
+        pp=lambda: scan(pp[:, 1:9], n0, T.cap[:, :], 0.0, ADD, MIN, ["num", "nl0", "cap"], ["pp"]),
+        nc=lambda: tt(nn[:, 0:8], pp[:, 1:9], pp[:, 0:8], SUB, ["pp0", "pp"], ["nc"]),
+        dd8=lambda: ts(dd[:, 8:9], nn[:, 8:9], nn[:, 7:8], float(HALF - SLOT * own), SUB, ADD, ["nc", "spill"], ["dd8"]),
+        p2=lambda: scan(pp[:, 9:17], n1, nn[:, 8:16], pp[:, 8:9], ADD, SUB, ["mar", "nl1", "spill", "spill6", "pp"], ["p2"]),
+        dd9=lambda: tt(dd[:, 9:17], nn[:, 16:24], n1, SUB, ["mar", "nl1", "jump", "jump5", "jump7"], ["dd9"]),
+        firsts=lambda: runs(range(1 + ASIDE, 9), ["pp", "dd1", "dd8"]), seconds=lambda: runs(range(9, 17), ["p2", "dd9"]),
+        cs3=lambda: scan(T.cs3[:, :], T.seg[:, :], ta[:, :], 0.0, MIN, ADD, ["seg", "jj"] + ["run%d" % q for q in range(1, 17)], ["cs3"]),
+        fo=lambda: ts(T.fo[:, :], T.cs3[:, 16:340:17], float(ZERO + NZ - 1), None, MIN, None, ["cs3"], ["fo"]),
+        pick_own=lambda: pick(T.land, T.lsc, SLOT, T.xq, T.xs, TOK, so[:, 2 * own:2 * own + 4], 0, ["so0", "so1", "xq"], ["own"]),
+        zeros=lambda: act(T.zin[:, :], T.xin[:, 0:4 * NZ], ["xin"], ["zin"], scale=0.0),
+        quant_x=lambda: quant(T.xq[:, :], T.xs[:, :], T.xin[:, :], ["xin"], ["xq"]),
+        quant_z=lambda: quant(T.land[:, ZERO:ZERO + NZ], T.lsc[:, ZERO:ZERO + NZ], T.zin[:, :], ["zin"], ["zq"]),
+        quant_w0=lambda: quant(T.wq[:, 0:256], T.wsc[:, 0:256], T["win"][:, 0:1024], ["win0"], ["wq0"]),
+        quant_w1=lambda: quant(T.wq[:, 256:512], T.wsc[:, 256:512], T["win"][:, 1024:2048], ["win1"], ["wq1"]))
+
+    def products():
+        got = ["dat", "ownq", "owns", "zq", "fo"]
+        cut = 128
+        for i, (a, b) in enumerate(((0, cut), (cut, ROOM))):
+            pick(T.fq, T.fs, b - a, T.land, T.lsc, ZERO + NZ, T.fo[:, a // 16:b // 16], a, got, ["f%d" % i])
+        low, high = ["f0q", "f0s"], ["f1q", "f1s"]
+        pieces = [(0, 0, cut, low), (1, 0, cut, low), (0, cut, ROOM, high), (1, cut, ROOM, high)]
+        for o in range(2, O):
+            pieces += [(o, 0, ROOM // 2, low + high), (o, ROOM // 2, ROOM, low + high)]
+        for i, (o, a, b, reads) in enumerate(pieces):
+            op("t", g.tensor.matmul_mx, (T.acc[:, 512 * i:512 * i + b - a], T.wq[:, 128 * o:128 * o + 128], T.wsc[:, 128 * o:128 * o + 128],
+                                         T.fq[:, a:b], T.fs[:, a:b], True, True), ["wq%d" % (o // 2)] + reads, ["acc%d" % i])
+        for i, (o, a, b, reads) in enumerate(pieces):
+            src, dst = T.acc[:, 512 * i:512 * i + b - a], T.yo[:, ROOM * o + a:ROOM * o + b]
+            (cp if i in (1, 3, 4, 6) else act)(dst, src, ["acc%d" % i], ["yo%d" % i])
+            if o < 2:
+                dma("y", "dy", T.y[:, ROOM * o + a:ROOM * o + b], dst, ["yo%d" % i], ["yout"])
+            elif a > 0:
+                dma("y", "dy", T.y[:, ROOM * o:ROOM * o + ROOM], T.yo[:, ROOM * o:ROOM * o + ROOM], ["yo%d" % (i - 1), "yo%d" % i], ["yout"])
+
+    step["products"] = products
+    for name in ORDER:
+        step[name]()
     for sem in sorted(cnt):
         need("y", (sem, None))

from concourse.bass import DstId, RemoteDMATransfer
from concourse.mybir import dt, AluOpType, AxisListType, ActivationFunctionType

N, TOK, O, CAP, ROOM = 8, 256, 4, 288, 320
HALF = 32
SLOT = 2 * HALF
FIRST = 48
ZERO = N * SLOT
NZ = 128
WIN = N * FIRST
BASE = 64
LATE = BASE + WIN
BACK = 5
ROW = TOK + 32
BIG = 1024.0
ASIDE = 4


def _sb(n, d):
    return ("sbuf", [128, n], d)


F32, I32, U16, B16, MX, U8 = "float32", "int32", "uint16", "bfloat16", "float8_e4m3fn_x4", "uint8"
SCRATCH = {
    "lists": ("dram", [N, 128, 2], I32),
    "ct": _sb(48, I32), "xin": _sb(4 * TOK, B16), "win": _sb(512 * O, B16), "zin": _sb(4 * NZ, B16),
    "xq": _sb(TOK, MX), "xs": _sb(TOK, U8), "wq": _sb(128 * O, MX), "wsc": _sb(128 * O, U8),
    "cnt": _sb(8, F32), "ra": _sb(96, F32), "ca": _sb(96, F32), "ec": _sb(128, I32), "cut": _sb(128, F32), "seg": _sb(340, F32),
    "gr": _sb(64, F32), "gt": _sb(64, F32), "gl": _sb(4, U16), "lc": _sb(8, U16), "lf": _sb(12, F32), "lb": _sb(16, U16), "kc": _sb(16, F32),
    "v128": _sb(128, B16), "vals": _sb(128, B16), "j0": _sb(20, F32), "cap": _sb(8, F32),
    "pre": _sb(ROW, B16), "m1": _sb(ROW, B16), "cum1": _sb(ROW, B16), "t1": _sb(ROW, B16), "one1": _sb(64, B16),
    "one2": _sb(72, B16), "gm1": _sb(64, F32), "top1": _sb(64, F32), "tk": _sb(56, F32), "zi": _sb(16, I32),
    "off": _sb(16, U16), "kw": _sb(TOK, B16), "key": _sb(ROW, B16), "far2": _sb(64, F32),
    "al": _sb(64, I32), "eqs": _sb(192, B16), "bg": _sb(192, B16), "tg": _sb(64, B16), "gs": _sb(8, F32),
    "nl0": _sb(8 * N, B16), "nl1": _sb(8 * N, B16),
    "fa": _sb(ROW, B16), "fb": _sb(ROW, B16), "rf": _sb(8, F32), "ref": _sb(64, F32), "cum2": _sb(ROW, B16), "t2": _sb(ROW, B16),
    "both": _sb(128, F32), "top2": _sb(128, F32),
    "scat": _sb(LATE + WIN, B16), "tw": _sb(4 * WIN, B16), "hh": _sb(48, F32), "so": _sb(32, U16),
    "sq": _sb(2 * (N - 1) * HALF, MX), "sp": _sb(2 * (N - 1) * HALF, U8),
    "hn0": _sb(2 * N, B16), "hn1": _sb(2 * N, B16), "hq": _sb(2 * (N - 1) * HALF, MX), "hs": _sb(2 * (N - 1) * HALF, U8),
    "land": _sb(ZERO + NZ, MX), "lsc": _sb(ZERO + NZ, U8),
    "pp": _sb(24, F32), "nn": _sb(24, F32), "dd": _sb(24, F32), "sd": _sb(16, F32), "sg": _sb(20 * ASIDE, F32),
    "ta": _sb(340, F32), "cs3": _sb(340, F32),
    "fo": _sb(20, U16), "fq": _sb(ROOM, MX), "fs": _sb(ROOM, U8),
    "acc": ("psum", [128, 512 * 2 * O], F32), "yo": _sb(ROOM * O, F32),
}
SEMAPHORES = ["cv", "cs", "cg", "ct", "dl0", "dc1", "dc2", "dx", "dw0", "dw1", "dal", "dy", "lst", "num", "mar", "dat",
              "hn0", "hn1", "hq0", "hs0", "hq1", "hs1", "left"]

ORDER = """
loads patterns send_lists cut pad tails blocks gaps blanks constants
columns pre columns2 z0 m1 sign lb one1 clear0 values less cum1 z1 t1 one2 edge gm1 top1 over
kk pos1 kw u2 off0 own_n0 far2 reload hand_n0 straight_n0 patterns4 w0 w1 scatter0 named0 named1 gt counted0 counted1 gl
turned0 turned1 key ahead0 ahead1 refused turn00 fa fb stay cum2 turn01 t2 own_n1 clear1 hand_n1 straight_n1 join00 join01
ref quant_x gm2 lists0 top2 pick_h0 off1 pick_s0 scatter1 wave0 jj zeros turn10 turn11 join10 join11 lists1 pick_h1 pick_s1 wave1 seg
pp spill pick_own nc aside p2 dd9 dd8 quant_w0 seconds firsts quant_z cs3 quant_w1 fo products
""".split()

ADD, SUB, MUL, MIN, MAX = AluOpType.add, AluOpType.subtract, AluOpType.mult, AluOpType.min, AluOpType.max
GE, GT, LT, EQ = AluOpType.is_ge, AluOpType.is_gt, AluOpType.is_lt, AluOpType.is_equal
AND = AluOpType.bitwise_and
COPY, IDENT, SIGN, RELU, ABS = (ActivationFunctionType.Copy, ActivationFunctionType.Identity, ActivationFunctionType.Sign,
                                ActivationFunctionType.Relu, ActivationFunctionType.Abs)


def deal(keys, engines):
    k = len(engines) // len(keys)
    return {z: engines[k * i:k * i + k] for i, z in enumerate(keys)}


def plan(me, cores, topo):
    core = cores[me]
    to = [cores[(me + 1 + z) % N] for z in range(N - 1)]
    near = [z for z in range(N - 1) if topo.chip(to[z]) == topo.chip(core)][0]
    far = [z for z in range(N - 1) if z != near]
    pairs = [far[0:2], far[2:4], far[4:6]]
    out = topo.engines(core, to[far[0]])
    inn = [e for e in topo.engines(core, to[near]) if e not in out]
    turn = sorted((core, to[near])).index(core)
    free = [c for c in topo.cores_of(core) if c not in cores]
    wide = [c for c in free if topo.may_write(c, to[far[0]])]
    same = [c for c in free if c not in wide and topo.die(c) == topo.die(core)]
    other = [c for c in free if c not in wide and topo.die(c) != topo.die(core)]
    first, second = wide[turn], (same, other)[turn][turn]
    on = {first: deal(pairs[0], out), second: deal(pairs[1], out)}
    counts = {"hand": {first: (pairs[0], inn[:4]), second: (pairs[1], inn[4:])}, "straight": {**deal(pairs[2], out), near: inn}, "on": on}
    columns = {"hand": {first: (pairs[0], out), second: (pairs[1], inn)}, "straight": {**deal(pairs[2], out), near: inn}, "on": on}
    return {"to": to, "lists": out[::4], "last": far[3], "n0": counts, "n1": counts,
            "q0": columns, "s0": columns, "q1": columns, "s1": columns}


def mask(engines):
    m = 0
    for e in engines:
        m |= 1 << e
    return m


def at(core, topo):
    rid, pid, _ = topo.addr(core)
    return DstId(rid=rid, pnc=pid)


def codes(buf, c, n):
    return buf[:, c:c + n].bitcast(dt.uint8)


def plane(buf, c, n):
    return buf[:, c:c + n]


def place(z):
    return N - 1 - z


def entry(late, z):
    return 2 * N - 1 - z if late else z


def goods(T):
    def columns(late, cut, src, home, far):
        return (lambda z: entry(late, z) - 2 * late, lambda a, n: cut(src, HALF * a, HALF * n),
                lambda a, n: cut(home, HALF * a, HALF * n), lambda k: cut(far, SLOT * k + HALF * late, HALF), "dat")

    def counts(src, c, home, far, sem):
        return (lambda z: z, lambda a, n: src[:, c + 2 * a:c + 2 * (a + n) - 1], lambda a, n: home[:, 2 * a:2 * (a + n) - 1],
                lambda k: far[:, 8 * k:8 * k + 1], sem)

    return {"n0": counts(T.t1, TOK + 2 * N, T.hn0, T.nl0, "num"),
            "n1": counts(T.t2, TOK, T.hn1, T.nl1, "mar"),
            "q0": columns(0, codes, T.sq, T.hq, T.land), "s0": columns(0, plane, T.sp, T.hs, T.lsc),
            "q1": columns(1, codes, T.sq, T.hq, T.land), "s1": columns(1, plane, T.sp, T.hs, T.lsc)}


def helper_program(g, p, core, T, topo):
    left = 0
    for name, (number, _, home, far, sem) in goods(T).items():
        engines = p[name]["on"][core]
        g.wait_ge(T.sem["h" + name], len(p[name]["hand"][core][1]))
        g.remote_dma_fused([RemoteDMATransfer(dst_ids=[at(p["to"][z], topo)], dma_engine_mask=mask(e), remote_sem=T.sem[sem],
                                              src=home(number(z), 1), dst=far(place(z))) for z, e in engines.items()], local_sem=T.sem["left"])
        left += sum(len(e) for e in engines.values())
    g.wait_ge(T.sem["left"], left)


def rank_program(g, core, T, topo):
    cores = [int(c) for c in T.cores]
    me = T.rank_of(core)
    if me is None:
        for r in range(N):
            p = plan(r, cores, topo)
            if core in p["q0"]["on"]:
                helper_program(g, p, core, T, topo)
        return
    p = plan(me, cores, topo)
    own = N - 1
    queue = {"v": g.vector, "s": g.scalar, "t": g.tensor, "g": g, "y": g.sync}
    cnt, seen, wr, rd = {}, {}, {}, {}

    def need(q, tok):
        sem, val = tok
        if val is None:
            val = cnt[sem]
        if seen.get((q, sem), 0) < val:
            queue[q].wait_ge(T.sem[sem], val)
            seen[(q, sem)] = val

    def before(q, reads, writes):
        toks = {}
        for k in reads:
            for t in wr[k]:
                toks.setdefault(t[0], []).append(t)
        for k in writes:
            for t in wr.get(k, []) + rd.get(k, []):
                toks.setdefault(t[0], []).append(t)
        for sem in toks:
            v = [t[1] for t in toks[sem]]
            need(q, (sem, None if None in v else max(v)))

    def after(tok, reads, writes, more):
        for k in writes:
            wr[k] = (wr.get(k, []) if more else []) + [tok]
            if not more:
                rd[k] = []
        for k in reads:
            rd.setdefault(k, []).append(tok)

    def op(q, call, args, reads, writes, **kw):
        before(q, reads, writes)
        sem = "c" + q
        call(*args, **kw).then_inc(T.sem[sem], 1)
        cnt[sem] = cnt.get(sem, 0) + 1
        after((sem, cnt[sem]), reads, writes, False)

    def dma(q, sem, out, in_, reads, writes):
        before(q, reads, [])
        queue[q].dma_start(out, in_).then_inc(T.sem[sem], 16)
        cnt[sem] = cnt.get(sem, 0) + 16
        after((sem, None), reads, writes, True)

    V = g.vector

    def ts(out, in0, s1, s2, op0, op1, reads, writes):
        a = (out, in0, s1, s2, op0) if op1 is None else (out, in0, s1, s2, op0, op1)
        op("v", V.tensor_scalar, a, reads, writes)

    def tt(out, a, b, o, reads, writes):
        op("v", V.tensor_tensor, (out, a, b, o), reads, writes)

    def cp(out, a, reads, writes):
        op("v", V.tensor_copy, (out, a), reads, writes)

    def red(out, a, reads, writes):
        op("v", V.tensor_reduce, (out, a, AxisListType.X, ADD), reads, writes)

    def tr(out, a, reads, writes):
        op("v", V.transpose, (out, a), reads, writes)

    def quant(oq, os_, tile, reads, writes):
        op("v", V.quantize_mx, (oq, os_, tile), reads, writes)

    def scan(out, a, b, init, op0, op1, reads, writes):
        op("v", V.tensor_tensor_scan, (out, a, b, init, op0, op1), reads, writes)

    def count(out, a, init, reads, writes):
        scan(out, a, a, init, ADD, MAX, reads, writes)

    def top(out, cut, a, reads, writes):
        scan(out, cut, a, 0.0, MIN, MAX, reads + ["cut"], writes)

    def fill(ap, val, key):
        op("v", V.memset, (ap, val), [], [key])

    def iota(ap, key, pattern, base):
        op("g", g.iota, (ap, pattern, base, 0), [], [key], allow_small_or_imprecise_dtypes=True)

    def act(out, a, reads, writes, **kw):
        op("s", g.scalar.activation, (out, a, COPY), reads, writes, **kw)

    def line(out, a, scale, bias, reads, writes, func=IDENT):
        op("s", g.scalar.activation, (out, a, func, bias, scale), reads, writes)

    def call(transfers, reads):
        before("g", reads, [])
        g.remote_dma_fused([RemoteDMATransfer(dst_ids=[at(c, topo) for c in to], dma_engine_mask=mask(e), remote_sem=T.sem[sem],
                                              srcs=[src], dsts=dst) for to, e, sem, src, dst in transfers], local_sem=T.sem["left"])
        cnt["left"] = cnt.get("left", 0) + sum(len(t[1]) for t in transfers)

    sent = goods(T)
    cnt["lst"] = cnt["num"] = cnt["mar"] = cnt["dat"] = 0
    for k in range(1, N):
        o, z = plan((me + k) % N, cores, topo), N - 1 - k
        cnt["lst"] += len(o["lists"])
        for name, piece in sent.items():
            cnt[piece[4]] += sum(len(e.get(z, [])) for e in [o[name]["straight"]] + list(o[name]["on"].values()))
    for sem in ("lst", "num", "mar", "dat"):
        wr[sem] = [(sem, cnt[sem])]

    def hand(name, reads):
        number, src, home, _, _ = sent[name]
        runs = [(h, e, min(number(z) for z in zs), len(zs)) for h, (zs, e) in p[name]["hand"].items()]
        call([([h], e, "h" + name, src(a, n), [home(a, n)]) for h, e, a, n in runs], reads)

    def straight(name, reads):
        number, src, _, far, sem = sent[name]
        call([([p["to"][z]], e, sem, src(number(z), 1), [far(place(z))]) for z, e in p[name]["straight"].items()], reads)

    ra, kc, pre, scat, key, tk, zi, lb, rf = T.ra, T.kc, T.pre, T.scat, T.key, T.tk, T.zi, T.lb, T.rf
    eqs, tg, gs, pp, nn, dd, tw, hh, so, ta = T.eqs, T.tg, T.gs, T.pp, T.nn, T.dd, T.tw, T.hh, T.so, T.ta
    zc, hi, odd = [T.ca[:, 32 * j:32 * j + 1] for j in range(3)]
    base1, qc, z2, two, less, over, half0, many0, mid, reach = [kc[:, j:j + 1] for j in range(10)]
    sgn, kk, edge, pos1, u2, way = [tk[:, 8 * j:8 * j + 8] for j in range(6)]
    ec, kw = ["ec%d" % z for z in range(N)], ["kw%d" % b for b in range(8)]
    num1 = T.top1[:, 7:64:8]
    step = {}

    def loads():
        dma("y", "dl0", T.lists[0], T.c1[:, :], [], ["l0"])
        for b in range(8):
            dma("sy"[b % 2], "dc1", T.ct[16 * b:16 * b + 16, 8 - b % 2:24 - b % 2], T.c1[:, :], [], ["c1"])
        for b in range(8):
            dma("sy"[b % 2], "dc2", T.ct[16 * b:16 * b + 16, 32 - b % 2:48 - b % 2], T.c2[:, :], [], ["c2"])
        dma("y", "dx", T.xin[:, :], T.x[:, :], [], ["xin"])

    def reload():
        for b in range(4):
            dma("y", "dal", T.al[32 * b:32 * b + 32, 0:64], T.lists[:, :, :], ["lst", "l0"], ["al"])

    step.update(
        loads=loads, reload=reload,
        w0=lambda: dma("y", "dw0", T["win"][:, 0:1024], T.w[:, 0:1024], ["al"], ["win0"]),
        w1=lambda: dma("y", "dw1", T["win"][:, 1024:2048], T.w[:, 1024:2048], ["al"], ["win1"]),
        send_lists=lambda: call([(p["to"], p["lists"], "lst", T.lists[0], [T.lists[place(z)] for z in range(N - 1)])], ["l0"]),
        hand_n0=lambda: hand("n0", ["t1", "al"]), straight_n0=lambda: straight("n0", ["t1"]),
        hand_n1=lambda: hand("n1", ["t2"]), straight_n1=lambda: straight("n1", ["t2"]))

    def patterns():
        iota(T.cnt[:, :], "cnt", [[1, 8]], 0)
        iota(ra[:, 0:32], "ra0", [[0, 4], [1, 8]], 0)
        iota(ra[:, 32:64], "ra1", [[0, 2], [1, 2], [0, 8]], 0)
        iota(ra[:, 64:96], "ra2", [[16, 2], [0, 16]], 0)

    def blocks():
        iota(T.v128[:, :], "v128", [[32, 8], [1, 16]], 0)
        n = FIRST // 16
        iota(T.gr[:, 32:64], "gr1", [[-1, 2], [-n, N], [1, 2]], 1 + n * own)
        iota(T.gr[:, 0:32], "gr0", [[-1, 2], [n, N], [1, 2]], 1)
        iota(T.gr[:, 47:64:16], "gr1", [[-1, 2]], 1 + BACK)

    def blanks():
        iota(key[:, TOK:ROW], "keyz", [[0, 32]], 0)
        iota(T.both[:, 0:128:2], "bothz", [[0, 64]], 0)

    def clear0():
        for a, b in ((BASE - 16, BASE + TOK), (BASE + TOK, LATE)):
            act(scat[:, a:b], pre[:, 0:b - a], ["pre"], ["scat%d" % a], scale=0.0)

    def patterns4():
        iota(T.j0[:, :], "j0", [[16, 20]], 0)
        iota(T.cap[:, :], "cap", [[0, 8]], CAP)
        iota(nn[:, 14:16], "spill6", [[0, 2]], 0)
        iota(nn[:, 21:23], "jump5", [[HALF - FIRST, 2]], SLOT + FIRST - HALF)
        iota(nn[:, 23:24], "jump7", [[0, 1]], SLOT - FIRST)
        iota(pp[:, 0:1], "pp0", [[0, 1]], 0)

    def constants():
        for z in range(N):
            fill(T.ec[:, z:128:N], (me + 1 + z) % N, "ec%d" % z)
        fill(pre[:, :], 0.0, "pre")
        ts(T.lc[:, :], T.cnt[:, :], 2.0, None, MUL, None, ["cnt"], ["lc0"])

    def columns2():
        f8, f2, fr = [T.lf[:, 4 * j:4 * j + 4] for j in range(3)]
        line(fr, T.cnt[:, 0:4], 2.0, hi, ["cnt", "ca"], ["fr"])
        line(z2, zc, 2.0, 0.0, ["ca"], ["z2"])
        line(base1, odd, (1.0 - BASE) / 16, BASE - 1.0, ["ca"], ["base1"])
        line(qc, hi, 8.0, zc, ["ca"], ["qc"])
        line(f8, fr, 32.0, z2, ["fr", "z2"], ["f8"])
        line(f2, fr, 2.0, 0.0, ["fr"], ["f2"])
        line(two, qc, 1.0, -3.5, ["qc"], ["two"], SIGN)

    l8, l2, lr = [lb[:, 4 * j:4 * j + 4] for j in range(3)]
    step.update(
        patterns=patterns, blocks=blocks, blanks=blanks, clear0=clear0, patterns4=patterns4, constants=constants, columns2=columns2,
        cut=lambda: iota(T.cut[:, :], "cut", [[0, 8], [int(BIG), 16]], 0),
        values=lambda: line(T.vals[:, :], T.v128[:, :], 1.0, odd, ["v128", "ca"], ["vals"]),
        seg=lambda: iota(T.seg[:, :], "seg", [[0, 20], [int(BIG), 17]], 0),
        clear1=lambda: act(scat[:, LATE:LATE + WIN], T.xin[:, 0:WIN], ["xin"], ["scat%d" % LATE], scale=0.0),
        pad=lambda: iota(T.one2[:, 64:72], "one2z", [[0, 8]], 0), gaps=lambda: iota(T.kw[:, 1:TOK:2], "kwz", [[0, 128]], 0),
        less=lambda: line(less, two, BIG, -(BASE + HALF - 1.0 + BIG), ["two"], ["less"]),
        tails=lambda: [iota(eqs[:, 96 * i + 64:96 * i + 96], "eqz%d" % i, [[0, 32]], 0) for i in range(2)],
        columns=lambda: tr(T.ca[:, :], ra[:, :], ["ra0", "ra1", "ra2"], ["ca"]),
        lb=lambda: cp(lb[:, 0:12], T.lf[:, :], ["f8", "f2", "fr"], ["l8", "l2", "lr"]),
        gt=lambda: tr(T.gt[:, :], T.gr[:, :], ["gr0", "gr1"], ["gt"]),
        gl=lambda: cp(T.gl[:, 0:4:2], T.gt[:, 0:64:32], ["gt"], ["gl"]))

    def keys():
        for b in range(8):
            line(T.kw[:, 32 * b:32 * b + 32:2], T.one2[:, 8 * b:8 * b + 16], tk[:, 8 + b:9 + b], 0.0, ["one2", "one2z", "kk"], ["kw%d" % b])

    def begins():
        for z in range(N):
            act(T.far2[:, z:64:N], T.one2[:, z:64:N], ["one2"], ["far%d" % z], scale=LATE - 1.0 + {0: 16 * BACK, 1: FIRST + 16}.get(z, FIRST * z))

    def moved():
        line(way, num1, 1.0, -(BASE + HALF - 0.5), ["top1"], ["way"], SIGN)
        line(u2, way, (WIN - HALF) / 2, (WIN - HALF) / 2, ["way"], ["u2"])

    step.update(
        pre=lambda: tt(pre[:, 0:TOK:2], T.ct[:, 8:23].indirect(T.lc[:, 0:8]), T.ec[:, :], EQ, ["c1", "lc0"] + ec, ["pre"]),
        m1=lambda: tr(T.m1[:, :], pre[:, :], ["pre"], ["m1"]),
        sign=lambda: tt(sgn, pre[:, 0:TOK:32], pre[:, 2:TOK:32], SUB, ["pre"], ["sgn"]),
        one1=lambda: act(T.one1[:, :], pre[:, 0:TOK].indirect(l8), ["pre", "l8"], ["one1"]),
        cum1=lambda: count(T.cum1[:, :], T.m1[:, :], base1, ["m1", "base1"], ["cum1"]),
        one2=lambda: tt(T.one2[:, 0:64], T.ct[:, 32:47].indirect(l2), T.ec[:, 0:64], EQ, ["c2", "l2"] + ec, ["one2"]),
        t1=lambda: tr(T.t1[:, :], T.cum1[:, :], ["cum1"], ["t1"]),
        gm1=lambda: tt(T.gm1[:, :], T.t1[:, 0:TOK].indirect(l8), T.one1[:, :], MUL, ["t1", "l8", "one1"], ["gm1"]),
        top1=lambda: top(T.top1[:, :], T.cut[:, 0:128:2], T.gm1[:, :], ["gm1"], ["top1"]),
        pos1=lambda: tt(pos1, num1, edge, ADD, ["top1", "edge"], ["pos1"]),
        off0=lambda: cp(T.off[:, 0:8], pos1, ["pos1"], ["off0"]),
        over=lambda: line(over, T.cum1[:, ROW - 1:ROW], 1.0, less, ["cum1", "less"], ["over"], RELU),
        z0=lambda: ts(zi[:, 0:8], T.ct[:, 8:23:2], float(N - 1 - me), None, ADD, None, ["c1"], ["zi0"]),
        z1=lambda: ts(zi[:, 8:16], zi[:, 0:8], N - 1, None, AND, None, ["zi0"], ["zi1"]),
        edge=lambda: ts(edge, zi[:, 8:16], float(FIRST), None, MUL, None, ["zi1"], ["edge"]),
        u2=moved,
        far2=begins,
        stay=lambda: tt(T.both[:, 0:128:16], u2, pos1, ADD, ["u2", "pos1", "bothz"], ["stay"]),
        kk=lambda: tt(kk, num1, sgn, MUL, ["top1", "sgn"], ["kk"]),
        kw=keys,
        key=lambda: tr(key[:, 0:TOK], T.kw[:, :], kw + ["kwz"], ["key"]))

    def named(i):
        ts(eqs[:, 96 * i:96 * i + 64], T.al[:, :], float((me + 1 + i) % N), None, EQ, None, ["al"], ["eq%d" % i])

    def counted(i):
        count(T.bg[:, 96 * i:96 * i + 96], eqs[:, 96 * i:96 * i + 96], 0.0, ["eq%d" % i, "eqz%d" % i], ["bg%d" % i])

    def turned(i):
        tr(tg[:, 32 * i:32 * i + 32], T.bg[:, 96 * i + 64:96 * i + 96], ["bg%d" % i], ["tg%d" % i])

    def ahead(i):
        red(gs[:, i:i + 1], tg[:, 36 * i + 4:32 * i + 32], ["tg%d" % i], ["gs%d" % i])

    limit = CAP + BASE - 1.0

    def refused():
        line(half0, gs[:, 0:1], 0.5, 0.0, ["gs0"], ["half0"])
        line(many0, gs[:, 0:1], BIG / 2, -BIG * limit, ["gs0"], ["many0"])
        line(mid, gs[:, 1:2], -0.5, half0, ["gs1", "half0"], ["mid"])
        line(reach, gs[:, 1:2], BIG / 2, many0, ["gs1", "many0"], ["reach"])
        line(way, kk, 1.0, mid, ["kk", "mid"], ["way"], ABS)
        line(rf[:, :], way, BIG, reach, ["way", "reach"], ["rf"], RELU)

    step.update(
        refused=refused,
        fa=lambda: ts(T.fa[:, :], key[:, :], gs[:, 0:1], limit, ADD, GT, ["key", "keyz", "gs0"], ["fa"]),
        fb=lambda: ts(T.fb[:, :], key[:, :], gs[:, 1:2], -limit, SUB, LT, ["key", "keyz", "gs1"], ["fb"]),
        cum2=lambda: scan(T.cum2[:, :], T.fa[:, :], T.fb[:, :], over, ADD, ADD, ["fa", "fb", "over"], ["cum2"]),
        t2=lambda: tr(T.t2[:, :], T.cum2[:, :], ["cum2"], ["t2"]),
        ref=lambda: tt(T.ref[:, :], rf[:, :].indirect(lr), T.far2[:, :], MIN, ["rf", "lr"] + ["far%d" % z for z in range(N)], ["ref"]),
        gm2=lambda: tt(T.both[:, 1:128:2], T.t2[:, :].indirect(l8), T.ref[:, :], ADD, ["t2", "ref", "l8"], ["gm2"]),
        top2=lambda: top(T.top2[:, :], T.cut[:, :], T.both[:, :], ["gm2", "stay", "bothz"], ["top2"]),
        off1=lambda: cp(T.off[:, 8:16], T.top2[:, 15:128:16], ["top2"], ["off1"]))

    def scatter(late):
        op("v", V.tensor_copy, (scat[:, 0:LATE + WIN * late].indirect(T.off[:, 8 * late:8 * late + 8]), T.vals[:, :]),
           ["off%d" % late, "vals"] + ["scat%d" % a for a in (BASE - 16, BASE + TOK, LATE)[:2 + late]], ["scat"])

    def turn(late, j):
        a, c = BASE + WIN * late - 16 * j, WIN * (2 * late + j)
        tr(tw[:, c:c + WIN], scat[:, a:a + WIN], ["scat"], ["tw%d%d" % (late, j)])

    def join(late, j):
        c = WIN * (2 * late + j)
        tt(hh[:, 24 * late + 1 - j:24 * late + 24:2], tw[:, c:c + WIN:32], tw[:, c + 16:c + WIN:32], ADD, ["tw%d%d" % (late, j)], ["hh%d%d" % (late, j)])

    def lists(late):
        cp(so[:, 16 * late:16 * late + 16], hh[:, 24 * late:24 * late + 24].indirect(T.gl[:, 2 * late:2 * late + 1]),
           ["gl", "hh%d0" % late, "hh%d1" % late], ["so%d" % late])

    def pick(oq, os_, n, iq, is_, m, off, n0, reads, writes):
        op("v", V.tensor_copy, (oq[:, n0:n0 + n].bitcast(dt.uint32), iq[:, 0:m].bitcast(dt.uint32).indirect(off)), reads, [k + "q" for k in writes])
        act(os_[:, n0:n0 + n], is_[:, 0:m].indirect(off), reads, [k + "s" for k in writes])

    def slots(late, zs, keys):
        a, b = min(entry(late, z) for z in zs), max(entry(late, z) for z in zs) + 1
        pick(T.sq, T.sp, HALF * (b - a), T.xq, T.xs, TOK, so[:, 2 * a:2 * b], HALF * (a - 2 * late), ["so%d" % late, "xq"], keys)

    def wave(late):
        for kind in "qs":
            hand(kind + str(late), ["h%d%s" % (late, kind)])
        for kind in "qs":
            straight(kind + str(late), ["h%d%s" % (late, kind), "s%d%s" % (late, kind)])

    last = p["last"]
    for i in range(2):
        for name, f in (("named", named), ("counted", counted), ("turned", turned), ("ahead", ahead), ("scatter", scatter),
                        ("lists", lists), ("wave", wave)):
            step[name + str(i)] = lambda f=f, i=i: f(i)
        for j in range(2):
            step["turn%d%d" % (i, j)] = lambda i=i, j=j: turn(i, j)
            step["join%d%d" % (i, j)] = lambda i=i, j=j: join(i, j)
        step["pick_h%d" % i] = lambda i=i: slots(i, range(last + 1), ["h%d" % i])
        step["pick_s%d" % i] = lambda i=i: slots(i, range(last + 1, own), ["s%d" % i])

    n0, n1 = T.nl0[:, 0:8 * N:8], T.nl1[:, 0:8 * N:8]
    places = ta[:, 0:340:17]

    def runs(qs, reads):
        for q in qs:
            ts(ta[:, q:q + 324:17], places, pp[:, q:q + 1], dd[:, q:q + 1], GE, MUL, ["jj"] + reads, ["run%d" % q])

    def spill():
        line(nn[:, 8:14], T.nl0[:, 0:48:8], 1.0, -float(HALF), ["num", "nl0"], ["spill"], RELU)
        line(nn[:, 16:21], nn[:, 9:14], 1.0, float(SLOT), ["spill"], ["jump"])

    def aside():
        sd, sg = T.sd, T.sg
        line(sd[:, 0:ASIDE], pp[:, 1:1 + ASIDE], -1.0, 0.5, ["pp"], ["sd0"])
        line(dd[:, 1:8], nn[:, 0:7], -1.0, float(SLOT), ["nc"], ["dd1"])
        line(sd[:, 8:8 + ASIDE], nn[:, 0:ASIDE], -0.5, SLOT / 2, ["nc"], ["sd1"])
        for q in range(ASIDE):
            line(sg[:, 20 * q:20 * q + 20], places, 1.0, sd[:, q:q + 1], ["jj", "sd0"], ["sg%d" % q], SIGN)
        for q in range(ASIDE):
            half = sd[:, 8 + q:9 + q]
            line(ta[:, q + 1:q + 325:17], sg[:, 20 * q:20 * q + 20], half, half, ["sg%d" % q, "sd1"], ["run%d" % (q + 1)])

    step.update(
        spill=spill, aside=aside,
        own_n0=lambda: act(T.nl0[:, 0:1], sent["n0"][1](own, 1), ["t1"], ["nl0"]),
        own_n1=lambda: act(T.nl1[:, 0:1], sent["n1"][1](own, 1), ["t2"], ["nl1"]),
        jj=lambda: line(places, T.j0[:, :], 1.0, qc, ["j0", "qc"], ["jj"]),
        pp=lambda: scan(pp[:, 1:9], n0, T.cap[:, :], 0.0, ADD, MIN, ["num", "nl0", "cap"], ["pp"]),
        nc=lambda: tt(nn[:, 0:8], pp[:, 1:9], pp[:, 0:8], SUB, ["pp0", "pp"], ["nc"]),
        dd8=lambda: ts(dd[:, 8:9], nn[:, 8:9], nn[:, 7:8], float(HALF - SLOT * own), SUB, ADD, ["nc", "spill"], ["dd8"]),
        p2=lambda: scan(pp[:, 9:17], n1, nn[:, 8:16], pp[:, 8:9], ADD, SUB, ["mar", "nl1", "spill", "spill6", "pp"], ["p2"]),
        dd9=lambda: tt(dd[:, 9:17], nn[:, 16:24], n1, SUB, ["mar", "nl1", "jump", "jump5", "jump7"], ["dd9"]),
        firsts=lambda: runs(range(1 + ASIDE, 9), ["pp", "dd1", "dd8"]), seconds=lambda: runs(range(9, 17), ["p2", "dd9"]),
        cs3=lambda: scan(T.cs3[:, :], T.seg[:, :], ta[:, :], 0.0, MIN, ADD, ["seg", "jj"] + ["run%d" % q for q in range(1, 17)], ["cs3"]),
        fo=lambda: ts(T.fo[:, :], T.cs3[:, 16:340:17], float(ZERO + NZ - 1), None, MIN, None, ["cs3"], ["fo"]),
        pick_own=lambda: pick(T.land, T.lsc, SLOT, T.xq, T.xs, TOK, so[:, 2 * own:2 * own + 4], 0, ["so0", "so1", "xq"], ["own"]),
        zeros=lambda: act(T.zin[:, :], T.xin[:, 0:4 * NZ], ["xin"], ["zin"], scale=0.0),
        quant_x=lambda: quant(T.xq[:, :], T.xs[:, :], T.xin[:, :], ["xin"], ["xq"]),
        quant_z=lambda: quant(T.land[:, ZERO:ZERO + NZ], T.lsc[:, ZERO:ZERO + NZ], T.zin[:, :], ["zin"], ["zq"]),
        quant_w0=lambda: quant(T.wq[:, 0:256], T.wsc[:, 0:256], T["win"][:, 0:1024], ["win0"], ["wq0"]),
        quant_w1=lambda: quant(T.wq[:, 256:512], T.wsc[:, 256:512], T["win"][:, 1024:2048], ["win1"], ["wq1"]))

    def products():
        got = ["dat", "ownq", "owns", "zq", "fo"]
        cut = 128
        for i, (a, b) in enumerate(((0, cut), (cut, ROOM))):
            pick(T.fq, T.fs, b - a, T.land, T.lsc, ZERO + NZ, T.fo[:, a // 16:b // 16], a, got, ["f%d" % i])
        low, high = ["f0q", "f0s"], ["f1q", "f1s"]
        pieces = [(0, 0, cut, low), (1, 0, cut, low), (0, cut, ROOM, high), (1, cut, ROOM, high)]
        for o in range(2, O):
            pieces += [(o, 0, ROOM // 2, low + high), (o, ROOM // 2, ROOM, low + high)]
        for i, (o, a, b, reads) in enumerate(pieces):
            op("t", g.tensor.matmul_mx, (T.acc[:, 512 * i:512 * i + b - a], T.wq[:, 128 * o:128 * o + 128], T.wsc[:, 128 * o:128 * o + 128],
                                         T.fq[:, a:b], T.fs[:, a:b], True, True), ["wq%d" % (o // 2)] + reads, ["acc%d" % i])
        for i, (o, a, b, reads) in enumerate(pieces):
            src, dst = T.acc[:, 512 * i:512 * i + b - a], T.yo[:, ROOM * o + a:ROOM * o + b]
            (cp if i in (1, 3, 4, 6) else act)(dst, src, ["acc%d" % i], ["yo%d" % i])
            if o < 2:
                dma("y", "dy", T.y[:, ROOM * o + a:ROOM * o + b], dst, ["yo%d" % i], ["yout"])
            elif a > 0:
                dma("y", "dy", T.y[:, ROOM * o:ROOM * o + ROOM], T.yo[:, ROOM * o:ROOM * o + ROOM], ["yo%d" % (i - 1), "yo%d" % i], ["yout"])

    step["products"] = products
    for name in ORDER:
        step[name]()
    for sem in sorted(cnt):
        need("y", (sem, None))
